import numpy as np, ml_dtypes
CORES = [3,11,19,27,35,43,51,59]
N = 8
BF = ml_dtypes.bfloat16
def gentries(a):
    return np.ascontiguousarray(a.reshape(8, 16, -1).transpose(0, 2, 1)).reshape(8, -1)
def gtable(e):
    e = np.asarray(e); return np.ascontiguousarray(e.reshape(8, -1, 16).transpose(0, 2, 1)).reshape(128, -1).astype(np.int32)
V, B, K, PH, CAP, R, ZP, M = 512, 512, 8, 1, 48, 4, 2048, 512
NC, TH = N * CAP, 2047
def parts(rng):
    c = rng.integers(0, 256, (N, 8, 16, V)); low = rng.random((N, 8, 1, V)) < 0.125; c = np.where(low, rng.integers(0, 41, c.shape), c)
    z = rng.integers(0, 256, (N, 8, 16, ZP)); hi = np.argsort(rng.random((N, 8, ZP)), axis=-1)[..., :ZP // 4]
    mark = np.zeros((N, 8, ZP), bool); np.put_along_axis(mark, hi, True, 2); z = np.where(mark[:, :, None], rng.integers(200, 256, z.shape), z)
    e = rng.integers(0, ZP, (N, 8, K, V)); far = np.take_along_axis(hi, rng.integers(0, ZP // 4, (N, 8, K * V)), 2).reshape(N, 8, K, V)
    e = np.where(low & (rng.random((N, 8, 1, V)) < 0.5), far, e)
    p = np.argsort(rng.random((8, K, N * V)), axis=-1)
    share = rng.choice(np.array([0.3, 0.5, 0.75, 1.0]), (N, 8, 1, 1))
    j = np.where(rng.random((N, 8, 1, M)) < share, rng.integers(0, 256, (N, 8, 16, M)), rng.integers(0, 7, (N, 8, 16, M)))
    x = np.clip(c + rng.integers(-6, 7, c.shape), 0, 255)
    return c, z, e, p, j, x
def order(a):
    s = a.shape[:-2]; return np.ascontiguousarray(np.swapaxes(a.reshape(s + (K, PH, B)), -3, -2)).reshape(s + (K * V,))
def small(a):
    return np.ascontiguousarray(a.reshape(N, 128, -1)).astype(np.float32).astype(BF)
def pack(c, z, e, p, j, x):
    n = order(np.ascontiguousarray(p.reshape(8, K, N, V).transpose(2, 0, 1, 3)))
    return {"cen": small(c), "pl": small(z), "ent": order(e).astype(np.int32), "nb": np.stack([gtable(a) for a in n]), "jmp": small(j), "wk": small(x)}
def even(c, j):
    c[:, :, 0] = c[:, :, 0] ^ (np.add.reduce(c, axis=2) & 1); j[..., 0::2] = 0
def steer(rng, c, p, x, cnt, face, last=None):
    x[..., :B] = c[..., :B]
    for g in range(8):
        al = c[:, g].transpose(1, 0, 2).reshape(16, N * V); P = np.full(N * V, -1); pos = {}
        for q in range(N):
            i = rng.permutation(B); at = 0
            if last is not None and last[g, q] >= 0:
                m = int(np.add.reduce(cnt[g, q, :int(last[g, q]) + 1])) - 1; i[i == B - 1] = i[m]; i[m] = B - 1
            for o in range(N):
                n = int(cnt[g, q, o]); pos[q, o] = q * V + i[at:at + n]; at += n
            s = pos[q, q]
            if len(s): P[s] = np.roll(s, 1) if len(s) > 1 else q * V + (s - q * V + 1) % V
        for o in range(N):
            left = rng.permutation(np.setdiff1d(np.arange(o * V, (o + 1) * V), P)); at = 0
            for q in range(N):
                if q != o:
                    s = pos[q, o]; P[s] = left[at:at + len(s)]; at += len(s)
        go = np.nonzero(P >= 0)[0]; r = go // V
        x[r, g, :, go - r * V] = al[:, P[go]].T
        P[P < 0] = rng.permutation(np.setdiff1d(np.arange(N * V), P)); p[g, face[g]] = P
def plant(P, at, val):
    i = int(np.argmax(P == val)); P[i] = P[at]; P[at] = val
def setup_inputs(rng):
    return pack(*parts(rng))
def setup_inputs_corners(rng):
    c, z, e, p, j, x = parts(rng); even(c, j); cnt = np.zeros((8, N, N), np.int64); many = B // 2
    face = rng.integers(0, K, 8); face[0] = K - 1; face[7] = 0
    for g in range(8):
        room = [V] * N
        for q in range(N):
            left = B
            for h in [1] + [int(a) for a in rng.permutation(N) if a != 1]:
                o = (q + h) % N; n = int(rng.choice(np.array([0, 1, CAP - 1, CAP, CAP + 1, many])))
                if q == 0 and h == 1: n = (CAP, CAP + 1, many, CAP - 1, 1, 0, CAP, CAP)[g]
                n = min(n, left, room[o]); cnt[g, q, o] = n; left -= n; room[o] -= n
    steer(rng, c, p, x, cnt, face)
    for g in (1, 5): p[g, (face[g] + 1) % K] = np.arange(N * V)
    m = rng.random((N, 4, 1, V)) < 0.5
    e[:, ::2] = np.where(m, rng.choice(np.array([0, NC - 1, NC, R * NC - 1, R * NC, ZP - 1]), (N, 4, K, V)), e[:, ::2])
    return pack(c, z, e, p, j, x)
def setup_inputs_crowd(rng):
    c, z, e, p, j, x = parts(rng); even(c, j); cnt = np.zeros((8, N, N), np.int64); face = rng.integers(0, K, 8); last = np.full((8, N), -1)
    for g in range(8):
        for q in range(N):
            n = int(rng.choice(np.array([B, B - 1, B // 2, 0])))
            if q == 0: n = B
            if q == 1: n = B - 1 if g == 0 else B
            if q == 2 and g % 2 == 1: n = min(n, B // 2)
            cnt[g, q, (q + g) % N] = n
        if g % 2 == 1:
            n = int(rng.choice(np.array([1, CAP]))); o = (g + 2) % N
            if g == 7: n = CAP
            cnt[g, 0, g % N] -= n; cnt[g, 0, o] += n; last[g, 0] = o
    steer(rng, c, p, x, cnt, face, last)
    return pack(c, z, e, p, j, x)
def setup_inputs_ties(rng):
    c, z, e, p, j, x = parts(rng)
    c = rng.integers(0, 9, c.shape); z = rng.integers(0, 9, z.shape); j = rng.integers(0, 9, j.shape); x = rng.integers(0, 9, x.shape)
    c[:, ::2, :, 1::2] = c[:, ::2, :, 0::2]
    z[:, 3] = rng.integers(128, 136, z[:, 3].shape); z[:, 5] = rng.integers(248, 256, z[:, 5].shape)
    e = np.where(rng.random((N, 8, 1, V)) < 0.6, rng.integers(0, ZP, (N, 8, 1, V)), rng.integers(0, ZP, (N, 8, K, V)))
    i = np.concatenate([np.array([0, B - 1]), 1 + rng.permutation(B - 2)[:6]])
    c[..., i] = 8; x[..., i] = 2; j[..., 0] = 0; z[..., ZP - 2:] = 8; z[:, :, 15, ZP - 2] = 7
    e[:, :, :K // 2, i] = ZP - 1; e[:, :, K // 2:, i] = ZP - 2
    return pack(c, z, e, p, j, x)
def setup_inputs_spread(rng):
    c, z, e, p, j, x = parts(rng)
    c, z, j, x = [(np.exp2(8 * rng.random((N, 8, 1, n))) * rng.random((N, 8, 16, n))).astype(np.int64) for n in (V, ZP, M, V)]
    e = np.minimum((ZP * rng.random(e.shape) ** 3).astype(np.int64), ZP - 1)
    return pack(c, z, e, p, j, x)
def setup_inputs_ends(rng):
    p = np.argsort(rng.random((8, K, N * V)), axis=-1)
    c, z, j, x = [255 * (rng.random((N, 8, 16, n)) < rng.choice(np.array([0.0, 0.1, 0.5, 0.9, 1.0]), (N, 8, 1, n))).astype(np.int64) for n in (V, ZP, M, V)]
    e = (ZP - 1) * rng.integers(0, 2, (N, 8, K, V))
    z[..., 0] = 255; z[..., ZP - 1] = 0; j[..., 65280 & (M - 1)] = 0
    for a, b in ((0, 1), (V - 1, V - 2)):
        c[..., a] = 0; c[..., b] = 255; x[..., a] = 255; e[..., a] = ZP - 1
    for a in (2, B - 3):
        c[..., a] = 0; x[..., a] = 255
    for g in range(8):
        for k in range(K):
            for a in range(N):
                o = ((a + 1) % N) * V; near = (g + k) % 2 == 0
                plant(p[g, k], a * V, o + (1 if near else 0)); plant(p[g, k], a * V + V - 1, o + (V - 2 if near else V - 1))
                plant(p[g, k], a * V + 2, o + 2); plant(p[g, k], a * V + B - 3, o + B - 3)
    u = rng.random((N, 1, V)); nz = np.where(u < 0.5, 8, np.where(u < 0.95, 7, 0))
    c[:, 6] = np.where(np.arange(16)[None, :, None] < nz, 0, 255); z[:, 6] = 255; x[:, 6] = 255; j[:, 6] = 0; e[:, 6] = ZP - 1
    return pack(c, z, e, p, j, x)
def check_inputs(d):
    bad = []
    for k, hi in (("cen", 255), ("pl", 255), ("jmp", 255), ("wk", 255), ("ent", ZP - 1), ("nb", N * V - 1)):
        v = np.asarray(d[k]).astype(np.float32)
        if not np.all((v >= 0) & (v <= hi) & (v == np.floor(v))): bad.append("range of " + k)
    a = np.stack([gentries(q) for q in d["nb"]]).reshape(N, 8, PH, K, B).transpose(1, 3, 0, 2, 4).reshape(8, K, N * V)
    if np.any(np.sort(a, axis=-1) != np.arange(N * V)): bad.append("neighbours k of all boxes all different")
    return bad
def reference(cen, pl, ent, nb, jmp, wk):
    C, Z, D, X = [a.astype(np.float32).astype(np.int32).reshape(N, 8, 16, -1) for a in (cen, pl, jmp, wk)]
    E = ent.astype(np.int32).reshape(N, 8, PH, K, B); F = np.ones((N, 8, PH, K, B), np.int32)
    L = np.stack([gentries(a) for a in nb]).reshape(N, 8, PH, K, B); A = [0] * N
    w = (2 * np.arange(16, dtype=np.int32) + 1)[None, None, :, None]
    for t in range(R):
        b = t % PH; lo, hi = b * B, b * B + B
        x = X[..., lo:hi]; ix = np.add.reduce(w * x, axis=2) & (M - 1)
        y = np.abs(x - np.take_along_axis(D, ix[:, :, None, :], 3))
        al = np.ascontiguousarray(C.transpose(1, 2, 0, 3)).reshape(8, 16, N * V)
        outs = []
        for q in range(N):
            c = C[q, :, :, lo:hi].astype(np.int32); yq = y[q]; n = L[q, :, b]
            v = np.take_along_axis(al, n.reshape(8, 1, K * B), 2).reshape(8, 16, K, B)
            d = np.add.reduce(np.abs(v - yq[:, :, None, :]), axis=1)
            k = np.argmin(d, axis=1); own = np.add.reduce(np.abs(c - yq), axis=1)
            go = np.min(d, axis=1) + (A[q] & 63) < own
            s = np.take_along_axis(Z[q], E[q, :, b].reshape(8, 1, K * B), 2).reshape(8, 16, K, B)
            h = np.add.reduce(np.abs(s - c[:, :, None, :]), axis=1)
            P = np.add.accumulate(F[q, :, b] * np.maximum(TH - h, 0), axis=1)
            u = np.add.reduce(yq, axis=1) & 63
            ok = 64 * P > (u * P[:, K - 1])[:, None, :]
            first = np.argmax(ok, axis=1)
            z = np.take_along_axis(s, first[:, None, None, :], 2)[:, :, 0]
            z = np.where(np.any(ok, axis=1)[:, None, :], z, c)
            new = np.where(go[:, None, :], z, yq)
            X[q, :, :, lo:hi] = new; C[q, :, :, lo:hi] = c + np.clip(new - c, -1, 1)
            A[q] = int(np.count_nonzero(go))
            outs.append((go, np.take_along_axis(n, k[:, None, :], 1)[:, 0], k))
        land = np.zeros((N, 8, 16, NC), np.int32)
        for q in range(N):
            go, to, k = outs[q]
            for o in range(N):
                hit = go & (to // V == o); at = np.add.accumulate(hit.astype(np.int64), axis=1) - 1
                g, i = np.nonzero(hit & (at < CAP)); s = q * CAP + at[g, i]
                land[o][g, :, s] = y[q][g, :, i]
                v = to[g, i] - o * V; bl = v // B; row = k[g, i] ^ 1
                E[o][g, bl, row, v - bl * B] = NC * t + s
                F[o][g, bl, row, v - bl * B] += 1
        Z[..., NC * t:NC * t + NC] = land
    return {"yc": C.reshape(N, 128, V).astype(np.float32).astype(BF), "yx": X.reshape(N, 128, V).astype(np.float32).astype(BF), "yz": Z.reshape(N, 128, ZP).astype(np.float32).astype(BF),
            "ye": E.reshape(N, 8, K * V).astype(np.float32), "yn": F.reshape(N, 8, K * V).astype(np.float32).astype(BF)}

@@ -1,0 +1,800 @@
+from concourse.bass import DstId, RemoteDMATransfer
+from concourse.mybir import AluOpType as OP, ActivationFunctionType as AF
+
+R = 4
+BF, F32, I32, U16 = "bfloat16", "float32", "int32", "uint16"
+D_PATH = ["CCCA", "CCCA", "CCCA", "CCCA"]
+H_BY_VECTOR = [(), (), (7,), ()]
+
+SCRATCH = {
+    "CA0": ("sbuf", [128, 4096], BF), "CA1": ("sbuf", [128, 4096], BF), "CA2": ("sbuf", [128, 4096], BF), "CA3": ("sbuf", [128, 4096], BF),
+    "HW0": ("sbuf", [128, 5136], BF), "HW1": ("sbuf", [128, 5136], BF),
+    "ZW": ("sbuf", [128, 3584], BF), "EW": ("sbuf", [128, 4608], BF), "MT": ("sbuf", [128, 4096], BF),
+    "AG": ("sbuf", [128, 4096], BF), "MX": ("sbuf", [128, 4096], BF), "MH": ("sbuf", [128, 4096], BF),
+    "JT": ("sbuf", [128, 512], BF), "WK": ("sbuf", [128, 512], BF), "XB": ("sbuf", [128, 512], BF), "JG": ("sbuf", [128, 512], BF),
+    "OA": ("sbuf", [128, 512], BF), "CM": ("sbuf", [128, 512], BF), "TM": ("sbuf", [128, 512], BF), "MS": ("sbuf", [128, 512], BF),
+    "XO": ("sbuf", [128, 512], BF), "CO": ("sbuf", [128, 512], BF),
+    "SB": ("sbuf", [128, 896], BF), "YS": ("sbuf", [128, 1536], BF), "VT": ("sbuf", [128, 384], BF), "VB": ("sbuf", [128, 384], BF),
+    "P1": ("sbuf", [128, 384], BF), "P2": ("sbuf", [128, 384], BF), "S48": ("sbuf", [128, 384], BF),
+    "META": ("sbuf", [128, 128], U16), "LM": ("sbuf", [128, 128], U16),
+    "NBI": ("sbuf", [128, 256], I32), "NX": ("sbuf", [128, 512], F32), "NT": ("sbuf", [128, 512], F32),
+    "NI": ("sbuf", [128, 256], I32), "N1": ("sbuf", [128, 256], I32), "N2": ("sbuf", [128, 256], I32), "N3": ("sbuf", [128, 256], I32),
+    "N4": ("sbuf", [128, 256], F32), "N5": ("sbuf", [128, 256], F32),
+    "NL0": ("sbuf", [128, 256], U16), "NL1": ("sbuf", [128, 256], U16), "EU": ("sbuf", [128, 256], U16),
+    "EI": ("sbuf", [128, 256], I32), "E1": ("sbuf", [128, 256], I32), "E2": ("sbuf", [128, 256], I32),
+    "ELO": ("sbuf", [128, 256], BF), "EHI": ("sbuf", [128, 256], BF),
+    "KHI": ("sbuf", [128, 256], BF), "KLO": ("sbuf", [128, 256], BF), "TLO": ("sbuf", [128, 256], BF), "THI": ("sbuf", [128, 256], BF),
+    "CT": ("sbuf", [128, 256], BF), "C8": ("sbuf", [128, 256], BF), "KX": ("sbuf", [128, 256], BF), "RT": ("sbuf", [128, 256], BF),
+    "M32": ("sbuf", [128, 256], BF), "M8": ("sbuf", [128, 256], F32), "KN": ("sbuf", [128, 256], BF),
+    "SG": ("sbuf", [128, 1024], BF), "RG": ("sbuf", [128, 256], F32), "G2": ("sbuf", [128, 256], F32), "PP": ("sbuf", [128, 256], F32),
+    "NC": ("sbuf", [128, 256], BF), "HIT": ("sbuf", [128, 256], BF), "INC": ("sbuf", [128, 256], BF), "PRD": ("sbuf", [128, 256], BF),
+    "EF": ("sbuf", [128, 256], F32), "EG": ("sbuf", [128, 256], F32), "NF": ("sbuf", [128, 256], BF),
+    "COL": ("sbuf", [128, 144], F32), "PI": ("sbuf", [128, 8], I32), "PF": ("sbuf", [128, 24], F32),
+    "WS": ("sbuf", [128, 9 * 144], BF), "ID": ("sbuf", [128, 128], BF), "NID": ("sbuf", [128, 128], BF), "IH": ("sbuf", [128, 128], BF),
+    "IG": ("sbuf", [128, 128], BF), "I32": ("sbuf", [128, 128], F32), "IS": ("sbuf", [128, 128], F32),
+    "ZID": ("sbuf", [128, 128], BF), "TRI": ("sbuf", [128, 128], BF), "TA": ("sbuf", [128, 128], BF), "TB": ("sbuf", [128, 128], BF), "ONE": ("sbuf", [128, 128], BF),
+    "LI": ("sbuf", [128, 96], I32), "LU": ("sbuf", [128, 128], U16),
+    "WF": ("sbuf", [128, 640], F32), "WI": ("sbuf", [128, 256], I32), "WU": ("sbuf", [128, 160], U16), "GO": ("sbuf", [128, 32], BF),
+    "SY2": ("sbuf", [128, 64], F32), "SC2": ("sbuf", [128, 64], F32), "RUN": ("sbuf", [128, 64], F32),
+    "B0": ("psum", [128, 512], F32), "B1": ("psum", [128, 512], F32), "B2": ("psum", [128, 512], F32), "B3": ("psum", [128, 512], F32),
+    "B4": ("psum", [128, 512], F32), "B5": ("psum", [128, 512], F32), "B6": ("psum", [128, 512], F32), "B7": ("psum", [128, 512], F32),
+}
+SEMAPHORES = (["qV", "qS", "qP", "qG", "lcen", "lent", "lpl", "lwk", "ljt", "lnb", "dew", "dmt", "oz0", "oz1", "oc", "ox", "oe", "on"]
+              + ["%s%s%d" % (a, k, t) for a in "lah" for k in "cmy" for t in range(R)])
+
+
+def bits(engs):
+    m = 0
+    for e in engs:
+        m |= 1 << e
+    return m
+
+
+def deal(engs, n):
+    w = 1
+    while 2 * w * n <= len(engs):
+        w *= 2
+    return [engs[i * w:(i + 1) * w] for i in range(n)]
+
+
+def plans(T, topo):
+    out = {"first": [], "later": [], "exits": [], "direct": []}
+    for c in T.cores:
+        mate, plane, far = [], [], []
+        for o, d in enumerate(T.cores):
+            if d != c:
+                a, b = topo.chip(c), topo.chip(d)
+                (mate if topo.mates(a, b) else plane if topo.same_plane(a, b) else far).append(o)
+        free = [h for h in topo.cores_of(c) if h not in T.cores]
+        port = [h for h in free if all(topo.may_write(h, T.cores[o]) for o in mate + far)]
+        there = [h for h in port if topo.die(h) != topo.die(c)][:2]
+        here = [h for h in port if topo.die(h) == topo.die(c)][0]
+        plain = [h for h in free if topo.die(h) == topo.die(c) and h != here][0]
+        two = {h: far[i::len(there)] for i, h in enumerate(there)}
+        out["later"].append((mate + plane, two))
+        out["first"].append(([], {**two, here: mate + plane[:1], plain: plane[1:]}))
+        out["direct"].append((mate + plane + far, {}))
+        out["exits"].append(([], {here: mate + far, plain: plane}))
+    return out
+
+
+def masks(T, topo, plan, q, keep):
+    c = T.cores[q]
+    near, hs = plan[q]
+    off = topo.engines(c, T.cores[(q + 1) % len(T.cores)])
+    if not hs:
+        return deal(off, len(near)), []
+    on = topo.engines(c, list(hs)[0])
+    if near or keep:
+        on = [e for e in on if e not in off]
+    return (deal(off, len(near)) if near else []), deal(on, len(hs))
+
+
+def helper_masks(T, topo, h, far):
+    return deal(topo.engines(h, T.cores[far[0]]), len(far))
+
+
+def counts(T, topo, plan, keep):
+    cnt, hc = [0] * len(T.cores), {}
+    for q in range(len(T.cores)):
+        near, hs = plan[q]
+        m1, m2 = masks(T, topo, plan, q, keep)
+        for o, m in zip(near, m1):
+            cnt[o] += len(m)
+        for h, m in zip(hs, m2):
+            hc[h] = len(m)
+            for o, m3 in zip(hs[h], helper_masks(T, topo, h, hs[h])):
+                cnt[o] += len(m3)
+    return cnt, hc
+
+
+def dst(topo, c):
+    a = topo.addr(c)
+    return DstId(rid=a[0], pnc=a[1])
+
+
+def pieces(T, kind, t):
+    if kind == "c":
+        ca = T["CA%d" % t]
+        return None, None, lambda q: ca[:, 512 * q:512 * q + 512]
+    if kind == "m":
+        return (T.META[:, 32 * t:32 * t + 24], lambda o: T.META[:, 32 * t + 3 * o:32 * t + 3 * o + 3],
+                lambda q: T.LM[:, 32 * t + 3 * q:32 * t + 3 * q + 3])
+    base = 2048 + 384 * t
+    return (T.YS[:, 384 * t:384 * t + 384], lambda o: T.YS[:, 384 * t + 48 * o:384 * t + 48 * o + 48],
+            lambda q: T.ZW[:, base + 48 * q:base + 48 * q + 48])
+
+
+def exchange(kind, t):
+    if kind == "c":
+        return "first" if t == 0 else "later", False
+    if t % 2:
+        return "direct" if kind == ("m" if t == R - 1 else "y") else "exits", True
+    return "exits", True
+
+
+def helper_program(g, core, T, topo, pl):
+    ends = []
+    for t in range(R):
+        for kind in "cmy":
+            name, keep = exchange(kind, t)
+            for q in range(len(T.cores)):
+                far = pl[name][q][1].get(core)
+                if not far:
+                    continue
+                whole, part, land = pieces(T, kind, t)
+                ms = helper_masks(T, topo, core, far)
+                g.wait_ge(T.sem["h%s%d" % (kind, t)], counts(T, topo, pl[name], keep)[1][core])
+                g.remote_dma_fused([RemoteDMATransfer(dst_ids=[dst(topo, T.cores[o])], dma_engine_mask=bits(m), remote_sem=T.sem["a%s%d" % (kind, t)],
+                                                      src=part(o) if part else land(q), dst=land(q)) for o, m in zip(far, ms)],
+                                   local_sem=T.sem["l%s%d" % (kind, t)])
+                ends.append(("l%s%d" % (kind, t), sum(len(m) for m in ms)))
+    for sem, n in ends:
+        g.wait_ge(T.sem[sem], n)
+
+
+def rank_program(g, core, T, topo):
+    pl = plans(T, topo)
+    q = T.rank_of(core)
+    if q is None:
+        helper_program(g, core, T, topo, pl)
+        return
+    Q = {"V": g.vector, "S": g.scalar, "P": g.tensor, "G": g, "Y": g.sync}
+    V, S, PE = g.vector, g.scalar, g.tensor
+    known = {e: {} for e in Q}
+    count, wr, rd, bank = {}, {}, {}, {}
+
+    def need(e, tok):
+        sem, val, clock = tok
+        if known[e].get(sem, 0) >= val:
+            return
+        Q[e].wait_ge(T.sem[sem], val)
+        known[e][sem] = val
+        for s, v in clock.items():
+            if known[e].get(s, 0) < v:
+                known[e][s] = v
+
+    def op(e, fn, r=(), w=(), b=(), sem=None, inc=1, total=None):
+        toks = [wr[x] for x in r if x in wr] + [wr[x] for x in w if x in wr]
+        for x in w:
+            toks += rd.get(x, [])
+        for x in b:
+            toks += [tk for ee, tk in bank.get(x, {}).items() if ee != e]
+        toks.sort(key=lambda tk: -tk[1])
+        for tk in toks:
+            if not (e == "P" and tk[0] == "qP"):
+                need(e, tk)
+        res = fn()
+        if sem is None:
+            sem = "q" + e
+            res.then_inc(T.sem[sem], 1)
+        count[sem] = count.get(sem, 0) + inc
+        tok = (sem, total or count[sem], dict(known[e]))
+        for x in r:
+            rd.setdefault(x, []).append(tok)
+        for x in w:
+            wr[x] = tok
+            rd[x] = []
+        for x in b:
+            bank.setdefault(x, {})[e] = tok
+        return tok
+
+    def dma(e, pairs, sem, r=(), w=(), total=None):
+        def fn():
+            for o, i in pairs:
+                Q[e].dma_start(o, i).then_inc(T.sem[sem], 16)
+        return op(e, fn, r, w, sem=sem, inc=16 * len(pairs), total=total)
+
+    def ts(out, in0, s1, s2, o0, o1=None):
+        if o1 is None:
+            return lambda: V.tensor_scalar(out, in0, s1, None, o0)
+        return lambda: V.tensor_scalar(out, in0, s1, s2, o0, o1)
+
+    def tt(out, a, b, o):
+        return lambda: V.tensor_tensor(out, a, b, o)
+
+    def cp(out, a):
+        return lambda: V.tensor_copy(out, a)
+
+    def act(out, a, f, **kw):
+        return lambda: S.activation(out, a, f, **kw)
+
+    def mm(items, start=True, stop=True):
+        def fn():
+            for n, (o, l, x) in enumerate(items):
+                res = PE.matmul(o, l, x, start and n == 0, stop and n == len(items) - 1)
+            return res
+        return fn
+
+    W1, WM2, W4096, WM2048, W2048, WJ, WE, WT, WY = range(9)
+
+    def sel(out, wi, src):
+        return [(out, T.WS[:, 144 * wi + 15 - r:144 * wi + 143 - r], src(r)) for r in range(16)]
+
+    def iota(out, pat, base, name):
+        op("G", lambda: g.iota(out, pat, base, 0, allow_small_or_imprecise_dtypes=True), w=[name])
+
+    def wf(j):
+        return T.WF[:, 32 * j:32 * j + 32]
+
+    def wi_(j):
+        return T.WI[:, 32 * j:32 * j + 32]
+
+    def wu(j):
+        return T.WU[:, 32 * j:32 * j + 32]
+
+    def pf(j):
+        return T.PF[:, j:j + 1]
+
+    HW = [T.HW0, T.HW1]
+    CA = [T["CA%d" % t] for t in range(R)]
+
+    def send(kind, t, name, landed, src=None, own=True):
+        plan, keep = exchange(kind, t)
+        near, hs = pl[plan][q]
+        m1, m2 = masks(T, topo, pl[plan], q, keep)
+        whole, part, land = pieces(T, kind, t)
+        a, h_, l = ("%s%s%d" % (x, kind, t) for x in "ahl")
+        tr = [RemoteDMATransfer(dst_ids=[dst(topo, T.cores[o])], dma_engine_mask=bits(m), remote_sem=T.sem[a],
+                                src=src if part is None else part(o), dst=land(q)) for o, m in zip(near, m1)]
+        tr += [RemoteDMATransfer(dst_ids=[dst(topo, h)], dma_engine_mask=bits(m), remote_sem=T.sem[h_], src=src if part is None else whole,
+                                 dst=land(q) if part is None else whole) for h, m in zip(hs, m2)]
+        op("G", lambda: g.remote_dma_fused(tr, local_sem=T.sem[l]), r=[name], sem=l, inc=sum(len(m) for m in m1 + m2))
+        total = counts(T, topo, pl[plan], keep)[0][q]
+        if own:
+            total += 16
+            dma("Y", [(land(q), src if part is None else part(q))], a, r=[name], total=total)
+        count[a] = total
+        wr[landed] = (a, total, {})
+
+    own0 = CA[0][:, 512 * q:512 * q + 512]
+    dma("Y", [(own0, T.cen[:])], "lcen", w=["cen"])
+    dma("S", [(T.ZW[:, 0:2048], T.pl[:])], "lpl", w=["Z"])
+    dma("Y", [(T.EI[:, 32 * k:32 * k + 32], T.ent[:, 512 * k:512 * k + 512]) for k in range(8)], "lent", w=["EI"])
+    dma("S", [(T.WK[:], T.wk[:])], "lwk", w=["WK"])
+    dma("S", [(T.JT[:], T.jmp[:])], "ljt", w=["JT"])
+    dma("S", [(T.NBI[:], T.nb[:])], "lnb", w=["NBI"])
+    op("G", lambda: g.iota(T.PI[:, 0:1], [[0, 1]], 0, 1), w=["PI0"])
+    iota(T.COL[:], [[1, 144]], 0, "COL")
+    op("G", lambda: g.iota(T.LI[:, 0:32], [[32, 8], [1, 2], [0, 2]], 0, 0), w=["LI0"])
+    op("G", lambda: g.iota(T.LI[:, 32:64], [[1, 16], [256, 2]], 0, 0), w=["LI1"])
+    iota(T.CT[:], [[0, 8], [1, 32]], 0, "CT")
+    iota(T.C8[:], [[0, 8], [8, 32]], 0, "C8")
+    send("c", 0, "cen", "CA0", src=own0, own=False)
+    iota(T.KX[:], [[64, 4], [-32, 2], [0, 32]], 32, "KX")
+    iota(T.KHI[:], [[256, 8], [0, 32]], 0, "KHI")
+    iota(T.MT[:], [[0, 4096]], 0, "MT")
+    iota(T.S48[:], [[0, 8], [1, 48]], 0, "S48")
+    iota(T.P1[:], [[0, 3], [1, 128]], 0, "P1")
+    iota(T.P2[:], [[1, 3], [0, 128]], 0, "P2")
+    iota(T.EW[:, 0:2048], [[0, 2048]], 0, "EW")
+
+    op("V", ts(T.PI[:, 1:2], T.PI[:, 0:1], 15, None, OP.bitwise_and), r=["PI0"], w=["PI1"])
+    op("V", ts(T.PI[:, 2:3], T.PI[:, 0:1], 112, None, OP.bitwise_and), r=["PI0"], w=["PI2"])
+    op("V", ts(T.PI[:, 3:4], T.PI[:, 0:1], 31, None, OP.bitwise_and), r=["PI0"], w=["PI3"])
+    op("V", cp(T.PF[:, 0:4], T.PI[:, 0:4]), r=["PI0", "PI1", "PI2", "PI3"], w=["PF0"])
+    op("V", lambda: V.memset(pf(12), 0.0), w=["A"])
+    op("V", ts(pf(2), pf(2), 15.0, None, OP.add), r=["PF0"], w=["PF2"])
+    op("V", ts(pf(8), pf(1), 32.0, None, OP.mult), r=["PF0"], w=["PF8"])
+    op("V", ts(pf(9), pf(1), 2.0, 1.0, OP.mult, OP.add), r=["PF0"], w=["PF9"])
+    op("V", ts(pf(10), pf(1), 2.0, None, OP.mult), r=["PF0"], w=["PF10"])
+    op("V", ts(T.PF[:, 4:8], T.COL[:, 0:4], pf(1), None, OP.is_equal), r=["PF0", "COL"], w=["PF4"])
+    op("V", ts(T.LU[:, 0:32], T.COL[:, 0:32], pf(8), None, OP.add), r=["PF8", "COL"], w=["LU0"])
+    op("V", ts(T.ID[:], T.COL[:, 0:128], pf(0), None, OP.is_equal), r=["PF0", "COL"], w=["ID"])
+
+    def weights(j, s, deps=()):
+        op("V", ts(T.WS[:, 144 * j:144 * j + 144], T.COL[:], pf(2), s, OP.is_equal, OP.mult), r=["PF2", "COL"] + list(deps), w=["WS%d" % j])
+
+    def scaled_identity(out, s, name):
+        op("V", ts(out, T.COL[:, 0:128], pf(0), s, OP.is_equal, OP.mult), r=["PF0", "COL"], w=[name])
+    weights(WJ, pf(9), ["PF9"])
+    weights(W1, 1.0)
+    scaled_identity(T.NID[:], -1.0, "NID")
+    scaled_identity(T.I32[:], 1.0, "I32")
+    weights(WM2, -2.0)
+    weights(W2048, 2048.0)
+    op("V", ts(T.LU[:, 32:64], T.LI[:, 0:32], pf(10), None, OP.add), r=["PF10", "LI0"], w=["LU1"])
+    op("V", ts(T.LU[:, 64:80], T.COL[:, 0:16], 32.0, pf(3), OP.mult, OP.add), r=["PF0", "COL"], w=["LU2"])
+    scaled_identity(T.IS[:], -2048.0, "IS")
+    weights(W4096, 4096.0)
+    weights(WM2048, -2048.0)
+    op("S", act(T.HW0[:, 4096:4608], own0.indirect(T.LU[:, 0:32]), AF.Copy), r=["cen", "LU0"], w=["C0"])
+    op("S", act(T.XB[:], T.WK[:, 0:512].indirect(T.LU[:, 0:32]), AF.Copy), r=["WK", "LU0"], w=["X"])
+
+    def consts_choice():
+        scaled_identity(T.IH[:], 0.5, "IH")
+        op("V", lambda: V.memset(T.ZID[:], 0.0), w=["ZID"])
+        op("V", lambda: V.memset(T.KN[:], 2.0), w=["KN"])
+        op("V", lambda: V.memset(T.M8[:], 1.0), w=["M8"])
+        op("V", lambda: V.memset(T.M32[:], 1.0), w=["M32"])
+        op("V", lambda: V.memset(T.M8[:, 0:256:8], 0.0), w=["M8"])
+        op("V", lambda: V.memset(T.M32[:, 0:256:32], 0.0), w=["M32"])
+
+    def consts_exits():
+        scaled_identity(T.IG[:], -1024.0, "IG")
+        op("V", ts(pf(11), pf(1), 256.0, None, OP.mult), r=["PF0"], w=["PF11"])
+        op("V", ts(pf(15), pf(5), 256.0, pf(4), OP.mult, OP.add), r=["PF4"], w=["PF15"])
+        op("V", ts(pf(16), pf(7), 16.0, pf(6), OP.mult, OP.add), r=["PF4"], w=["PF16"])
+        op("V", ts(pf(17), pf(4), float(64 * (q & 3)), None, OP.mult), r=["PF4"], w=["PF17"])
+        op("V", ts(wf(0), T.COL[:, 0:32], 16.0, pf(1), OP.mult, OP.add), r=["PF0", "COL"], w=["m"])
+        op("V", ts(pf(18), pf(5), float(16 + (q >> 2)), pf(17), OP.mult, OP.add), r=["PF4", "PF17"], w=["PF18"])
+        op("V", ts(T.TA[:], T.COL[:, 0:128], pf(0), None, OP.is_gt), r=["PF0", "COL"], w=["TA"])
+        op("V", ts(T.TB[:], T.COL[:, 0:128], pf(2), None, OP.is_le), r=["PF2", "COL"], w=["TB"])
+        op("V", ts(pf(19), pf(7), 32.0, pf(18), OP.mult, OP.add), r=["PF4", "PF18"], w=["PF19"])
+        op("V", ts(wf(1), wf(0), 4608.0, None, OP.add), r=["m"], w=["my"])
+        weights(WT, pf(15), ["PF15"])
+        weights(WY, pf(16), ["PF16"])
+        op("V", lambda: V.memset(T.ONE[:], 1.0), w=["ONE"])
+        op("V", tt(T.TRI[:], T.TA[:], T.TB[:], OP.mult), r=["TA", "TB"], w=["TRI"])
+        op("V", lambda: V.memset(T.HW0[:, 5120:5136], 0.0), w=["zero0"])
+        op("V", lambda: V.memset(T.HW1[:, 5120:5136], 0.0), w=["zero1"])
+
+    def neighbours_a():
+        op("V", cp(T.NX[:], T.NBI[:, 0:256].indirect(T.LU[:, 32:64])), r=["NBI", "LU1"], w=["NX"])
+        op("V", lambda: V.transpose(T.NT[:], T.NX[:]), r=["NX"], w=["NT"])
+        op("V", cp(T.NI[:], T.NT[:, 0:512].indirect(T.LU[:, 64:80])), r=["NT", "LU2"], w=["NI"])
+
+    def neighbours_b():
+        op("V", cp(T.NL0[:], T.NI[:]), r=["NI"], w=["NL0"])
+        op("V", ts(T.N1[:], T.NI[:], 9, None, OP.arith_shift_right), r=["NI"], w=["N1"])
+        op("V", ts(T.N2[:], T.NI[:], 31, None, OP.bitwise_and), r=["NI"], w=["N2"])
+        op("V", tt(T.KLO[:], T.N1[:], T.C8[:], OP.add), r=["N1", "C8"], w=["KLO"])
+
+    def neighbours_c():
+        op("V", ts(T.N3[:], T.NI[:], 5, 15, OP.arith_shift_right, OP.bitwise_and), r=["NI"], w=["N3"])
+        op("V", tt(T.TLO[:], T.N2[:], T.KX[:], OP.add), r=["N2", "KX"], w=["TLO"])
+        op("V", cp(T.THI[:], T.N3[:]), r=["N3"], w=["THI"])
+        op("V", ts(T.RT[:], T.CT[:], 0.0, pf(1), OP.mult, OP.add), r=["CT", "PF0"], w=["RT"])
+        dma("Y", [(T.MT[f:128:16, :], x[:]) for f, x in enumerate((T.TLO, T.THI, T.RT, T.CT))], "dmt",
+            r=["TLO", "THI", "RT", "CT"], w=["MT"])
+
+    def neighbours_d():
+        op("V", ts(T.N4[:], T.N1[:], 512.0, None, OP.mult), r=["N1"], w=["N4"])
+        op("V", ts(T.N5[:], T.N2[:], 16.0, None, OP.mult), r=["N2"], w=["N5"])
+        op("V", tt(T.N4[:], T.N4[:], T.N3[:], OP.add), r=["N4", "N3"], w=["N4"])
+        op("V", tt(T.N4[:], T.N4[:], T.N5[:], OP.add), r=["N4", "N5"], w=["N4"])
+        op("V", cp(T.NL1[:], T.N4[:]), r=["N4"], w=["NL1"])
+
+    def entries_0():
+        op("V", ts(T.E1[:], T.EI[:], 127, None, OP.bitwise_and), r=["EI"], w=["E1"])
+        op("V", ts(T.E2[:], T.EI[:], 7, None, OP.arith_shift_right), r=["EI"], w=["E2"])
+        op("V", cp(T.ELO[:], T.E1[:]), r=["E1"], w=["ELO"])
+        op("V", cp(T.EHI[:], T.E2[:]), r=["E2"], w=["EHI"])
+        op("V", lambda: V.memset(T.EW[:, 2048:4608], 0.0), w=["EWb"])
+        dma("Y", [(T.EW[0:128:16, 0:4096], T.ELO[:]), (T.EW[1:128:16, 0:4096], T.EHI[:])], "dew", r=["ELO", "EHI"], w=["EW", "EWb"])
+        op("V", ts(T.P1[:], T.P1[:], pf(4), None, OP.mult), r=["P1", "PF4"], w=["P1"])
+        op("V", ts(T.P2[:], T.P2[:], pf(5), None, OP.mult), r=["P2", "PF4"], w=["P2"])
+        op("V", ts(T.PF[:, 20:24], T.COL[:, 0:4], 3.0, 16.0, OP.mult, OP.add), r=["COL"], w=["PF20"])
+        op("V", ts(pf(14), pf(5), 128.0, pf(4), OP.mult, OP.add), r=["PF4"], w=["PF14"])
+        op("V", ts(pf(13), pf(1), 16.0, None, OP.mult), r=["PF0"], w=["PF13"])
+        op("V", tt(T.VB[:], T.P1[:], T.P2[:], OP.add), r=["P1", "P2"], w=["VB"])
+        op("V", ts(T.PF[:, 20:24], T.PF[:, 20:24], pf(5), None, OP.mult), r=["PF20", "PF4"], w=["PF20"])
+        weights(WE, pf(14), ["PF14"])
+        op("V", ts(T.LU[:, 96:128], T.LI[:, 32:64], pf(13), None, OP.add), r=["PF13", "LI1"], w=["LU3"])
+
+    def y_a(t):
+        op("P", mm(sel(T.B7[:, 0:32], WJ, lambda r: T.XB[:, r:512:16])), r=["X", "WS5"], w=["jP"], b=[7])
+
+    def y_b(t):
+        op("V", cp(wi_(0), T.B7[:, 0:32]), r=["jP"], w=["ji"], b=[7])
+        op("V", ts(wi_(1), wi_(0), 511, None, OP.bitwise_and), r=["ji"], w=["ja"])
+        op("V", cp(wu(0), wi_(1)), r=["ja"], w=["ju"])
+
+    def y_c1(t):
+        op("S", act(T.JG[:], T.JT[:, 0:512].indirect(wu(0)), AF.Copy), r=["JT", "ju"], w=["JG"])
+        op("P", mm([(T.B2[:], T.ID[:], T.XB[:]), (T.B2[:], T.NID[:], T.JG[:])]), r=["X", "JG", "ID", "NID"], w=["B2"], b=[2])
+
+    def y_c2(t):
+        H, p = HW[t % 2], t % 2
+        C, Y = H[:, 4096:4608], H[:, 4608:5120]
+        op("S", act(Y, T.B2[:], AF.Abs), r=["B2"], w=["Y%d" % p], b=[2])
+        op("P", mm([(T.B0[:], T.ID[:], Y)]), r=["Y%d" % p], w=["B0"], b=[0])
+        op("P", mm(sel(T.B7[:, 160:224], W1, lambda r: H[:, 4096 + r:5120:16])), r=["C%d" % p, "Y%d" % p, "WS0"], w=["SyP"], b=[7])
+        op("P", mm([(T.B2[:], T.ID[:], C), (T.B2[:], T.NID[:], Y)]), r=["C%d" % p, "Y%d" % p], w=["B2"], b=[2])
+
+    def y_c3(t):
+        op("S", act(T.SC2[:, 0:32], T.B7[:, 160:192], AF.Copy), r=["SyP"], w=["SC2a"], b=[7])
+        op("S", act(T.SC2[:, 32:64], T.B7[:, 160:192], AF.Copy), r=["SyP"], w=["SC2b"], b=[7])
+        op("S", act(T.SY2[:, 0:32], T.B7[:, 192:224], AF.Copy), r=["SyP"], w=["SY2a"], b=[7])
+        op("S", act(T.SY2[:, 32:64], T.B7[:, 192:224], AF.Copy), r=["SyP"], w=["SY2b"], b=[7])
+        op("S", act(T.OA[:], T.B2[:], AF.Abs), r=["B2"], w=["OA"], b=[2])
+        op("P", mm(sel(T.B7[:, 64:96], W2048, lambda r: T.OA[:, r:512:16])), r=["OA", "WS4"], w=["ownP"], b=[7])
+
+    def y_d(t):
+        op("V", cp(wi_(2), T.SY2[:, 0:32]), r=["SY2a"], w=["ui"])
+        op("V", ts(wf(2), T.B7[:, 64:96], pf(12), None, OP.subtract), r=["ownP", "A"], w=["thr"], b=[7])
+        op("V", ts(wi_(3), wi_(2), 63, None, OP.bitwise_and), r=["ui"], w=["ua"])
+        op("V", ts(wf(3), wi_(3), 1.0 / 64, None, OP.mult), r=["ua"], w=["u64"])
+
+    def c_prep(t):
+        H, p = HW[t % 2], t % 2
+        op("P", mm([(T.B1[:], T.ID[:], H[:, 4096:4608])]), r=["C%d" % p, "ID"], w=["B1"], b=[1])
+
+    def c_bounds(t):
+        C = HW[t % 2][:, 4096:4608]
+        op("S", act(T.CM[:], C, AF.Identity, bias=-1.0), r=["C%d" % (t % 2)], w=["CM"])
+        op("S", act(T.B2[:], C, AF.Identity, bias=1.0), r=["C%d" % (t % 2)], w=["B2"], b=[2])
+
+    def h_get(t, k):
+        H, p = HW[t % 2], t % 2
+        src = T.ZW[:, 0:2048 + 384 * t].indirect(T.EU[:, 32 * k:32 * k + 32])
+        dep = ["Z", "EU%d" % min(k // 2, 1)] + ["L%d" % u for u in range(t)]
+        if k in H_BY_VECTOR[t]:
+            op("V", cp(H[:, 512 * k:512 * k + 512], src), r=dep, w=["s%d_%d" % (p, k)])
+        else:
+            op("S", act(H[:, 512 * k:512 * k + 512], src, AF.Copy), r=dep, w=["s%d_%d" % (p, k)])
+
+    def h_max(t, k):
+        H, p, c = HW[t % 2], t % 2, k // 2
+        op("V", tt(T.MH[:, 512 * k:512 * k + 512], H[:, 512 * k:512 * k + 512], T.B1[:], OP.max),
+           r=["s%d_%d" % (p, k), "B1"], w=["MH%d" % k], b=[1])
+        if k % 2:
+            if (t, c) not in summed:
+                h_sum(t, c)
+            op("P", mm(sel(T.B5[:, 64 * c:64 * c + 64], WM2, lambda r: T.MH[:, 1024 * c + r:1024 * c + 1024:16]), start=False, stop=k == 7),
+               r=["MH%d" % (k - 1), "MH%d" % k, "WS1"], w=["G"], b=[5])
+
+    summed = set()
+
+    def h_sum(t, c):
+        H, p = HW[t % 2], t % 2
+        out = T.B5[:, 64 * c:64 * c + 64]
+        head = [(T.B5[:, 0:256], T.ZID[:], T.M32[:])] if c == 0 else []
+        summed.add((t, c))
+        op("P", mm(head + [(out, T.I32[:], T.SC2[:])] + sel(out, W1, lambda r: H[:, 1024 * c + r:1024 * c + 1024:16]), start=c == 0, stop=False),
+           r=["SC2a", "SC2b", "I32", "ZID", "M32", "s%d_%d" % (p, 2 * c), "s%d_%d" % (p, 2 * c + 1)], w=["G"], b=[5])
+
+    def flux(t):
+        items = [(T.B6[:, 256:512], T.IH[:], T.KN[:])] + [(T.B6[:, 256:512], T.IH[:], T.SG[:, 256 * u:256 * u + 256]) for u in range(t)]
+        op("P", mm(items), r=["IH", "KN"] + ["SG%d" % u for u in range(t)], w=["n"], b=[6])
+
+    def choice_a(t):
+        op("S", act(T.RG[:], T.B5[:, 0:256], AF.Relu, bias=2047.0), r=["G"], w=["RG"], b=[5])
+
+    def choice_b(t):
+        for k in range(8):
+            op("V", tt(T.G2[:, k:256:8], T.RG[:, 32 * k:32 * k + 32], T.B6[:, 256 + 32 * k:288 + 32 * k], OP.mult),
+               r=["RG", "n"], w=["G2_%d" % k], b=[6])
+        op("V", lambda: V.tensor_tensor_scan(T.PP[:], T.M8[:], T.G2[:], 0.0, OP.mult, OP.add), r=["M8"] + ["G2_%d" % k for k in range(8)], w=["PP"])
+
+    def choice_c(t):
+        op("V", tt(wf(4), T.PP[:, 7:256:8], wf(3), OP.mult), r=["PP", "u64"], w=["th2"])
+        for k in range(8):
+            op("V", tt(T.NC[:, 32 * k:32 * k + 32], T.PP[:, k:256:8], wf(4), OP.is_le), r=["PP", "th2"], w=["NC%d" % k])
+        op("P", mm([(T.B7[:, 96:128], T.ID[:], T.NC[:, 32 * k:32 * k + 32]) for k in range(8)]), r=["NC%d" % k for k in range(8)], w=["fP"], b=[7])
+
+    def choice_d(t):
+        op("V", ts(wf(5), T.B7[:, 96:128], -9.0, 512.0, OP.add, OP.mult), r=["fP"], w=["fz"], b=[7])
+
+    def d_phase(t, fill):
+        H, p = HW[t % 2], t % 2
+        Y = H[:, 4608:5120]
+        path = D_PATH[t]
+        lst, ln = (T.NL0, "NL0") if t == 0 else (T.NL1, "NL1")
+        dep = ["CA%d" % t, ln] + (["cen"] if t == 0 else [])
+        late = []
+        for k in range(8):
+            if path[k // 2] == "A":
+                late.append(lambda k=k: op("V", tt(T.AG[:, 512 * k:512 * k + 512], CA[t][:, 0:4096].indirect(lst[:, 32 * k:32 * k + 32]), Y, OP.subtract),
+                                           r=dep + ["Y%d" % p], w=["AG%d" % k]))
+        last = path.rindex("C")
+
+        def place(c):
+            bk = 4 if c == last else 3
+            out = T["B%d" % bk][:, 64 * c:64 * c + 64]
+            return bk, out, [(out, T.ID[:], T.KHI[:, 64 * c:64 * c + 64]), (out, T.ID[:], T.KLO[:, 64 * c:64 * c + 64])]
+
+        def by_abs(c):
+            bk, out, head = place(c)
+            while late:
+                late.pop(0)()
+            for k in (2 * c, 2 * c + 1):
+                op("S", act(T.MX[:, 512 * k:512 * k + 512], T.AG[:, 512 * k:512 * k + 512], AF.Abs), r=["AG%d" % k], w=["MX%d" % k])
+            op("P", mm(head + sel(out, W2048, lambda r: T.MX[:, 1024 * c + r:1024 * c + 1024:16])),
+               r=["KHI", "KLO", "WS4", "MX%d" % (2 * c), "MX%d" % (2 * c + 1)], w=["KD%d" % c], b=[bk])
+        for c in range(4):
+            bk, out, head = place(c)
+            ks = (2 * c, 2 * c + 1)
+            if path[c] == "C":
+                for k in ks:
+                    op("S", act(T.AG[:, 512 * k:512 * k + 512], CA[t][:, 0:4096].indirect(lst[:, 32 * k:32 * k + 32]), AF.Copy), r=dep, w=["AG%d" % k])
+                    if late and k % 2 == 0:
+                        late.pop(0)()
+                    op("V", tt(T.MX[:, 512 * k:512 * k + 512], T.AG[:, 512 * k:512 * k + 512], T.B0[:], OP.max), r=["AG%d" % k, "B0"], w=["MX%d" % k], b=[0])
+                op("P", mm(head + [(out, T.IS[:], T.SY2[:])] + sel(out, WM2048, lambda r: T.AG[:, 1024 * c + r:1024 * c + 1024:16]), stop=False),
+                   r=["KHI", "KLO", "IS", "SY2a", "SY2b", "WS3"] + ["AG%d" % k for k in ks], w=["KD%d" % c], b=[bk])
+                if c == last:
+                    for cc in range(last + 1, 4):
+                        by_abs(cc)
+                op("P", mm(sel(out, W4096, lambda r: T.MX[:, 1024 * c + r:1024 * c + 1024:16]), start=False),
+                   r=["WS2"] + ["MX%d" % k for k in ks], w=["KD%d" % c], b=[bk])
+            for f in fill.get(c, ()):
+                f()
+        order = [c for c in range(4) if c != last] + [last]
+        op("V", cp(T.RUN[:], place(order[0])[1]), r=["KD%d" % c for c in order[:3]], w=["RUN"], b=[3])
+        for c in order[1:]:
+            op("V", tt(T.RUN[:], T.RUN[:], place(c)[1], OP.min), r=["RUN", "KD%d" % c], w=["RUN"], b=[place(c)[0]])
+        op("V", tt(wf(6), T.RUN[:, 0:32], T.RUN[:, 32:64], OP.min), r=["RUN"], w=["km"])
+
+    def window(t):
+        p = t % 2
+        return HW[p][:, 0:5120].indirect(wu(2)), ["s%d_%d" % (p, k) for k in range(8)] + ["C%d" % p, "Y%d" % p, "xu"]
+
+    def x_1(t):
+        op("V", tt(wf(7), wf(5), T.GO[:], OP.mult), r=["fz", "go"], w=["x1"])
+
+    def x_2(t):
+        op("V", tt(wf(9), wf(7), wf(1), OP.add), r=["x1", "my"], w=["x2"])
+
+    def x_3(t):
+        op("V", cp(wu(2), wf(9)), r=["x2"], w=["xu"])
+
+    def x_get(t):
+        src, dep = window(t)
+        op("S", act(T.XB[:], src, AF.Copy), r=dep, w=["X"])
+
+    def c_max(t):
+        src, dep = window(t)
+        op("V", tt(T.TM[:], src, T.CM[:], OP.max), r=dep + ["CM"], w=["TM"])
+
+    def c_new(t):
+        pn = 1 - t % 2
+        op("V", tt(HW[pn][:, 4096:4608], T.TM[:], T.B2[:], OP.min), r=["TM", "B2"], w=["C%d" % pn], b=[2])
+        if t < R - 1:
+            send("c", t + 1, "C%d" % pn, "CA%d" % (t + 1), src=HW[pn][:, 4096:4608])
+
+    def exits(t, gap):
+        H, p = HW[t % 2], t % 2
+
+        def fill(i):
+            for f in gap.get(i, ()):
+                f()
+        op("V", cp(wi_(4), wf(6)), r=["km"], w=["kz"])
+        op("V", tt(T.GO[:], wf(6), wf(2), OP.is_lt), r=["km", "thr"], w=["go"])
+        op("V", ts(wi_(5), wi_(4), 7, None, OP.bitwise_and), r=["kz"], w=["o"])
+        op("V", ts(wi_(6), wi_(4), 3, 255, OP.arith_shift_right, OP.bitwise_and), r=["kz"], w=["kc"])
+        fill(0)
+        op("V", ts(wf(8), wi_(5), 1.0, None, OP.add), r=["o"], w=["o1"])
+        op("V", ts(wu(1), wi_(6), pf(11), None, OP.add), r=["kc", "PF11"], w=["mu"])
+        fill(1)
+        op("V", tt(wf(10), wf(8), T.GO[:], OP.mult), r=["o1", "go"], w=["og"])
+        fill(2)
+        op("S", act(T.MS[:], T.MT[:, 0:4096].indirect(wu(1)), AF.Copy), r=["MT", "mu"], w=["MS"])
+        fill(3)
+        for o in range(8):
+            op("V", ts(T.HIT[:, 32 * o:32 * o + 32], wf(10), float(o + 1), None, OP.is_equal), r=["og"], w=["HIT%d" % o])
+        hit = ["HIT%d" % o for o in range(8)]
+        op("V", lambda: V.tensor_tensor_scan(T.INC[:], T.M32[:], T.HIT[:], 0.0, OP.mult, OP.add), r=["M32"] + hit, w=["INC"])
+        op("P", mm([(T.B3[:, 256:512], T.ID[:], T.HIT[:]), (T.B3[:, 256:512:32], T.TRI[:], T.INC[:, 31:256:32])]), r=hit + ["INC", "TRI"], w=["pf"], b=[3])
+        op("V", ts(wf(11), wf(10), 48.0, 463.0 + 1024.0, OP.mult, OP.add), r=["og"], w=["t1"])
+        fill(4)
+        op("V", lambda: V.tensor_tensor_scan(T.B4[:, 256:512], T.M32[:], T.B3[:, 256:512], 0.0, OP.mult, OP.add), r=["M32", "pf"], w=["SC"], b=[3, 4])
+        op("V", tt(T.PRD[:], T.B4[:, 256:512], T.HIT[:], OP.mult), r=["SC"] + hit, w=["PRD"], b=[4])
+        op("P", mm([(T.B7[:, 128:160], T.IG[:], T.GO[:])] + [(T.B7[:, 128:160], T.ID[:], T.PRD[:, 32 * o:32 * o + 32]) for o in range(8)]),
+           r=["PRD", "go", "IG"], w=["cnt"], b=[7])
+        fill(5)
+        op("V", ts(wf(12), T.B7[:, 128:160], 48.0 - 1024.0, None, OP.is_le), r=["cnt"], w=["ar"], b=[7])
+        op("V", tt(wf(13), T.B7[:, 128:160], wf(11), OP.add), r=["cnt", "t1"], w=["val"], b=[7])
+        if t < R - 1:
+            op("P", mm([(T.B6[:, 64:65], T.ONE[:], T.INC[:, 31 + 32 * o:32 + 32 * o]) for o in range(8)]), r=["INC", "ONE"], w=["AP"], b=[6])
+        fill(6)
+        op("V", tt(wf(14), wf(13), wf(12), OP.mult), r=["val", "ar"], w=["v2"])
+        op("V", tt(wf(15), wf(14), wf(0), OP.max), r=["v2", "m"], w=["v3"])
+        op("V", cp(wu(3), wf(15)), r=["v3"], w=["su"])
+        fill(7)
+        op("V", cp(T.SB[:, 0:896].indirect(wu(3)), T.MS[:]), r=["MS", "su"], w=["SB"])
+        op("P", mm(sel(T.B4[:, 0:24], WT, lambda r: T.SB[:, 512 + r:896:16])), r=["SB", "WS7"], w=["mP"], b=[4])
+        op("P", mm(sel(T.B3[:, 256:280], WY, lambda r: T.SB[:, 512 + r:896:16])), r=["SB", "WS8"], w=["pf"], b=[3])
+        fill(8)
+        op("V", cp(T.META[:, 32 * t:32 * t + 24], T.B4[:, 0:24]), r=["mP"], w=["META%d" % t], b=[4])
+        send("m", t, "META%d" % t, "LM%d" % t)
+        fill(9)
+        op("V", cp(T.WU[:, 128:152], T.B3[:, 256:280]), r=["pf"], w=["yu"], b=[3])
+        op("S", act(T.YS[:, 384 * t:384 * t + 384], H[:, 4608:5136].indirect(T.WU[:, 128:152]), AF.Copy),
+           r=["Y%d" % p, "zero%d" % p, "yu"], w=["YS%d" % t])
+        send("y", t, "YS%d" % t, "L%d" % t)
+
+    def penalty(t):
+        op("V", cp(T.PI[:, 4:5], T.B6[:, 64:65]), r=["AP"], w=["Ai"], b=[6])
+        op("V", lambda: V.memset(T.KN[:], float(3 + t)), w=["KN"])
+        op("V", ts(T.PI[:, 5:6], T.PI[:, 4:5], 63, None, OP.bitwise_and), r=["Ai"], w=["Aa"])
+        op("V", ts(pf(12), T.PI[:, 5:6], 2048.0, None, OP.mult), r=["Aa"], w=["A"])
+
+    def slots_ready(t):
+        op("S", act(T.SB[:, 512:896], T.S48[:], AF.Identity, bias=pf(19), scale=pf(4)), r=["S48", "PF19", "PF4"], w=["SB"])
+
+    def places(t):
+        op("S", act(T.VT[:], T.VB[:], AF.Identity, bias=pf(20 + t)), r=["VB", "PF20"], w=["VT"])
+
+    def u_rest(t):
+        return (T.B3[:, 256:448], 3, "pf") if t % 2 else (T.B5[:, 256:448], 5, "U1")
+
+    def take_exits(t):
+        op("V", cp(T.EW[:, 0:4608].indirect(T.LM[:, 32 * t:32 * t + 24]), T.VT[:]), r=["VT", "LM%d" % t], w=["EW"])
+        op("P", mm(sel(T.B6[:, 0:64], WE, lambda r: T.EW[:, 256 * r:256 * r + 64])), r=["EW", "WS6"], w=["U0"], b=[6])
+
+    def take_rest(t):
+        out, bk, name = u_rest(t)
+        op("P", mm(sel(out, WE, lambda r: T.EW[:, 256 * r + 64:256 * r + 256])), r=["EW", "WS6"], w=[name], b=[bk])
+
+    def pool_in(t):
+        op("V", cp(T.ZW[:, 384 * t:384 * t + 384], T.ZW[:, 2048 + 384 * t:2048 + 384 * t + 384]), r=["L%d" % t], w=["Z"])
+        if t == R - 2:
+            dma("Y", [(T.yz[:, 0:1152], T.ZW[:, 0:1152]), (T.yz[:, 1536:2048], T.ZW[:, 1536:2048])], "oz0", r=["Z"])
+
+    def list_0(t):
+        op("V", cp(T.EU[:, 0:64], T.B6[:, 0:64]), r=["U0"], w=["EU0"], b=[6])
+
+    def list_1(t):
+        out, bk, name = u_rest(t)
+        op("V", cp(T.EU[:, 64:256], out), r=[name], w=["EU1"], b=[bk])
+
+    def signs(t):
+        out, bk, name = u_rest(t)
+        lim = 0.5 - (2048 + 384 * t)
+        op("S", act(T.SG[:, 256 * t:256 * t + 64], T.B6[:, 0:64], AF.Sign, bias=lim), r=["U0"], w=["SGa"], b=[6])
+        op("S", act(T.SG[:, 256 * t + 64:256 * t + 256], out, AF.Sign, bias=lim), r=[name, "SGa"], w=["SG%d" % t], b=[bk])
+
+    def F(fn, *a):
+        return lambda: fn(*a)
+
+    def early(t):
+        exits(t, {0: [F(x_1, t)], 1: [F(x_2, t)], 2: [F(x_3, t), F(x_get, t), F(c_max, t), F(c_new, t)],
+                  4: [F(y_a, t + 1)], 5: [F(y_b, t + 1), F(y_c1, t + 1)], 7: [F(y_c2, t + 1)], 8: [neighbours_d] if t == 0 else []})
+        y_c3(t + 1)
+        c_prep(t + 1)
+        penalty(t)
+
+    def late(t):
+        rest = {4: [F(list_1, t - 1), F(signs, t - 1)] + hs_(t, 2, 3, 4, 5, 6, 7) + hv_(t, 0), 5: hv_(t, 1)}
+        if t == R - 1:
+            d_phase(t, {0: [F(places, t - 1)], 3: [F(take_exits, t - 1), F(take_rest, t - 1)]})
+            return {0: [F(list_0, t - 1), F(pool_in, t - 1)] + hs_(t, 0), 3: hs_(t, 1), **rest}
+        d_phase(t, {0: [F(places, t - 1)], 1: [F(take_exits, t - 1)], 2: [F(list_0, t - 1), F(pool_in, t - 1)],
+                    3: [F(take_rest, t - 1)] + hs_(t, 0, 1)})
+        return rest
+
+    def hs_(t, *ks):
+        return [F(h_get, t, k) for k in ks]
+
+    def hv_(t, *ks):
+        return [F(h_max, t, k) for k in ks]
+
+    consts_choice()
+    op("V", cp(T.EU[:], T.EI[:]), r=["EI"], w=["EU0", "EU1"])
+    consts_exits()
+    c_prep(0)
+    y_a(0)
+    h_get(0, 0)
+    y_b(0)
+    y_c1(0)
+    neighbours_a()
+    h_get(0, 1)
+    y_c2(0)
+    h_get(0, 2)
+    h_max(0, 0)
+    h_get(0, 3)
+    y_c3(0)
+    h_max(0, 1)
+    neighbours_b()
+    h_max(0, 2)
+    h_get(0, 4)
+    h_max(0, 3)
+    h_get(0, 5)
+    neighbours_c()
+    h_max(0, 4)
+    flux(0)
+    h_get(0, 6)
+    y_d(0)
+    h_max(0, 5)
+    h_get(0, 7)
+    h_max(0, 6)
+    h_max(0, 7)
+    d_phase(0, {0: [F(choice_a, 0), F(choice_b, 0)], 1: [F(choice_c, 0)], 2: [F(choice_d, 0)], 3: [F(c_bounds, 0), F(slots_ready, 0)]})
+    early(0)
+    slots_ready(1)
+    c_bounds(1)
+    entries_0()
+    y_d(1)
+    exits(1, {**late(1), 7: hv_(1, 2, 3) + [F(flux, 1), F(h_sum, 1, 2)], 8: [F(h_sum, 1, 3)] + hv_(1, 4, 5)})
+    h_max(1, 6)
+    h_max(1, 7)
+    choice_a(1)
+    penalty(1)
+    places(1)
+    choice_b(1)
+    choice_c(1)
+    choice_d(1)
+    x_1(1)
+    x_2(1)
+    x_3(1)
+    x_get(1)
+    c_max(1)
+    y_a(2)
+    c_new(1)
+    c_prep(2)
+    y_b(2)
+    y_c1(2)
+    y_c2(2)
+    take_exits(1)
+    take_rest(1)
+    y_c3(2)
+    list_0(1)
+    pool_in(1)
+    h_get(2, 0)
+    h_get(2, 1)
+    list_1(1)
+    signs(1)
+    for k in H_BY_VECTOR[2]:
+        h_get(2, k)
+    for k in range(8):
+        if k > 1 and k not in H_BY_VECTOR[2]:
+            h_get(2, k)
+        h_max(2, k)
+        if k == 2:
+            y_d(2)
+    flux(2)
+    d_phase(2, {0: [F(choice_a, 2), F(choice_b, 2)], 1: [F(choice_c, 2)], 2: [F(choice_d, 2)], 3: [F(c_bounds, 2), F(slots_ready, 2)]})
+    early(2)
+    y_d(3)
+    slots_ready(3)
+    c_bounds(3)
+    exits(3, {**late(3), 7: [F(flux, 3), F(h_sum, 3, 1)], 8: hv_(3, 2)})
+    h_sum(3, 2)
+    h_max(3, 3)
+    h_sum(3, 3)
+    for k in range(4, 8):
+        h_max(3, k)
+    places(3)
+    choice_a(3)
+    op("V", lambda: V.memset(T.KN[:], float(3 + R - 1)), w=["KN"])
+    t = R - 1
+    choice_b(3)
+    choice_c(3)
+    choice_d(3)
+    x_1(3)
+    x_2(3)
+    x_3(3)
+    x_get(3)
+    take_exits(t)
+    take_rest(t)
+    op("S", act(T.XO[:], T.XB[:, 0:512].indirect(T.LU[:, 96:128]), AF.Copy), r=["X", "LU3"], w=["XO"])
+    dma("Y", [(T.yx[:], T.XO[:])], "ox", r=["XO"])
+    c_max(3)
+    c_new(3)
+    dma("Y", [(T.yz[:, 1152:1536], T.ZW[:, 3200:3584])], "oz1", r=["L3"])
+    op("V", ts(T.EG[:, 0:64], T.B6[:, 0:64], 2048.0, 2048.0, OP.is_ge, OP.mult), r=["U0"], w=["EGa"], b=[6])
+    op("V", tt(T.EF[:, 0:64], T.B6[:, 0:64], T.EG[:, 0:64], OP.subtract), r=["U0", "EGa"], w=["EFa"], b=[6])
+    dma("Y", [(T.ye[:, 512 * k:512 * k + 512], T.EF[:, 32 * k:32 * k + 32]) for k in range(2)], "oe", r=["EFa"], total=128)
+    signs(t)
+    flux(R)
+    op("V", ts(T.EG[:, 64:256], T.B3[:, 256:448], 2048.0, 2048.0, OP.is_ge, OP.mult), r=["pf"], w=["EGb"], b=[3])
+    op("V", tt(T.EF[:, 64:256], T.B3[:, 256:448], T.EG[:, 64:256], OP.subtract), r=["pf", "EGb"], w=["EFb"], b=[3])
+    dma("Y", [(T.ye[:, 512 * k:512 * k + 512], T.EF[:, 32 * k:32 * k + 32]) for k in range(2, 8)], "oe", r=["EFb"])
+    op("V", cp(T.CO[:], T.HW0[:, 4096:4608].indirect(T.LU[:, 96:128])), r=["C0", "LU3"], w=["CO"])
+    op("S", act(T.NF[:], T.B6[:, 256:512], AF.Copy), r=["n"], w=["NF"], b=[6])
+    dma("S", [(T.yn[:, 512 * k:512 * k + 512], T.NF[:, 32 * k:32 * k + 32]) for k in range(8)], "on", r=["NF"])
+    dma("Y", [(T.yc[:], T.CO[:])], "oc", r=["CO"])
+    for sem, val in count.items():
+        if known["G"].get(sem, 0) < val:
+            g.wait_ge(T.sem[sem], val)

@@ -3,44 +3,54 @@ from concourse.mybir import AluOpType as OP, ActivationFunctionType as AF
 
 R = 4
 BF, F32, I32, U16 = "bfloat16", "float32", "int32", "uint16"
-D_PATH = ["CCCA", "CCCA", "CCCA", "CCCA"]
-H_BY_VECTOR = [(), (), (7,), ()]
+CFG = {
+    "D": ["CCRC", "CCAC", "CCRC", "CCAC"],
+    "H": ["SSSSSSSS", "SSSSSSEE", "SSSVSSSV", "SSSSSSEE"], "CUTS": [0, 1, 2, 4],
+    "CASES": [(1.0, 1.0, 1.0), (1.3, 1.0, 1.2), (1.0, 1.5, 1.15), (0.9, 0.8, 0.88)], "SEED": 1,
+    "FOLD": [False, True, False, True],
+    "JV": [False, False, False, False],
+    "XM": ["direct"] * 4, "XY": ["exits"] * 4,
+    "LC": 8.7, "LC0": 14.3, "exits": 5.5, "direct": 4.2, "HOP": 0.08, "ROUNDS": 1000, "CP": "S", "CM": "S",
+}
 
 SCRATCH = {
     "CA0": ("sbuf", [128, 4096], BF), "CA1": ("sbuf", [128, 4096], BF), "CA2": ("sbuf", [128, 4096], BF), "CA3": ("sbuf", [128, 4096], BF),
     "HW0": ("sbuf", [128, 5136], BF), "HW1": ("sbuf", [128, 5136], BF),
     "ZW": ("sbuf", [128, 3584], BF), "EW": ("sbuf", [128, 4608], BF), "MT": ("sbuf", [128, 4096], BF),
     "AG": ("sbuf", [128, 4096], BF), "MX": ("sbuf", [128, 4096], BF), "MH": ("sbuf", [128, 4096], BF),
-    "JT": ("sbuf", [128, 512], BF), "WK": ("sbuf", [128, 512], BF), "XB": ("sbuf", [128, 512], BF), "JG": ("sbuf", [128, 512], BF),
+    "JT": ("sbuf", [128, 512], BF), "XB": ("sbuf", [128, 512], BF), "JG": ("sbuf", [128, 512], BF),
     "OA": ("sbuf", [128, 512], BF), "CM": ("sbuf", [128, 512], BF), "TM": ("sbuf", [128, 512], BF), "MS": ("sbuf", [128, 512], BF),
-    "XO": ("sbuf", [128, 512], BF), "CO": ("sbuf", [128, 512], BF),
-    "SB": ("sbuf", [128, 896], BF), "YS": ("sbuf", [128, 1536], BF), "VT": ("sbuf", [128, 384], BF), "VB": ("sbuf", [128, 384], BF),
+    "ONE": ("sbuf", [128, 512], BF),
+    "SB": ("sbuf", [128, 896], BF), "YS": ("sbuf", [128, 1536], BF), "VT": ("sbuf", [128, 1536], BF), "VB": ("sbuf", [128, 384], BF),
     "P1": ("sbuf", [128, 384], BF), "P2": ("sbuf", [128, 384], BF), "S48": ("sbuf", [128, 384], BF),
     "META": ("sbuf", [128, 128], U16), "LM": ("sbuf", [128, 128], U16),
-    "NBI": ("sbuf", [128, 256], I32), "NX": ("sbuf", [128, 512], F32), "NT": ("sbuf", [128, 512], F32),
-    "NI": ("sbuf", [128, 256], I32), "N1": ("sbuf", [128, 256], I32), "N2": ("sbuf", [128, 256], I32), "N3": ("sbuf", [128, 256], I32),
-    "N4": ("sbuf", [128, 256], F32), "N5": ("sbuf", [128, 256], F32),
-    "NL0": ("sbuf", [128, 256], U16), "NL1": ("sbuf", [128, 256], U16), "EU": ("sbuf", [128, 256], U16),
+    "NBI": ("sbuf", [128, 256], I32), "NX": ("sbuf", [128, 512], BF), "NT": ("sbuf", [128, 512], BF),
+    "N1": ("sbuf", [128, 256], I32), "N2": ("sbuf", [128, 256], I32), "N3": ("sbuf", [128, 256], I32),
+    "NQ": ("sbuf", [128, 256], BF), "NP": ("sbuf", [128, 256], BF),
+    "NL": ("sbuf", [128, 256], U16), "EU": ("sbuf", [128, 256], U16),
     "EI": ("sbuf", [128, 256], I32), "E1": ("sbuf", [128, 256], I32), "E2": ("sbuf", [128, 256], I32),
     "ELO": ("sbuf", [128, 256], BF), "EHI": ("sbuf", [128, 256], BF),
     "KHI": ("sbuf", [128, 256], BF), "KLO": ("sbuf", [128, 256], BF), "TLO": ("sbuf", [128, 256], BF), "THI": ("sbuf", [128, 256], BF),
     "CT": ("sbuf", [128, 256], BF), "C8": ("sbuf", [128, 256], BF), "KX": ("sbuf", [128, 256], BF), "RT": ("sbuf", [128, 256], BF),
-    "M32": ("sbuf", [128, 256], BF), "M8": ("sbuf", [128, 256], F32), "KN": ("sbuf", [128, 256], BF),
+    "M32": ("sbuf", [128, 256], BF), "M8": ("sbuf", [128, 256], F32),
     "SG": ("sbuf", [128, 1024], BF), "RG": ("sbuf", [128, 256], F32), "G2": ("sbuf", [128, 256], F32), "PP": ("sbuf", [128, 256], F32),
     "NC": ("sbuf", [128, 256], BF), "HIT": ("sbuf", [128, 256], BF), "INC": ("sbuf", [128, 256], BF), "PRD": ("sbuf", [128, 256], BF),
     "EF": ("sbuf", [128, 256], F32), "EG": ("sbuf", [128, 256], F32), "NF": ("sbuf", [128, 256], BF),
     "COL": ("sbuf", [128, 144], F32), "PI": ("sbuf", [128, 8], I32), "PF": ("sbuf", [128, 24], F32),
-    "WS": ("sbuf", [128, 9 * 144], BF), "ID": ("sbuf", [128, 128], BF), "NID": ("sbuf", [128, 128], BF), "IH": ("sbuf", [128, 128], BF),
-    "IG": ("sbuf", [128, 128], BF), "I32": ("sbuf", [128, 128], F32), "IS": ("sbuf", [128, 128], F32),
-    "ZID": ("sbuf", [128, 128], BF), "TRI": ("sbuf", [128, 128], BF), "TA": ("sbuf", [128, 128], BF), "TB": ("sbuf", [128, 128], BF), "ONE": ("sbuf", [128, 128], BF),
-    "LI": ("sbuf", [128, 96], I32), "LU": ("sbuf", [128, 128], U16),
-    "WF": ("sbuf", [128, 640], F32), "WI": ("sbuf", [128, 256], I32), "WU": ("sbuf", [128, 160], U16), "GO": ("sbuf", [128, 32], BF),
-    "SY2": ("sbuf", [128, 64], F32), "SC2": ("sbuf", [128, 64], F32), "RUN": ("sbuf", [128, 64], F32),
+    "WS": ("sbuf", [128, 10 * 144], BF), "ID": ("sbuf", [128, 128], BF), "NID": ("sbuf", [128, 128], BF), "IH": ("sbuf", [128, 128], BF),
+    "I512": ("sbuf", [128, 128], BF), "I16": ("sbuf", [128, 128], BF), "I32": ("sbuf", [128, 128], F32), "IS": ("sbuf", [128, 128], F32),
+    "ZID": ("sbuf", [128, 128], BF), "GRP": ("sbuf", [128, 128], BF), "NUP": ("sbuf", [128, 128], BF),
+    "TA": ("sbuf", [128, 128], BF), "TB": ("sbuf", [128, 128], BF), "TC": ("sbuf", [128, 128], BF),
+    "LI": ("sbuf", [128, 32], I32), "LJ": ("sbuf", [128, 32], I32), "LU": ("sbuf", [128, 96], U16),
+    "EX": ("sbuf", [128, 512], F32), "ET": ("sbuf", [128, 512], F32),
+    "WF": ("sbuf", [128, 640], F32), "WI": ("sbuf", [128, 320], I32), "WU": ("sbuf", [128, 160], U16), "GO": ("sbuf", [128, 32], BF),
+    "SY2": ("sbuf", [128, 64], F32), "SC2": ("sbuf", [128, 64], F32), "RUN": ("sbuf", [128, 64], F32), "THR": ("sbuf", [128, 64], F32),
     "B0": ("psum", [128, 512], F32), "B1": ("psum", [128, 512], F32), "B2": ("psum", [128, 512], F32), "B3": ("psum", [128, 512], F32),
     "B4": ("psum", [128, 512], F32), "B5": ("psum", [128, 512], F32), "B6": ("psum", [128, 512], F32), "B7": ("psum", [128, 512], F32),
 }
-SEMAPHORES = (["qV", "qS", "qP", "qG", "lcen", "lent", "lpl", "lwk", "ljt", "lnb", "dew", "dmt", "oz0", "oz1", "oc", "ox", "oe", "on"]
+SEMAPHORES = (["qV", "qS", "qP", "qG", "lcen", "lent", "lown", "lpl", "lwk", "ljt", "lnb", "dew", "dmt", "oz0", "oz1", "oc", "ox", "oe", "on"]
               + ["%s%s%d" % (a, k, t) for a in "lah" for k in "cmy" for t in range(R)])
+ORDER = {}
 
 
 def bits(engs):
@@ -128,9 +138,7 @@ def pieces(T, kind, t):
 def exchange(kind, t):
     if kind == "c":
         return "first" if t == 0 else "later", False
-    if t % 2:
-        return "direct" if kind == ("m" if t == R - 1 else "y") else "exits", True
-    return "exits", True
+    return CFG["XM" if kind == "m" else "XY"][t], True
 
 
 def helper_program(g, core, T, topo, pl):
@@ -153,6 +161,115 @@ def helper_program(g, core, T, topo, pl):
         g.wait_ge(T.sem[sem], n)
 
 
+def place_calls(calls, before, rank, free):
+    hop = CFG["HOP"]
+    start, lines = [None] * len(calls), {}
+
+    def first_after(line, s):
+        lo, hi = 0, len(line)
+        while lo < hi:
+            mid = (lo + hi) // 2
+            if line[mid][1] <= s:
+                lo = mid + 1
+            else:
+                hi = mid
+        return lo
+
+    def place(i):
+        e, c, s = calls[i]["e"], calls[i]["c"], free[i]
+        for p, delay in before[i].items():
+            if start[p] is None:
+                place(p)
+            s = max(s, start[p] + calls[p]["c"] + delay)
+        if e is not None:
+            mine = [lines.setdefault(x, []) for x in (e,) + calls[i]["b"]]
+            moved = True
+            while moved:
+                moved = False
+                for n, line in enumerate(mine):
+                    j = first_after(line, s - hop)
+                    while j < len(line) and line[j][0] - hop < s + c:
+                        a, z, ee = line[j]
+                        gap = 0.0 if n == 0 or ee == e else hop
+                        if a - gap < s + c - 1e-9 and z + gap > s + 1e-9:
+                            s, moved = z + gap, True
+                        j += 1
+            for line in mine:
+                line.insert(first_after(line, s), (s, s + c, e))
+        start[i] = s
+    for i in rank:
+        if start[i] is None:
+            place(i)
+    return start
+
+
+def replay(calls, before, order, work, wire):
+    hop = CFG["HOP"]
+    end, queue, bank, last = [0.0] * len(calls), {}, {}, 0.0
+    for i in order:
+        k = calls[i]
+        s = queue.get(k["e"], 0.0)
+        for p, delay in before[i].items():
+            s = max(s, end[p] + (delay * wire if calls[p]["e"] is None else delay))
+        for x in k["b"]:
+            for e, z in bank.setdefault(x, {}).items():
+                if e != k["e"]:
+                    s = max(s, z + hop)
+        end[i] = s + k["c"] * (work if k["e"] in ("V", "S", "P") else 1.0)
+        if k["e"] is not None:
+            queue[k["e"]] = end[i]
+        for x in k["b"]:
+            bank[x][k["e"]] = end[i]
+        last = max(last, end[i] + k["lat"])
+    return last
+
+
+def order_calls(calls):
+    n = len(calls)
+    before, after = [{} for _ in calls], [{} for _ in calls]
+    wr, rd = {}, {}
+    for i, k in enumerate(calls):
+        met = [(wr[x], x) for x in k["r"] + k["w"] if x in wr] + [(p, x) for x in k["w"] for p in rd.get(x, ())]
+        for p, x in met:
+            if p != i:
+                delay = 0.0 if x[0] == "~" or k["e"] == calls[p]["e"] == "P" else calls[p]["lat"] + CFG["HOP"]
+                before[i][p] = after[p][i] = max(delay, before[i].get(p, 0.0))
+        for x in k["r"]:
+            rd.setdefault(x, []).append(i)
+        for x in k["w"]:
+            wr[x] = i
+            rd[x] = []
+    way = [0.0] * n
+    for i in range(n - 1, -1, -1):
+        way[i] = calls[i]["c"] + max([way[j] + d for j, d in after[i].items()] + [calls[i]["lat"]])
+    tails = [0.0 if after[i] else k["lat"] for i, k in enumerate(calls)]
+
+    def forward(urgency):
+        start = place_calls(calls, before, sorted(range(n), key=lambda i: (-urgency[i], i)), [0.0] * n)
+        order = sorted(range(n), key=lambda i: (start[i], i))
+        return sum(replay(calls, before, order, a, b) / c for a, b, c in CFG["CASES"]) / len(CFG["CASES"]), urgency, start, order
+
+    def backward(start):
+        back = place_calls(calls, after, sorted(range(n), key=lambda i: (-start[i] - calls[i]["c"], -i)), tails)
+        return [back[i] + calls[i]["c"] for i in range(n)]
+    state = [CFG["SEED"]]
+
+    def draw():
+        state[0] = (state[0] * 6364136223846793005 + 1442695040888963407) % (1 << 64)
+        return (state[0] >> 11) / float(1 << 53)
+    best = now = forward(way)
+    for turn in range(CFG["ROUNDS"]):
+        urgency = backward(now[2]) if turn % 3 == 2 else now[1]
+        a, width, size = draw() * max(now[2]), 3.0 * 10.0 ** draw(), 0.3 * 20.0 ** draw()
+        new = forward([urgency[i] + size * (2 * draw() - 1) if a <= now[2][i] < a + width and draw() < 0.3 else urgency[i] for i in range(n)])
+        if new[0] <= now[0] + 0.15 * draw():
+            now = new
+        if new[0] < best[0]:
+            best = new
+    ORDER["plan"] = (best[0], [(k["e"], best[2][i], k["c"], (k["w"] + k["r"])[0]) for i, k in enumerate(calls)])
+    return best[3]
+
+
 def rank_program(g, core, T, topo):
     pl = plans(T, topo)
     q = T.rank_of(core)
@@ -163,6 +280,7 @@ def rank_program(g, core, T, topo):
     V, S, PE = g.vector, g.scalar, g.tensor
     known = {e: {} for e in Q}
     count, wr, rd, bank = {}, {}, {}, {}
+    calls = []
 
     def need(e, tok):
         sem, val, clock = tok
@@ -174,7 +292,13 @@ def rank_program(g, core, T, topo):
             if known[e].get(s, 0) < v:
                 known[e][s] = v
 
-    def op(e, fn, r=(), w=(), b=(), sem=None, inc=1, total=None):
+    def issue(k):
+        e, r, w, b, sem = k["e"], k["r"], k["w"], k["b"], k["sem"]
+        if e is None:
+            count[sem] = k["total"]
+            for x in w:
+                wr[x] = (sem, k["total"], {})
+            return
         toks = [wr[x] for x in r if x in wr] + [wr[x] for x in w if x in wr]
         for x in w:
             toks += rd.get(x, [])
@@ -184,55 +308,75 @@ def rank_program(g, core, T, topo):
         for tk in toks:
             if not (e == "P" and tk[0] == "qP"):
                 need(e, tk)
-        res = fn()
+        res = k["fn"]()
         if sem is None:
             sem = "q" + e
             res.then_inc(T.sem[sem], 1)
-        count[sem] = count.get(sem, 0) + inc
-        tok = (sem, total or count[sem], dict(known[e]))
+        count[sem] = max(count.get(sem, 0) + k["inc"], k["total"] or 0) if k["total"] is None else k["total"]
+        tok = (sem, count[sem], dict(known[e]))
         for x in r:
             rd.setdefault(x, []).append(tok)
         for x in w:
-            wr[x] = tok
-            rd[x] = []
+            if x[0] != "~":
+                wr[x] = tok
+                rd[x] = []
         for x in b:
             bank.setdefault(x, {})[e] = tok
-        return tok
 
-    def dma(e, pairs, sem, r=(), w=(), total=None):
+    def op(e, fc, r=(), w=(), b=(), sem=None, inc=1, total=None, lat=0.0):
+        calls.append(dict(e=e, fn=fc[0], c=fc[1], r=list(r), w=list(w), b=tuple(b), sem=sem, inc=inc, total=total, lat=lat))
+
+    def dma(e, pairs, sem, r=(), w=(), total=None, lat=2.0):
         def fn():
             for o, i in pairs:
                 Q[e].dma_start(o, i).then_inc(T.sem[sem], 16)
-        return op(e, fn, r, w, sem=sem, inc=16 * len(pairs), total=total)
+        op(e, (fn, 0.1 * len(pairs)), r, w, sem=sem, inc=16 * len(pairs), total=total, lat=lat)
 
-    def ts(out, in0, s1, s2, o0, o1=None):
+    CYC = 0.00087
+
+    def us(n):
+        return max(n, 64) * CYC
+
+    def got(n):
+        return 0.06 + 1.56 * n * CYC
+
+    def put(n):
+        return 0.05 + 3.8 * n * CYC
+
+    def ts(out, in0, s1, s2, o0, o1=None, c=us(0)):
         if o1 is None:
-            return lambda: V.tensor_scalar(out, in0, s1, None, o0)
-        return lambda: V.tensor_scalar(out, in0, s1, s2, o0, o1)
+            return lambda: V.tensor_scalar(out, in0, s1, None, o0), c
+        return lambda: V.tensor_scalar(out, in0, s1, s2, o0, o1), c
 
-    def tt(out, a, b, o):
-        return lambda: V.tensor_tensor(out, a, b, o)
+    def tt(out, a, b, o, c=us(0)):
+        return lambda: V.tensor_tensor(out, a, b, o), c
 
-    def cp(out, a):
-        return lambda: V.tensor_copy(out, a)
+    def cp(out, a, c=us(0)):
+        return lambda: V.tensor_copy(out, a), c
 
-    def act(out, a, f, **kw):
-        return lambda: S.activation(out, a, f, **kw)
+    def fill(out, x, c=us(0)):
+        return lambda: V.memset(out, x), c
 
-    def mm(items, start=True, stop=True):
+    def scan(out, a, b, c):
+        return lambda: V.tensor_tensor_scan(out, a, b, 0.0, OP.mult, OP.add), c
+
+    def act(out, a, f, c=us(0), **kw):
+        return lambda: S.activation(out, a, f, **kw), c
+
+    def mm(items, n=64, more=0, start=True, stop=True):
         def fn():
-            for n, (o, l, x) in enumerate(items):
-                res = PE.matmul(o, l, x, start and n == 0, stop and n == len(items) - 1)
+            for j, (o, l, x) in enumerate(items):
+                res = PE.matmul(o, l, x, start and j == 0, stop and j == len(items) - 1)
             return res
-        return fn
+        return fn, (len(items) * max(n, 64) + more) * CYC / 2
 
-    W1, WM2, W4096, WM2048, W2048, WJ, WE, WT, WY = range(9)
+    W1, WM2, W8192, WM4096, W4096, WJ, WE, WT, WY, WM1 = range(10)
 
     def sel(out, wi, src):
         return [(out, T.WS[:, 144 * wi + 15 - r:144 * wi + 143 - r], src(r)) for r in range(16)]
 
-    def iota(out, pat, base, name):
-        op("G", lambda: g.iota(out, pat, base, 0, allow_small_or_imprecise_dtypes=True), w=[name])
+    def iota(out, pat, base, name, n, ch=0):
+        op("G", (lambda: g.iota(out, pat, base, ch, allow_small_or_imprecise_dtypes=True), 0.13 + 2 * n * CYC), w=[name])
 
     def wf(j):
         return T.WF[:, 32 * j:32 * j + 32]
@@ -249,7 +393,7 @@ def rank_program(g, core, T, topo):
     HW = [T.HW0, T.HW1]
     CA = [T["CA%d" % t] for t in range(R)]
 
-    def send(kind, t, name, landed, src=None, own=True):
+    def send(kind, t, name, landed, src=None):
         plan, keep = exchange(kind, t)
         near, hs = pl[plan][q]
         m1, m2 = masks(T, topo, pl[plan], q, keep)
@@ -259,542 +403,361 @@ def rank_program(g, core, T, topo):
                                 src=src if part is None else part(o), dst=land(q)) for o, m in zip(near, m1)]
         tr += [RemoteDMATransfer(dst_ids=[dst(topo, h)], dma_engine_mask=bits(m), remote_sem=T.sem[h_], src=src if part is None else whole,
                                  dst=land(q) if part is None else whole) for h, m in zip(hs, m2)]
-        op("G", lambda: g.remote_dma_fused(tr, local_sem=T.sem[l]), r=[name], sem=l, inc=sum(len(m) for m in m1 + m2))
+        chain = ["~c"] if kind == "c" else ["~x"]
+        first = kind == "c" and t == 0
+        op("G", (lambda: g.remote_dma_fused(tr, local_sem=T.sem[l]), 3.5 if first else 0.45), r=[name], w=chain + ["~s" + a] + (["~x"] if first else []),
+           sem=l, inc=sum(len(m) for m in m1 + m2))
         total = counts(T, topo, pl[plan], keep)[0][q]
-        if own:
+        got_ = ["~s" + a]
+        if part is not None:
             total += 16
-            dma("Y", [(land(q), src if part is None else part(q))], a, r=[name], total=total)
-        count[a] = total
-        wr[landed] = (a, total, {})
+            dma("Y", [(land(q), part(q))], a, r=[name], w=["~o" + a], total=total)
+            got_.append("~o" + a)
+        op(None, (None, 0.0), r=got_, w=[landed], sem=a, total=total, lat=(CFG["LC0"] - 3.5 if first else CFG["LC"] if kind == "c" else CFG[plan]) - 0.45)
 
     own0 = CA[0][:, 512 * q:512 * q + 512]
-    dma("Y", [(own0, T.cen[:])], "lcen", w=["cen"])
-    dma("S", [(T.ZW[:, 0:2048], T.pl[:])], "lpl", w=["Z"])
-    dma("Y", [(T.EI[:, 32 * k:32 * k + 32], T.ent[:, 512 * k:512 * k + 512]) for k in range(8)], "lent", w=["EI"])
-    dma("S", [(T.WK[:], T.wk[:])], "lwk", w=["WK"])
-    dma("S", [(T.JT[:], T.jmp[:])], "ljt", w=["JT"])
-    dma("S", [(T.NBI[:], T.nb[:])], "lnb", w=["NBI"])
-    op("G", lambda: g.iota(T.PI[:, 0:1], [[0, 1]], 0, 1), w=["PI0"])
-    iota(T.COL[:], [[1, 144]], 0, "COL")
-    op("G", lambda: g.iota(T.LI[:, 0:32], [[32, 8], [1, 2], [0, 2]], 0, 0), w=["LI0"])
-    op("G", lambda: g.iota(T.LI[:, 32:64], [[1, 16], [256, 2]], 0, 0), w=["LI1"])
-    iota(T.CT[:], [[0, 8], [1, 32]], 0, "CT")
-    iota(T.C8[:], [[0, 8], [8, 32]], 0, "C8")
-    send("c", 0, "cen", "CA0", src=own0, own=False)
-    iota(T.KX[:], [[64, 4], [-32, 2], [0, 32]], 32, "KX")
-    iota(T.KHI[:], [[256, 8], [0, 32]], 0, "KHI")
-    iota(T.MT[:], [[0, 4096]], 0, "MT")
-    iota(T.S48[:], [[0, 8], [1, 48]], 0, "S48")
-    iota(T.P1[:], [[0, 3], [1, 128]], 0, "P1")
-    iota(T.P2[:], [[1, 3], [0, 128]], 0, "P2")
-    iota(T.EW[:, 0:2048], [[0, 2048]], 0, "EW")
+    dma("Y", [(own0, T.cen[:])], "lcen", w=["cen", "~ld"])
+    dma("Y", [(T.EI[:], T.ent[:])], "lent", w=["EI", "~ld"], lat=2.3)
+    dma("Y", [(T.XB[:], T.wk[:])], "lwk", w=["X", "~ld"], lat=2.6)
+    dma("Y", [(T.JT[:], T.jmp[:])], "ljt", w=["JT", "~ld"], lat=2.9)
+    dma("Y", [(T.HW0[:, 4096:4608], T.cen[:])], "lown", w=["C0", "~ld"], lat=3.2)
+    dma("Y", [(T.ZW[:, 0:2048], T.pl[:])], "lpl", w=["Z", "~ld"], lat=4.4)
+    dma("Y", [(T.NBI[:], T.nb[:])], "lnb", w=["NBI", "~ld"], lat=4.7)
+    send("c", 0, "cen", "CA0", src=own0)
+    op("G", (lambda: g.iota(T.PI[:, 0:1], [[0, 1]], 0, 1), 0.13), w=["PI0"])
+    iota(T.COL[:], [[1, 144]], 0, "COL", 144)
+    op("G", (lambda: g.iota(T.LI[:], [[1, 16], [0, 2]], 0, 0), 0.19), w=["LI"])
+    op("G", (lambda: g.iota(T.LJ[:], [[16, 16], [0, 2]], 0, 0), 0.19), w=["LJ"])
+    iota(T.CT[:], [[0, 8], [1, 32]], 0, "CT", 256)
+    iota(T.C8[:], [[0, 8], [8, 32]], 0, "C8", 256)
+    iota(T.KX[:], [[4, 4], [-2, 2], [0, 32]], 2, "KX", 256)
+    iota(T.KHI[:], [[256, 8], [0, 32]], 2048, "KHI", 256)
+    for j in range(4):
+        iota(T.MT[:, 1024 * j:1024 * j + 1024], [[0, 1024]], 0, "MT%d" % j, 1024)
+    iota(T.S48[:], [[0, 8], [1, 48]], 0, "S48", 384)
+    iota(T.P1[:], [[0, 3], [1, 128]], 0, "P1", 384)
+    iota(T.P2[:], [[1, 3], [0, 128]], 0, "P2", 384)
+    for j in range(4):
+        op("V", fill(T.EW[:, 1024 * j:1024 * j + 1024], 0.0, us(512)), w=["EW%d" % j])
 
     op("V", ts(T.PI[:, 1:2], T.PI[:, 0:1], 15, None, OP.bitwise_and), r=["PI0"], w=["PI1"])
     op("V", ts(T.PI[:, 2:3], T.PI[:, 0:1], 112, None, OP.bitwise_and), r=["PI0"], w=["PI2"])
     op("V", ts(T.PI[:, 3:4], T.PI[:, 0:1], 31, None, OP.bitwise_and), r=["PI0"], w=["PI3"])
     op("V", cp(T.PF[:, 0:4], T.PI[:, 0:4]), r=["PI0", "PI1", "PI2", "PI3"], w=["PF0"])
-    op("V", lambda: V.memset(pf(12), 0.0), w=["A"])
-    op("V", ts(pf(2), pf(2), 15.0, None, OP.add), r=["PF0"], w=["PF2"])
-    op("V", ts(pf(8), pf(1), 32.0, None, OP.mult), r=["PF0"], w=["PF8"])
+    op("V", fill(pf(12), 0.0), w=["A"])
+    op("V", ts(pf(10), pf(2), 15.0, None, OP.add), r=["PF0"], w=["PF10"])
     op("V", ts(pf(9), pf(1), 2.0, 1.0, OP.mult, OP.add), r=["PF0"], w=["PF9"])
-    op("V", ts(pf(10), pf(1), 2.0, None, OP.mult), r=["PF0"], w=["PF10"])
     op("V", ts(T.PF[:, 4:8], T.COL[:, 0:4], pf(1), None, OP.is_equal), r=["PF0", "COL"], w=["PF4"])
-    op("V", ts(T.LU[:, 0:32], T.COL[:, 0:32], pf(8), None, OP.add), r=["PF8", "COL"], w=["LU0"])
-    op("V", ts(T.ID[:], T.COL[:, 0:128], pf(0), None, OP.is_equal), r=["PF0", "COL"], w=["ID"])
 
     def weights(j, s, deps=()):
-        op("V", ts(T.WS[:, 144 * j:144 * j + 144], T.COL[:], pf(2), s, OP.is_equal, OP.mult), r=["PF2", "COL"] + list(deps), w=["WS%d" % j])
+        op("V", ts(T.WS[:, 144 * j:144 * j + 144], T.COL[:], pf(10), s, OP.is_equal, OP.mult, c=us(144)), r=["PF10", "COL"] + list(deps), w=["WS%d" % j])
 
-    def scaled_identity(out, s, name):
-        op("V", ts(out, T.COL[:, 0:128], pf(0), s, OP.is_equal, OP.mult), r=["PF0", "COL"], w=[name])
+    def scaled_identity(name, s):
+        op("V", ts(T[name][:], T.COL[:, 0:128], pf(0), s, OP.is_equal, OP.mult, c=us(128)), r=["PF0", "COL"], w=[name])
+    for name, s in (("ID", 1.0), ("NID", -1.0), ("I32", 1.0), ("IS", -4096.0), ("IH", 0.5), ("I512", 512.0), ("I16", 16.0)):
+        scaled_identity(name, s)
     weights(WJ, pf(9), ["PF9"])
-    weights(W1, 1.0)
-    scaled_identity(T.NID[:], -1.0, "NID")
-    scaled_identity(T.I32[:], 1.0, "I32")
-    weights(WM2, -2.0)
-    weights(W2048, 2048.0)
-    op("V", ts(T.LU[:, 32:64], T.LI[:, 0:32], pf(10), None, OP.add), r=["PF10", "LI0"], w=["LU1"])
-    op("V", ts(T.LU[:, 64:80], T.COL[:, 0:16], 32.0, pf(3), OP.mult, OP.add), r=["PF0", "COL"], w=["LU2"])
-    scaled_identity(T.IS[:], -2048.0, "IS")
-    weights(W4096, 4096.0)
-    weights(WM2048, -2048.0)
-    op("S", act(T.HW0[:, 4096:4608], own0.indirect(T.LU[:, 0:32]), AF.Copy), r=["cen", "LU0"], w=["C0"])
-    op("S", act(T.XB[:], T.WK[:, 0:512].indirect(T.LU[:, 0:32]), AF.Copy), r=["WK", "LU0"], w=["X"])
+    for j, s in ((W1, 1.0), (WM2, -2.0), (W8192, 8192.0), (WM4096, -4096.0), (W4096, 4096.0), (WM1, -1.0)):
+        weights(j, s)
+    op("V", ts(T.LU[:, 32:48], T.COL[:, 0:16], 32.0, pf(3), OP.mult, OP.add), r=["PF0", "COL"], w=["LU2"])
+    op("V", fill(T.ZID[:], 0.0), w=["ZID"])
+    op("V", fill(T.ONE[:], 1.0, us(256)), w=["ONE"])
+    op("V", fill(T.M8[:], 1.0, us(256)), w=["M8"])
+    op("V", fill(T.M32[:], 1.0, us(128)), w=["M32"])
+    op("V", fill(T.M8[:, 0:256:8], 0.0), w=["M8"])
+    op("V", fill(T.M32[:, 0:256:32], 0.0), w=["M32"])
+    op("V", ts(pf(11), pf(1), 256.0, None, OP.mult), r=["PF0"], w=["PF11"])
+    op("V", ts(pf(15), pf(5), 256.0, pf(4), OP.mult, OP.add), r=["PF4"], w=["PF15"])
+    op("V", ts(pf(16), pf(7), 16.0, pf(6), OP.mult, OP.add), r=["PF4"], w=["PF16"])
+    op("V", ts(pf(17), pf(4), float(64 * (q & 3)), None, OP.mult), r=["PF4"], w=["PF17"])
+    op("V", ts(wf(0), T.COL[:, 0:32], 16.0, pf(1), OP.mult, OP.add), r=["PF0", "COL"], w=["m"])
+    op("V", ts(pf(18), pf(5), float(16 + (q >> 2)), pf(17), OP.mult, OP.add), r=["PF4", "PF17"], w=["PF18"])
+    op("V", ts(T.TA[:], T.COL[:, 0:128], pf(2), None, OP.is_ge, c=us(128)), r=["PF0", "COL"], w=["TA"])
+    op("V", ts(T.TB[:], T.COL[:, 0:128], pf(10), None, OP.is_le, c=us(128)), r=["PF10", "COL"], w=["TB"])
+    op("V", ts(T.TC[:], T.COL[:, 0:128], pf(0), -1.0, OP.is_lt, OP.mult, c=us(128)), r=["PF0", "COL"], w=["TC"])
+    op("V", ts(pf(19), pf(7), 32.0, pf(18), OP.mult, OP.add), r=["PF4", "PF18"], w=["PF19"])
+    op("V", ts(wf(1), wf(0), 4608.0, None, OP.add), r=["m"], w=["my"])
+    weights(WT, pf(15), ["PF15"])
+    weights(WY, pf(16), ["PF16"])
+    op("V", tt(T.GRP[:], T.TA[:], T.TB[:], OP.mult, us(256)), r=["TA", "TB"], w=["GRP"])
+    op("V", tt(T.NUP[:], T.TA[:], T.TC[:], OP.mult, us(256)), r=["TA", "TC"], w=["NUP"])
+    op("V", fill(T.HW0[:, 5120:5136], 0.0), w=["zero0"])
+    op("V", fill(T.HW1[:, 5120:5136], 0.0), w=["zero1"])
+    op("V", cp(T.NL[:], T.NBI[:], us(256)), r=["NBI"], w=["NL"])
+    op("V", ts(T.N1[:], T.NBI[:], 9, None, OP.arith_shift_right, c=us(256)), r=["NBI"], w=["N1"])
+    op("V", ts(T.N2[:], T.NBI[:], 255, None, OP.bitwise_and, c=us(256)), r=["NBI"], w=["N2"])
+    op("V", tt(T.KLO[:], T.N1[:], T.C8[:], OP.add, us(512)), r=["N1", "C8"], w=["KLO"])
+    op("V", ts(T.N3[:], T.NBI[:], 8, 1, OP.arith_shift_right, OP.bitwise_and, c=us(256)), r=["NBI"], w=["N3"])
+    op("V", cp(T.TLO[:], T.N2[:], us(256)), r=["N2"], w=["TLO"])
+    op("V", tt(T.THI[:], T.N3[:], T.KX[:], OP.add, us(512)), r=["N3", "KX"], w=["THI"])
+    op("S", act(T.RT[:], T.CT[:], AF.Identity, us(256), bias=pf(1), scale=0.0), r=["CT", "PF0"], w=["RT"])
+    dma("Y", [(T.MT[f:128:16, :], x[:]) for f, x in enumerate((T.TLO, T.THI, T.RT, T.CT))], "dmt",
+        r=["TLO", "THI", "RT", "CT"], w=["MT"] + ["MT%d" % j for j in range(4)], lat=2.6)
+    op("V", ts(T.LU[:, 48:80], T.LJ[:], pf(1), None, OP.add), r=["PF0", "LJ"], w=["LU3"])
+    op("V", ts(pf(8), pf(1), 31.0, pf(3), OP.mult, OP.add), r=["PF0"], w=["PF8"])
+    op("V", ts(T.LU[:, 80:96], T.COL[:, 0:16], pf(8), None, OP.add), r=["PF8", "COL"], w=["LU4"])
+    op("V", cp(T.EX[:], T.EI[:, 0:256].indirect(T.LU[:, 48:80]), got(512)), r=["EI", "LU3"], w=["EX"])
+    op("V", (lambda: V.transpose(T.ET[:], T.EX[:]), us(512)), r=["EX"], w=["ET"])
+    op("V", cp(T.EG[:], T.ET[:, 0:512].indirect(T.LU[:, 80:96]), got(256)), r=["ET", "LU4"], w=["EG0", "EG1"])
+    op("V", cp(T.EU[:], T.EG[:], us(256)), r=["EG0", "EG1"], w=["EU%d" % c for c in range(4)])
+    op("V", ts(T.E1[:], T.EI[:], 127, None, OP.bitwise_and, c=us(256)), r=["EI"], w=["E1"])
+    op("V", ts(T.E2[:], T.EI[:], 7, None, OP.arith_shift_right, c=us(256)), r=["EI"], w=["E2"])
+    op("V", cp(T.ELO[:], T.E1[:], us(256)), r=["E1"], w=["ELO"])
+    op("V", cp(T.EHI[:], T.E2[:], us(256)), r=["E2"], w=["EHI"])
+    dma("Y", [(T.EW[0:128:16, 0:4096], T.ELO[:]), (T.EW[1:128:16, 0:4096], T.EHI[:])], "dew", r=["ELO", "EHI"],
+        w=["EW"] + ["EW%d" % j for j in range(4)], lat=2.6)
+    op("V", ts(T.P1[:], T.P1[:], pf(4), None, OP.mult, c=us(192)), r=["P1", "PF4"], w=["P1"])
+    op("V", ts(T.P2[:], T.P2[:], pf(5), None, OP.mult, c=us(192)), r=["P2", "PF4"], w=["P2"])
+    op("V", ts(T.PF[:, 20:24], T.COL[:, 0:4], 3.0, 16.0, OP.mult, OP.add), r=["COL"], w=["PF20"])
+    op("V", ts(pf(14), pf(5), 128.0, pf(4), OP.mult, OP.add), r=["PF4"], w=["PF14"])
+    op("V", ts(pf(13), pf(1), 16.0, None, OP.mult), r=["PF0"], w=["PF13"])
+    op("V", tt(T.VB[:], T.P1[:], T.P2[:], OP.add, us(768)), r=["P1", "P2"], w=["VB"])
+    op("V", ts(T.PF[:, 20:24], T.PF[:, 20:24], pf(5), None, OP.mult), r=["PF20", "PF4"], w=["PF20"])
+    weights(WE, pf(14), ["PF14"])
+    op("V", ts(T.LU[:, 0:32], T.LI[:], pf(13), None, OP.add), r=["PF13", "LI"], w=["LU1"])
+    for t in range(R):
+        op("S", act(T.VT[:, 384 * t:384 * t + 384], T.VB[:], AF.Identity, us(384), bias=pf(20 + t)), r=["VB", "PF20"], w=["VT%d" % t])
 
-    def consts_choice():
-        scaled_identity(T.IH[:], 0.5, "IH")
-        op("V", lambda: V.memset(T.ZID[:], 0.0), w=["ZID"])
-        op("V", lambda: V.memset(T.KN[:], 2.0), w=["KN"])
-        op("V", lambda: V.memset(T.M8[:], 1.0), w=["M8"])
-        op("V", lambda: V.memset(T.M32[:], 1.0), w=["M32"])
-        op("V", lambda: V.memset(T.M8[:, 0:256:8], 0.0), w=["M8"])
-        op("V", lambda: V.memset(T.M32[:, 0:256:32], 0.0), w=["M32"])
-
-    def consts_exits():
-        scaled_identity(T.IG[:], -1024.0, "IG")
-        op("V", ts(pf(11), pf(1), 256.0, None, OP.mult), r=["PF0"], w=["PF11"])
-        op("V", ts(pf(15), pf(5), 256.0, pf(4), OP.mult, OP.add), r=["PF4"], w=["PF15"])
-        op("V", ts(pf(16), pf(7), 16.0, pf(6), OP.mult, OP.add), r=["PF4"], w=["PF16"])
-        op("V", ts(pf(17), pf(4), float(64 * (q & 3)), None, OP.mult), r=["PF4"], w=["PF17"])
-        op("V", ts(wf(0), T.COL[:, 0:32], 16.0, pf(1), OP.mult, OP.add), r=["PF0", "COL"], w=["m"])
-        op("V", ts(pf(18), pf(5), float(16 + (q >> 2)), pf(17), OP.mult, OP.add), r=["PF4", "PF17"], w=["PF18"])
-        op("V", ts(T.TA[:], T.COL[:, 0:128], pf(0), None, OP.is_gt), r=["PF0", "COL"], w=["TA"])
-        op("V", ts(T.TB[:], T.COL[:, 0:128], pf(2), None, OP.is_le), r=["PF2", "COL"], w=["TB"])
-        op("V", ts(pf(19), pf(7), 32.0, pf(18), OP.mult, OP.add), r=["PF4", "PF18"], w=["PF19"])
-        op("V", ts(wf(1), wf(0), 4608.0, None, OP.add), r=["m"], w=["my"])
-        weights(WT, pf(15), ["PF15"])
-        weights(WY, pf(16), ["PF16"])
-        op("V", lambda: V.memset(T.ONE[:], 1.0), w=["ONE"])
-        op("V", tt(T.TRI[:], T.TA[:], T.TB[:], OP.mult), r=["TA", "TB"], w=["TRI"])
-        op("V", lambda: V.memset(T.HW0[:, 5120:5136], 0.0), w=["zero0"])
-        op("V", lambda: V.memset(T.HW1[:, 5120:5136], 0.0), w=["zero1"])
-
-    def neighbours_a():
-        op("V", cp(T.NX[:], T.NBI[:, 0:256].indirect(T.LU[:, 32:64])), r=["NBI", "LU1"], w=["NX"])
-        op("V", lambda: V.transpose(T.NT[:], T.NX[:]), r=["NX"], w=["NT"])
-        op("V", cp(T.NI[:], T.NT[:, 0:512].indirect(T.LU[:, 64:80])), r=["NT", "LU2"], w=["NI"])
-
-    def neighbours_b():
-        op("V", cp(T.NL0[:], T.NI[:]), r=["NI"], w=["NL0"])
-        op("V", ts(T.N1[:], T.NI[:], 9, None, OP.arith_shift_right), r=["NI"], w=["N1"])
-        op("V", ts(T.N2[:], T.NI[:], 31, None, OP.bitwise_and), r=["NI"], w=["N2"])
-        op("V", tt(T.KLO[:], T.N1[:], T.C8[:], OP.add), r=["N1", "C8"], w=["KLO"])
-
-    def neighbours_c():
-        op("V", ts(T.N3[:], T.NI[:], 5, 15, OP.arith_shift_right, OP.bitwise_and), r=["NI"], w=["N3"])
-        op("V", tt(T.TLO[:], T.N2[:], T.KX[:], OP.add), r=["N2", "KX"], w=["TLO"])
-        op("V", cp(T.THI[:], T.N3[:]), r=["N3"], w=["THI"])
-        op("V", ts(T.RT[:], T.CT[:], 0.0, pf(1), OP.mult, OP.add), r=["CT", "PF0"], w=["RT"])
-        dma("Y", [(T.MT[f:128:16, :], x[:]) for f, x in enumerate((T.TLO, T.THI, T.RT, T.CT))], "dmt",
-            r=["TLO", "THI", "RT", "CT"], w=["MT"])
-
-    def neighbours_d():
-        op("V", ts(T.N4[:], T.N1[:], 512.0, None, OP.mult), r=["N1"], w=["N4"])
-        op("V", ts(T.N5[:], T.N2[:], 16.0, None, OP.mult), r=["N2"], w=["N5"])
-        op("V", tt(T.N4[:], T.N4[:], T.N3[:], OP.add), r=["N4", "N3"], w=["N4"])
-        op("V", tt(T.N4[:], T.N4[:], T.N5[:], OP.add), r=["N4", "N5"], w=["N4"])
-        op("V", cp(T.NL1[:], T.N4[:]), r=["N4"], w=["NL1"])
-
-    def entries_0():
-        op("V", ts(T.E1[:], T.EI[:], 127, None, OP.bitwise_and), r=["EI"], w=["E1"])
-        op("V", ts(T.E2[:], T.EI[:], 7, None, OP.arith_shift_right), r=["EI"], w=["E2"])
-        op("V", cp(T.ELO[:], T.E1[:]), r=["E1"], w=["ELO"])
-        op("V", cp(T.EHI[:], T.E2[:]), r=["E2"], w=["EHI"])
-        op("V", lambda: V.memset(T.EW[:, 2048:4608], 0.0), w=["EWb"])
-        dma("Y", [(T.EW[0:128:16, 0:4096], T.ELO[:]), (T.EW[1:128:16, 0:4096], T.EHI[:])], "dew", r=["ELO", "EHI"], w=["EW", "EWb"])
-        op("V", ts(T.P1[:], T.P1[:], pf(4), None, OP.mult), r=["P1", "PF4"], w=["P1"])
-        op("V", ts(T.P2[:], T.P2[:], pf(5), None, OP.mult), r=["P2", "PF4"], w=["P2"])
-        op("V", ts(T.PF[:, 20:24], T.COL[:, 0:4], 3.0, 16.0, OP.mult, OP.add), r=["COL"], w=["PF20"])
-        op("V", ts(pf(14), pf(5), 128.0, pf(4), OP.mult, OP.add), r=["PF4"], w=["PF14"])
-        op("V", ts(pf(13), pf(1), 16.0, None, OP.mult), r=["PF0"], w=["PF13"])
-        op("V", tt(T.VB[:], T.P1[:], T.P2[:], OP.add), r=["P1", "P2"], w=["VB"])
-        op("V", ts(T.PF[:, 20:24], T.PF[:, 20:24], pf(5), None, OP.mult), r=["PF20", "PF4"], w=["PF20"])
-        weights(WE, pf(14), ["PF14"])
-        op("V", ts(T.LU[:, 96:128], T.LI[:, 32:64], pf(13), None, OP.add), r=["PF13", "LI1"], w=["LU3"])
-
-    def y_a(t):
+    def jump(t):
+        H, p = HW[t % 2], t % 2
+        C, Y, c_, y_ = H[:, 4096:4608], H[:, 4608:5120], "C%d" % p, "Y%d" % p
         op("P", mm(sel(T.B7[:, 0:32], WJ, lambda r: T.XB[:, r:512:16])), r=["X", "WS5"], w=["jP"], b=[7])
-
-    def y_b(t):
         op("V", cp(wi_(0), T.B7[:, 0:32]), r=["jP"], w=["ji"], b=[7])
         op("V", ts(wi_(1), wi_(0), 511, None, OP.bitwise_and), r=["ji"], w=["ja"])
         op("V", cp(wu(0), wi_(1)), r=["ja"], w=["ju"])
-
-    def y_c1(t):
-        op("S", act(T.JG[:], T.JT[:, 0:512].indirect(wu(0)), AF.Copy), r=["JT", "ju"], w=["JG"])
-        op("P", mm([(T.B2[:], T.ID[:], T.XB[:]), (T.B2[:], T.NID[:], T.JG[:])]), r=["X", "JG", "ID", "NID"], w=["B2"], b=[2])
-
-    def y_c2(t):
-        H, p = HW[t % 2], t % 2
-        C, Y = H[:, 4096:4608], H[:, 4608:5120]
-        op("S", act(Y, T.B2[:], AF.Abs), r=["B2"], w=["Y%d" % p], b=[2])
-        op("P", mm([(T.B0[:], T.ID[:], Y)]), r=["Y%d" % p], w=["B0"], b=[0])
-        op("P", mm(sel(T.B7[:, 160:224], W1, lambda r: H[:, 4096 + r:5120:16])), r=["C%d" % p, "Y%d" % p, "WS0"], w=["SyP"], b=[7])
-        op("P", mm([(T.B2[:], T.ID[:], C), (T.B2[:], T.NID[:], Y)]), r=["C%d" % p, "Y%d" % p], w=["B2"], b=[2])
-
-    def y_c3(t):
-        op("S", act(T.SC2[:, 0:32], T.B7[:, 160:192], AF.Copy), r=["SyP"], w=["SC2a"], b=[7])
-        op("S", act(T.SC2[:, 32:64], T.B7[:, 160:192], AF.Copy), r=["SyP"], w=["SC2b"], b=[7])
-        op("S", act(T.SY2[:, 0:32], T.B7[:, 192:224], AF.Copy), r=["SyP"], w=["SY2a"], b=[7])
-        op("S", act(T.SY2[:, 32:64], T.B7[:, 192:224], AF.Copy), r=["SyP"], w=["SY2b"], b=[7])
-        op("S", act(T.OA[:], T.B2[:], AF.Abs), r=["B2"], w=["OA"], b=[2])
-        op("P", mm(sel(T.B7[:, 64:96], W2048, lambda r: T.OA[:, r:512:16])), r=["OA", "WS4"], w=["ownP"], b=[7])
-
-    def y_d(t):
-        op("V", cp(wi_(2), T.SY2[:, 0:32]), r=["SY2a"], w=["ui"])
-        op("V", ts(wf(2), T.B7[:, 64:96], pf(12), None, OP.subtract), r=["ownP", "A"], w=["thr"], b=[7])
+        if CFG["JV"][t]:
+            op("V", tt(T.JG[:], T.JT[:, 0:512].indirect(wu(0)), T.XB[:], OP.subtract, got(512)), r=["JT", "ju", "X"], w=["JG"])
+            op("S", act(Y, T.JG[:], AF.Abs, us(512)), r=["JG"], w=[y_])
+        else:
+            op("S", act(T.JG[:], T.JT[:, 0:512].indirect(wu(0)), AF.Copy, got(512)), r=["JT", "ju"], w=["JG"])
+            op("P", mm([(T.B2[:], T.ID[:], T.XB[:]), (T.B2[:], T.NID[:], T.JG[:])], 512), r=["X", "JG", "ID", "NID"], w=["B2"], b=[2])
+            op("S", act(Y, T.B2[:], AF.Abs, us(512)), r=["B2"], w=[y_], b=[2])
+        op("P", mm(sel(T.B7[:, 160:224], W1, lambda r: H[:, 4096 + r:5120:16])), r=[c_, y_, "WS0"], w=["SyP"], b=[7])
+        op("P", mm([(T.B2[:], T.ID[:], C), (T.B2[:], T.NID[:], Y)], 512), r=[c_, y_, "ID", "NID"], w=["B2"], b=[2])
+        for j in range(2):
+            op("S", act(T.SC2[:, 32 * j:32 * j + 32], T.B7[:, 160:192], AF.Copy), r=["SyP"], w=["SC2%d" % j], b=[7])
+            op("S", act(T.SY2[:, 32 * j:32 * j + 32], T.B7[:, 192:224], AF.Copy), r=["SyP"], w=["SY2%d" % j], b=[7])
+        op("S", act(T.OA[:], T.B2[:], AF.Abs, us(512)), r=["B2"], w=["OA"], b=[2])
+        op("P", mm(sel(T.B7[:, 64:96], W4096, lambda r: T.OA[:, r:512:16])), r=["OA", "WS4"], w=["ownP"], b=[7])
+        for j in range(2):
+            op("V", ts(T.THR[:, 32 * j:32 * j + 32], T.B7[:, 64:96], pf(12), None, OP.subtract), r=["ownP", "A"], w=["thr%d" % j], b=[7])
+        op("V", cp(wi_(2), T.SY2[:, 0:32]), r=["SY20"], w=["ui"])
         op("V", ts(wi_(3), wi_(2), 63, None, OP.bitwise_and), r=["ui"], w=["ua"])
         op("V", ts(wf(3), wi_(3), 1.0 / 64, None, OP.mult), r=["ua"], w=["u64"])
 
-    def c_prep(t):
-        H, p = HW[t % 2], t % 2
-        op("P", mm([(T.B1[:], T.ID[:], H[:, 4096:4608])]), r=["C%d" % p, "ID"], w=["B1"], b=[1])
-
-    def c_bounds(t):
-        C = HW[t % 2][:, 4096:4608]
-        op("S", act(T.CM[:], C, AF.Identity, bias=-1.0), r=["C%d" % (t % 2)], w=["CM"])
-        op("S", act(T.B2[:], C, AF.Identity, bias=1.0), r=["C%d" % (t % 2)], w=["B2"], b=[2])
-
-    def h_get(t, k):
-        H, p = HW[t % 2], t % 2
-        src = T.ZW[:, 0:2048 + 384 * t].indirect(T.EU[:, 32 * k:32 * k + 32])
-        dep = ["Z", "EU%d" % min(k // 2, 1)] + ["L%d" % u for u in range(t)]
-        if k in H_BY_VECTOR[t]:
-            op("V", cp(H[:, 512 * k:512 * k + 512], src), r=dep, w=["s%d_%d" % (p, k)])
+    def bounds(t):
+        C, c_ = HW[t % 2][:, 4096:4608], "C%d" % (t % 2)
+        if CFG["CM"] == "S":
+            op("S", act(T.CM[:], C, AF.Identity, us(512), bias=-1.0), r=[c_], w=["CM"])
         else:
-            op("S", act(H[:, 512 * k:512 * k + 512], src, AF.Copy), r=dep, w=["s%d_%d" % (p, k)])
+            op("V", ts(T.CM[:], C, -1.0, None, OP.add, c=us(256)), r=[c_], w=["CM"])
+        op("P", mm([(T.B2[:], T.ID[:], C), (T.B2[:], T.ID[:], T.ONE[:])], 512), r=[c_, "ID", "ONE"], w=["B2"], b=[2])
 
-    def h_max(t, k):
-        H, p, c = HW[t % 2], t % 2, k // 2
-        op("V", tt(T.MH[:, 512 * k:512 * k + 512], H[:, 512 * k:512 * k + 512], T.B1[:], OP.max),
-           r=["s%d_%d" % (p, k), "B1"], w=["MH%d" % k], b=[1])
-        if k % 2:
-            if (t, c) not in summed:
-                h_sum(t, c)
-            op("P", mm(sel(T.B5[:, 64 * c:64 * c + 64], WM2, lambda r: T.MH[:, 1024 * c + r:1024 * c + 1024:16]), start=False, stop=k == 7),
-               r=["MH%d" % (k - 1), "MH%d" % k, "WS1"], w=["G"], b=[5])
-
-    summed = set()
-
-    def h_sum(t, c):
+    def entries(t):
         H, p = HW[t % 2], t % 2
-        out = T.B5[:, 64 * c:64 * c + 64]
-        head = [(T.B5[:, 0:256], T.ZID[:], T.M32[:])] if c == 0 else []
-        summed.add((t, c))
-        op("P", mm(head + [(out, T.I32[:], T.SC2[:])] + sel(out, W1, lambda r: H[:, 1024 * c + r:1024 * c + 1024:16]), start=c == 0, stop=False),
-           r=["SC2a", "SC2b", "I32", "ZID", "M32", "s%d_%d" % (p, 2 * c), "s%d_%d" % (p, 2 * c + 1)], w=["G"], b=[5])
+        op("P", mm([(T.B1[:], T.ID[:], H[:, 4096:4608])], 512), r=["C%d" % p, "ID"], w=["B1"], b=[1])
+        op("P", mm([(T.B5[:, 0:256], T.ZID[:], T.M32[:])], 256, stop=False), r=["ZID", "M32"], w=["G", "Go"], b=[5])
+        kinds = CFG["H"][t]
+        op("P", mm([(T.B5[:, 64 * c:64 * c + 64], T.I32[:], T.SC2[:]) for c in range(4) if kinds[2 * c] != "E"], 256, start=False, stop=False),
+           r=["SC20", "SC21", "I32", "Go"], w=["Gc"], b=[5])
+        for k in range(8):
+            c = k // 2
+            src = T.ZW[:, 0:2048 + 384 * t].indirect(T.EU[:, 32 * k:32 * k + 32])
+            dep = ["Z", "EU%d" % c] + ["L%d" % u for u in range(t)]
+            s_, sk, mh = H[:, 512 * k:512 * k + 512], "s%d_%d" % (p, k), T.MH[:, 512 * k:512 * k + 512]
+            if kinds[k] == "V":
+                op("V", cp(s_, src, got(512)), r=dep, w=[sk])
+            else:
+                op("S", act(s_, src, AF.Copy, got(512)), r=dep, w=[sk, "~S"])
+            if kinds[k] == "E":
+                op("P", mm([(T.B0[:], T.ID[:], s_), (T.B0[:], T.NID[:], H[:, 4096:4608])], 512), r=[sk, "C%d" % p, "ID", "NID"], w=["B0"], b=[0])
+                op("S", act(mh, T.B0[:], AF.Abs, us(512)), r=["B0"], w=["MH%d" % k], b=[0])
+            else:
+                op("V", tt(mh, s_, T.B1[:], OP.max, us(512)), r=[sk, "B1"], w=["MH%d" % k], b=[1])
+            if k % 2:
+                out = T.B5[:, 64 * c:64 * c + 64]
+                if kinds[k] != "E":
+                    op("P", mm(sel(out, W1, lambda r, c=c: H[:, 1024 * c + r:1024 * c + 1024:16]), start=False, stop=False),
+                       r=["Go", "WS0", "s%d_%d" % (p, k - 1), sk], w=["Ga%d" % c], b=[5])
+                op("P", mm(sel(out, WM1 if kinds[k] == "E" else WM2, lambda r, c=c: T.MH[:, 1024 * c + r:1024 * c + 1024:16]), start=False, stop=False),
+                   r=["Go", "WS1", "WS9", "MH%d" % (k - 1), "MH%d" % k], w=["Gb%d" % c], b=[5])
+        op("P", mm([(T.B5[:, 0:64], T.ZID[:], T.M32[:, 0:64])], start=False), r=["Gc"] + ["G%s%d" % (x, c) for x in "ab" for c in range(4)], w=["G"], b=[5])
 
     def flux(t):
-        items = [(T.B6[:, 256:512], T.IH[:], T.KN[:])] + [(T.B6[:, 256:512], T.IH[:], T.SG[:, 256 * u:256 * u + 256]) for u in range(t)]
-        op("P", mm(items), r=["IH", "KN"] + ["SG%d" % u for u in range(t)], w=["n"], b=[6])
+        n = T.B6[:, 256:512]
+        items = [(n, T.ID[:], T.ONE[:, 0:256])]
+        for u in range(t):
+            items += [(n, T.IH[:], T.ONE[:, 0:256]), (n, T.IH[:], T.SG[:, 256 * u:256 * u + 256])]
+        op("P", mm(items, 256), r=["IH", "ID", "ONE"] + ["SG%d" % u for u in range(t)], w=["n"], b=[6])
 
-    def choice_a(t):
-        op("S", act(T.RG[:], T.B5[:, 0:256], AF.Relu, bias=2047.0), r=["G"], w=["RG"], b=[5])
+    def neighbours(t):
+        H, p = HW[t % 2], t % 2
+        Y, y_ = H[:, 4608:5120], "Y%d" % p
+        dep = ["CA%d" % t, "NL", "cen" if t == 0 else "CAown"]
+        op("P", mm([(T.B0[:], T.ID[:], Y)], 512), r=[y_, "ID"], w=["B0"], b=[0])
+        for c in range(4):
+            kind, bk = CFG["D"][t][c], 3 + c % 2
+            out = T["B%d" % bk][:, 64 * c:64 * c + 64]
+            head = [(out, T.ID[:], T.KHI[:, 64 * c:64 * c + 64]), (out, T.ID[:], T.KLO[:, 64 * c:64 * c + 64])]
+            free = ["KD%d" % (c - 2)] if c > 1 else ["pf", "mP"]
+            for k in (2 * c, 2 * c + 1):
+                src = CA[t][:, 0:4096].indirect(T.NL[:, 32 * k:32 * k + 32])
+                ag, mx = T.AG[:, 512 * k:512 * k + 512], T.MX[:, 512 * k:512 * k + 512]
+                if kind == "C":
+                    op("S", act(ag, src, AF.Copy, got(512)), r=dep, w=["AG%d" % k, "~S"])
+                    op("V", tt(mx, ag, T.B0[:], OP.max, us(512)), r=["AG%d" % k, "B0"], w=["MX%d" % k], b=[0])
+                elif kind == "E":
+                    op("S", act(ag, src, AF.Copy, got(512)), r=dep, w=["AG%d" % k, "~S"])
+                    op("P", mm([(T.B1[:], T.ID[:], ag), (T.B1[:], T.NID[:], Y)], 512), r=["AG%d" % k, y_, "ID", "NID"], w=["B1"], b=[1])
+                    op("S", act(mx, T.B1[:], AF.Abs, us(512)), r=["B1"], w=["MX%d" % k], b=[1])
+                else:
+                    op("V", tt(ag, src, Y, OP.subtract, got(512)), r=dep + [y_], w=["AG%d" % k])
+                    if kind == "A":
+                        op("S", act(mx, ag, AF.Abs, us(512)), r=["AG%d" % k], w=["MX%d" % k])
+                    else:
+                        op("V", ts(mx, ag, 0.0, None, OP.max, c=us(256)), r=["AG%d" % k], w=["MX%d" % k])
+            ags, mxs = ["AG%d" % (2 * c), "AG%d" % (2 * c + 1)], ["MX%d" % (2 * c), "MX%d" % (2 * c + 1)]
+            if kind not in "AE":
+                sy = [(out, T.IS[:], T.SY2[:])] if kind == "C" else []
+                op("P", mm(sy + sel(out, WM4096, lambda r, c=c: T.AG[:, 1024 * c + r:1024 * c + 1024:16]), more=192 * len(sy), stop=False),
+                   r=["IS", "SY20", "SY21", "WS3"] + ags + free, w=["KD%d" % c], b=[bk])
+            op("P", mm(sel(out, W4096 if kind in "AE" else W8192, lambda r, c=c: T.MX[:, 1024 * c + r:1024 * c + 1024:16]) + head, start=kind in "AE"),
+               r=["WS2", "WS4", "KHI", "KLO", "ID"] + mxs + free, w=["KD%d" % c], b=[bk])
+            op("V", tt(T.RUN[:], T.THR[:] if c == 0 else T.RUN[:], out, OP.min), r=["thr0", "thr1", "RUN", "KD%d" % c], w=["RUN"], b=[bk])
+        op("V", tt(wi_(4), T.RUN[:, 0:32], T.RUN[:, 32:64], OP.min), r=["RUN"], w=["kz"])
 
-    def choice_b(t):
+    def choice(t):
+        op("S", act(T.RG[:], T.B5[:, 0:256], AF.Relu, us(256), bias=2047.0), r=["G"], w=["RG"], b=[5])
         for k in range(8):
             op("V", tt(T.G2[:, k:256:8], T.RG[:, 32 * k:32 * k + 32], T.B6[:, 256 + 32 * k:288 + 32 * k], OP.mult),
                r=["RG", "n"], w=["G2_%d" % k], b=[6])
-        op("V", lambda: V.tensor_tensor_scan(T.PP[:], T.M8[:], T.G2[:], 0.0, OP.mult, OP.add), r=["M8"] + ["G2_%d" % k for k in range(8)], w=["PP"])
-
-    def choice_c(t):
-        op("V", tt(wf(4), T.PP[:, 7:256:8], wf(3), OP.mult), r=["PP", "u64"], w=["th2"])
+        op("V", scan(T.PP[:], T.M8[:], T.G2[:], us(256)), r=["M8"] + ["G2_%d" % k for k in range(8)], w=["PP"])
+        fold = CFG["FOLD"][t]
+        if fold:
+            op("V", tt(T.GO[:], wi_(4), T.THR[:, 0:32], OP.is_ge), r=["kz", "thr0"], w=["go"])
+            op("V", tt(wf(2), wf(3), T.GO[:], OP.max), r=["u64", "go"], w=["uf"])
+        op("V", tt(wf(4), T.PP[:, 7:256:8], wf(2) if fold else wf(3), OP.mult), r=["PP", "u64", "uf"], w=["th2"])
         for k in range(8):
             op("V", tt(T.NC[:, 32 * k:32 * k + 32], T.PP[:, k:256:8], wf(4), OP.is_le), r=["PP", "th2"], w=["NC%d" % k])
-        op("P", mm([(T.B7[:, 96:128], T.ID[:], T.NC[:, 32 * k:32 * k + 32]) for k in range(8)]), r=["NC%d" % k for k in range(8)], w=["fP"], b=[7])
+        out = T.B7[:, 96:128]
+        items = [(out, T.I512[:], T.NC[:, 32 * k:32 * k + 32]) for k in range(8)]
+        nc = ["NC%d" % k for k in range(8)] + ["I512"]
+        if fold:
+            items = [(out, T.I512[:], T.GO[:]), (out, T.I16[:], T.CT[:, 0:32]), (out, T.ID[:], T.RT[:, 0:32])] + items
+            op("P", mm(items), r=nc + ["go", "I16", "CT", "ID", "RT"], w=["fP"], b=[7])
+            op("V", cp(wu(2), out), r=["fP"], w=["xu"], b=[7])
+        else:
+            op("P", mm(items), r=nc, w=["fP"], b=[7])
+            op("V", ts(wf(5), out, -4608.0, None, OP.add), r=["fP"], w=["fz"], b=[7])
+            op("V", tt(T.GO[:], wi_(4), T.THR[:, 0:32], OP.is_lt), r=["kz", "thr0"], w=["go"])
+            op("V", tt(wf(7), wf(5), T.GO[:], OP.mult), r=["fz", "go"], w=["x1"])
+            op("V", tt(wf(9), wf(7), wf(1), OP.add), r=["x1", "my"], w=["x2"])
+            op("V", cp(wu(2), wf(9)), r=["x2"], w=["xu"])
 
-    def choice_d(t):
-        op("V", ts(wf(5), T.B7[:, 96:128], -9.0, 512.0, OP.add, OP.mult), r=["fP"], w=["fz"], b=[7])
-
-    def d_phase(t, fill):
-        H, p = HW[t % 2], t % 2
-        Y = H[:, 4608:5120]
-        path = D_PATH[t]
-        lst, ln = (T.NL0, "NL0") if t == 0 else (T.NL1, "NL1")
-        dep = ["CA%d" % t, ln] + (["cen"] if t == 0 else [])
-        late = []
-        for k in range(8):
-            if path[k // 2] == "A":
-                late.append(lambda k=k: op("V", tt(T.AG[:, 512 * k:512 * k + 512], CA[t][:, 0:4096].indirect(lst[:, 32 * k:32 * k + 32]), Y, OP.subtract),
-                                           r=dep + ["Y%d" % p], w=["AG%d" % k]))
-        last = path.rindex("C")
-
-        def place(c):
-            bk = 4 if c == last else 3
-            out = T["B%d" % bk][:, 64 * c:64 * c + 64]
-            return bk, out, [(out, T.ID[:], T.KHI[:, 64 * c:64 * c + 64]), (out, T.ID[:], T.KLO[:, 64 * c:64 * c + 64])]
-
-        def by_abs(c):
-            bk, out, head = place(c)
-            while late:
-                late.pop(0)()
-            for k in (2 * c, 2 * c + 1):
-                op("S", act(T.MX[:, 512 * k:512 * k + 512], T.AG[:, 512 * k:512 * k + 512], AF.Abs), r=["AG%d" % k], w=["MX%d" % k])
-            op("P", mm(head + sel(out, W2048, lambda r: T.MX[:, 1024 * c + r:1024 * c + 1024:16])),
-               r=["KHI", "KLO", "WS4", "MX%d" % (2 * c), "MX%d" % (2 * c + 1)], w=["KD%d" % c], b=[bk])
-        for c in range(4):
-            bk, out, head = place(c)
-            ks = (2 * c, 2 * c + 1)
-            if path[c] == "C":
-                for k in ks:
-                    op("S", act(T.AG[:, 512 * k:512 * k + 512], CA[t][:, 0:4096].indirect(lst[:, 32 * k:32 * k + 32]), AF.Copy), r=dep, w=["AG%d" % k])
-                    if late and k % 2 == 0:
-                        late.pop(0)()
-                    op("V", tt(T.MX[:, 512 * k:512 * k + 512], T.AG[:, 512 * k:512 * k + 512], T.B0[:], OP.max), r=["AG%d" % k, "B0"], w=["MX%d" % k], b=[0])
-                op("P", mm(head + [(out, T.IS[:], T.SY2[:])] + sel(out, WM2048, lambda r: T.AG[:, 1024 * c + r:1024 * c + 1024:16]), stop=False),
-                   r=["KHI", "KLO", "IS", "SY2a", "SY2b", "WS3"] + ["AG%d" % k for k in ks], w=["KD%d" % c], b=[bk])
-                if c == last:
-                    for cc in range(last + 1, 4):
-                        by_abs(cc)
-                op("P", mm(sel(out, W4096, lambda r: T.MX[:, 1024 * c + r:1024 * c + 1024:16]), start=False),
-                   r=["WS2"] + ["MX%d" % k for k in ks], w=["KD%d" % c], b=[bk])
-            for f in fill.get(c, ()):
-                f()
-        order = [c for c in range(4) if c != last] + [last]
-        op("V", cp(T.RUN[:], place(order[0])[1]), r=["KD%d" % c for c in order[:3]], w=["RUN"], b=[3])
-        for c in order[1:]:
-            op("V", tt(T.RUN[:], T.RUN[:], place(c)[1], OP.min), r=["RUN", "KD%d" % c], w=["RUN"], b=[place(c)[0]])
-        op("V", tt(wf(6), T.RUN[:, 0:32], T.RUN[:, 32:64], OP.min), r=["RUN"], w=["km"])
-
-    def window(t):
-        p = t % 2
-        return HW[p][:, 0:5120].indirect(wu(2)), ["s%d_%d" % (p, k) for k in range(8)] + ["C%d" % p, "Y%d" % p, "xu"]
-
-    def x_1(t):
-        op("V", tt(wf(7), wf(5), T.GO[:], OP.mult), r=["fz", "go"], w=["x1"])
-
-    def x_2(t):
-        op("V", tt(wf(9), wf(7), wf(1), OP.add), r=["x1", "my"], w=["x2"])
-
-    def x_3(t):
-        op("V", cp(wu(2), wf(9)), r=["x2"], w=["xu"])
-
-    def x_get(t):
-        src, dep = window(t)
-        op("S", act(T.XB[:], src, AF.Copy), r=dep, w=["X"])
-
-    def c_max(t):
-        src, dep = window(t)
-        op("V", tt(T.TM[:], src, T.CM[:], OP.max), r=dep + ["CM"], w=["TM"])
-
-    def c_new(t):
-        pn = 1 - t % 2
-        op("V", tt(HW[pn][:, 4096:4608], T.TM[:], T.B2[:], OP.min), r=["TM", "B2"], w=["C%d" % pn], b=[2])
+    def move(t):
+        p, pn = t % 2, 1 - t % 2
+        src = HW[p][:, 0:5120].indirect(wu(2))
+        dep = ["s%d_%d" % (p, k) for k in range(8)] + ["C%d" % p, "Y%d" % p, "xu"]
+        new = HW[pn][:, 4096:4608]
+        op("V", tt(T.TM[:], src, T.CM[:], OP.max, got(512)), r=dep + ["CM"], w=["TM"])
+        op("V", tt(new, T.TM[:], T.B2[:], OP.min, us(512)), r=["TM", "B2"], w=["C%d" % pn], b=[2])
+        op("S", act(T.XB[:], src, AF.Copy, got(512)), r=dep, w=["X"])
         if t < R - 1:
-            send("c", t + 1, "C%d" % pn, "CA%d" % (t + 1), src=HW[pn][:, 4096:4608])
+            send("c", t + 1, "C%d" % pn, "CA%d" % (t + 1), src=new)
+            own = CA[t + 1][:, 512 * q:512 * q + 512]
+            if CFG["CP"] == "S":
+                op("S", act(own, new, AF.Copy, us(512)), r=["C%d" % pn], w=["CAown"])
+            else:
+                op("V", cp(own, new, us(256)), r=["C%d" % pn], w=["CAown"])
 
-    def exits(t, gap):
+    def exits(t):
         H, p = HW[t % 2], t % 2
-
-        def fill(i):
-            for f in gap.get(i, ()):
-                f()
-        op("V", cp(wi_(4), wf(6)), r=["km"], w=["kz"])
-        op("V", tt(T.GO[:], wf(6), wf(2), OP.is_lt), r=["km", "thr"], w=["go"])
-        op("V", ts(wi_(5), wi_(4), 7, None, OP.bitwise_and), r=["kz"], w=["o"])
+        op("S", act(T.SB[:, 512:896], T.S48[:], AF.Identity, us(384), bias=pf(19), scale=pf(4)), r=["S48", "PF19", "PF4"], w=["SB"])
+        op("V", ts(wi_(5), wi_(4), 2055, None, OP.bitwise_and), r=["kz"], w=["og"])
         op("V", ts(wi_(6), wi_(4), 3, 255, OP.arith_shift_right, OP.bitwise_and), r=["kz"], w=["kc"])
-        fill(0)
-        op("V", ts(wf(8), wi_(5), 1.0, None, OP.add), r=["o"], w=["o1"])
         op("V", ts(wu(1), wi_(6), pf(11), None, OP.add), r=["kc", "PF11"], w=["mu"])
-        fill(1)
-        op("V", tt(wf(10), wf(8), T.GO[:], OP.mult), r=["o1", "go"], w=["og"])
-        fill(2)
-        op("S", act(T.MS[:], T.MT[:, 0:4096].indirect(wu(1)), AF.Copy), r=["MT", "mu"], w=["MS"])
-        fill(3)
+        op("S", act(T.MS[:], T.MT[:, 0:4096].indirect(wu(1)), AF.Copy, got(512)), r=["MT", "mu"], w=["MS"])
         for o in range(8):
-            op("V", ts(T.HIT[:, 32 * o:32 * o + 32], wf(10), float(o + 1), None, OP.is_equal), r=["og"], w=["HIT%d" % o])
+            op("V", ts(T.HIT[:, 32 * o:32 * o + 32], wi_(5), float(2048 + o), None, OP.is_equal), r=["og"], w=["HIT%d" % o])
         hit = ["HIT%d" % o for o in range(8)]
-        op("V", lambda: V.tensor_tensor_scan(T.INC[:], T.M32[:], T.HIT[:], 0.0, OP.mult, OP.add), r=["M32"] + hit, w=["INC"])
-        op("P", mm([(T.B3[:, 256:512], T.ID[:], T.HIT[:]), (T.B3[:, 256:512:32], T.TRI[:], T.INC[:, 31:256:32])]), r=hit + ["INC", "TRI"], w=["pf"], b=[3])
-        op("V", ts(wf(11), wf(10), 48.0, 463.0 + 1024.0, OP.mult, OP.add), r=["og"], w=["t1"])
-        fill(4)
-        op("V", lambda: V.tensor_tensor_scan(T.B4[:, 256:512], T.M32[:], T.B3[:, 256:512], 0.0, OP.mult, OP.add), r=["M32", "pf"], w=["SC"], b=[3, 4])
-        op("V", tt(T.PRD[:], T.B4[:, 256:512], T.HIT[:], OP.mult), r=["SC"] + hit, w=["PRD"], b=[4])
-        op("P", mm([(T.B7[:, 128:160], T.IG[:], T.GO[:])] + [(T.B7[:, 128:160], T.ID[:], T.PRD[:, 32 * o:32 * o + 32]) for o in range(8)]),
-           r=["PRD", "go", "IG"], w=["cnt"], b=[7])
-        fill(5)
-        op("V", ts(wf(12), T.B7[:, 128:160], 48.0 - 1024.0, None, OP.is_le), r=["cnt"], w=["ar"], b=[7])
+        op("V", scan(T.INC[:], T.M32[:], T.HIT[:], us(128)), r=["M32"] + hit, w=["INC"])
+        op("P", mm([(T.B3[:, 256:512], T.NUP[:], T.HIT[:]), (T.B3[:, 256:512], T.GRP[:], T.INC[:])], 256), r=hit + ["INC", "GRP", "NUP"], w=["pf"], b=[3])
+        op("V", ts(wf(11), wi_(5), 48.0, 511.0 - 48.0 * 2048, OP.mult, OP.add), r=["og"], w=["t1"])
+        op("V", tt(T.PRD[:], T.B3[:, 256:512], T.HIT[:], OP.mult, us(256)), r=["pf"] + hit, w=["PRD"], b=[3])
+        op("P", mm([(T.B7[:, 128:160], T.ID[:], T.PRD[:, 32 * o:32 * o + 32]) for o in range(8)]), r=["PRD", "ID"], w=["cnt"], b=[7])
+        op("V", ts(wf(12), T.B7[:, 128:160], 48.0, None, OP.is_le), r=["cnt"], w=["ar"], b=[7])
         op("V", tt(wf(13), T.B7[:, 128:160], wf(11), OP.add), r=["cnt", "t1"], w=["val"], b=[7])
-        if t < R - 1:
-            op("P", mm([(T.B6[:, 64:65], T.ONE[:], T.INC[:, 31 + 32 * o:32 + 32 * o]) for o in range(8)]), r=["INC", "ONE"], w=["AP"], b=[6])
-        fill(6)
         op("V", tt(wf(14), wf(13), wf(12), OP.mult), r=["val", "ar"], w=["v2"])
         op("V", tt(wf(15), wf(14), wf(0), OP.max), r=["v2", "m"], w=["v3"])
         op("V", cp(wu(3), wf(15)), r=["v3"], w=["su"])
-        fill(7)
-        op("V", cp(T.SB[:, 0:896].indirect(wu(3)), T.MS[:]), r=["MS", "su"], w=["SB"])
+        op("V", cp(T.SB[:, 0:896].indirect(wu(3)), T.MS[:], put(512)), r=["MS", "su"], w=["SB"])
         op("P", mm(sel(T.B4[:, 0:24], WT, lambda r: T.SB[:, 512 + r:896:16])), r=["SB", "WS7"], w=["mP"], b=[4])
         op("P", mm(sel(T.B3[:, 256:280], WY, lambda r: T.SB[:, 512 + r:896:16])), r=["SB", "WS8"], w=["pf"], b=[3])
-        fill(8)
         op("V", cp(T.META[:, 32 * t:32 * t + 24], T.B4[:, 0:24]), r=["mP"], w=["META%d" % t], b=[4])
         send("m", t, "META%d" % t, "LM%d" % t)
-        fill(9)
         op("V", cp(T.WU[:, 128:152], T.B3[:, 256:280]), r=["pf"], w=["yu"], b=[3])
-        op("S", act(T.YS[:, 384 * t:384 * t + 384], H[:, 4608:5136].indirect(T.WU[:, 128:152]), AF.Copy),
+        op("S", act(T.YS[:, 384 * t:384 * t + 384], H[:, 4608:5136].indirect(T.WU[:, 128:152]), AF.Copy, got(384)),
            r=["Y%d" % p, "zero%d" % p, "yu"], w=["YS%d" % t])
         send("y", t, "YS%d" % t, "L%d" % t)
+        if t < R - 1:
+            op("P", mm([(T.B7[:, 224:225], T.ONE[:, 0:128], T.INC[:, 31 + 32 * o:32 + 32 * o]) for o in range(8)]), r=["INC", "ONE"], w=["AP"], b=[7])
+            op("V", cp(T.PI[:, 4:5], T.B7[:, 224:225]), r=["AP"], w=["Ai"], b=[7])
+            op("V", ts(T.PI[:, 5:6], T.PI[:, 4:5], 63, None, OP.bitwise_and), r=["Ai"], w=["Aa"])
+            op("V", ts(pf(12), T.PI[:, 5:6], 4096.0, None, OP.mult), r=["Aa"], w=["A"])
 
-    def penalty(t):
-        op("V", cp(T.PI[:, 4:5], T.B6[:, 64:65]), r=["AP"], w=["Ai"], b=[6])
-        op("V", lambda: V.memset(T.KN[:], float(3 + t)), w=["KN"])
-        op("V", ts(T.PI[:, 5:6], T.PI[:, 4:5], 63, None, OP.bitwise_and), r=["Ai"], w=["Aa"])
-        op("V", ts(pf(12), T.PI[:, 5:6], 2048.0, None, OP.mult), r=["Aa"], w=["A"])
-
-    def slots_ready(t):
-        op("S", act(T.SB[:, 512:896], T.S48[:], AF.Identity, bias=pf(19), scale=pf(4)), r=["S48", "PF19", "PF4"], w=["SB"])
-
-    def places(t):
-        op("S", act(T.VT[:], T.VB[:], AF.Identity, bias=pf(20 + t)), r=["VB", "PF20"], w=["VT"])
-
-    def u_rest(t):
-        return (T.B3[:, 256:448], 3, "pf") if t % 2 else (T.B5[:, 256:448], 5, "U1")
-
-    def take_exits(t):
-        op("V", cp(T.EW[:, 0:4608].indirect(T.LM[:, 32 * t:32 * t + 24]), T.VT[:]), r=["VT", "LM%d" % t], w=["EW"])
-        op("P", mm(sel(T.B6[:, 0:64], WE, lambda r: T.EW[:, 256 * r:256 * r + 64])), r=["EW", "WS6"], w=["U0"], b=[6])
-
-    def take_rest(t):
-        out, bk, name = u_rest(t)
-        op("P", mm(sel(out, WE, lambda r: T.EW[:, 256 * r + 64:256 * r + 256])), r=["EW", "WS6"], w=[name], b=[bk])
-
-    def pool_in(t):
-        op("V", cp(T.ZW[:, 384 * t:384 * t + 384], T.ZW[:, 2048 + 384 * t:2048 + 384 * t + 384]), r=["L%d" % t], w=["Z"])
+    def arrivals(t):
+        op("V", cp(T.EW[:, 0:4608].indirect(T.LM[:, 32 * t:32 * t + 24]), T.VT[:, 384 * t:384 * t + 384], put(384)), r=["VT%d" % t, "LM%d" % t], w=["EW"])
+        lim = 0.5 - (2048 + 384 * t)
+        if t == R - 1:
+            return results(lim)
+        cuts = CFG["CUTS"]
+        for a, z in zip(cuts, cuts[1:]):
+            u, us_ = T.B6[:, 64 * a:64 * z], ["U%d" % c for c in range(a, z)]
+            op("P", mm(sel(u, WE, lambda r, a=a, z=z: T.EW[:, 1024 * a + r:1024 * z:16]), 64 * (z - a)), r=["EW", "WS6"], w=us_ + ["~U"], b=[6])
+            op("V", cp(T.EU[:, 64 * a:64 * z], u, us(64 * (z - a))), r=us_, w=["EU%d" % c for c in range(a, z)], b=[6])
+        op("S", act(T.SG[:, 256 * t:256 * t + 256], T.B6[:, 0:256], AF.Sign, us(256), bias=lim), r=["U%d" % c for c in range(4)], w=["SG%d" % t], b=[6])
+        op("V", cp(T.ZW[:, 384 * t:384 * t + 384], T.ZW[:, 2048 + 384 * t:2048 + 384 * t + 384], us(192)), r=["L%d" % t], w=["Z"])
         if t == R - 2:
             dma("Y", [(T.yz[:, 0:1152], T.ZW[:, 0:1152]), (T.yz[:, 1536:2048], T.ZW[:, 1536:2048])], "oz0", r=["Z"])
 
-    def list_0(t):
-        op("V", cp(T.EU[:, 0:64], T.B6[:, 0:64]), r=["U0"], w=["EU0"], b=[6])
+    def results(lim):
+        op("S", act(T.NQ[:], T.B6[:, 256:512], AF.Copy, us(256)), r=["n"], w=["NQ"], b=[6])
+        op("S", act(T.NX[:], T.NQ[:, 0:256].indirect(T.LU[:, 0:32]), AF.Copy, got(512)), r=["NQ", "LU1"], w=["NX"])
+        op("V", (lambda: V.transpose(T.NT[:], T.NX[:]), us(256)), r=["NX"], w=["NT"])
+        op("S", act(T.NP[:], T.NT[:, 0:512].indirect(T.LU[:, 32:48]), AF.Copy, got(256)), r=["NT", "LU2"], w=["NP"])
+        for x, bk in ((0, 6), (1, 4)):
+            part = slice(128 * x, 128 * x + 128)
+            u, n = T["B%d" % bk][:, 0:128], T["B%d" % bk][:, 128:256]
+            names = ["U0", "U1", "U2", "U3"] if bk == 6 else ["mP", "KD1", "KD3"]
+            op("P", mm(sel(u, WE, lambda r, x=x: T.EW[:, 256 * r + 128 * x:256 * r + 128 * x + 128]), 128), r=["EW", "WS6"], w=names + ["~U"], b=[bk])
+            op("V", ts(T.EG[:, part], u, 2048.0, 2048.0, OP.is_ge, OP.mult, c=us(128)), r=names, w=["EG%d" % x], b=[bk])
+            op("V", tt(T.EF[:, part], u, T.EG[:, part], OP.subtract, us(128)), r=names + ["EG%d" % x], w=["EF%d" % x], b=[bk])
+            sg = T.SG[:, 768 + 128 * x:896 + 128 * x]
+            op("S", act(sg, u, AF.Sign, us(128), bias=lim), r=names, w=["SGx%d" % x], b=[bk])
+            op("P", mm([(n, T.ID[:], T.NP[:, part]), (n, T.IH[:], T.ONE[:, 0:128]), (n, T.IH[:], sg)], 128),
+               r=["NP", "ID", "IH", "ONE", "SGx%d" % x], w=["nx%d" % x], b=[bk])
+            op("S", act(T.NF[:, part], n, AF.Copy, us(128)), r=["nx%d" % x], w=["NF%d" % x], b=[bk])
+        dma("Y", [(T.ye[:], T.EF[:])], "oe", r=["EF0", "EF1"])
+        dma("S", [(T.yn[:], T.NF[:])], "on", r=["NF0", "NF1"])
 
-    def list_1(t):
-        out, bk, name = u_rest(t)
-        op("V", cp(T.EU[:, 64:256], out), r=[name], w=["EU1"], b=[bk])
-
-    def signs(t):
-        out, bk, name = u_rest(t)
-        lim = 0.5 - (2048 + 384 * t)
-        op("S", act(T.SG[:, 256 * t:256 * t + 64], T.B6[:, 0:64], AF.Sign, bias=lim), r=["U0"], w=["SGa"], b=[6])
-        op("S", act(T.SG[:, 256 * t + 64:256 * t + 256], out, AF.Sign, bias=lim), r=[name, "SGa"], w=["SG%d" % t], b=[bk])
-
-    def F(fn, *a):
-        return lambda: fn(*a)
-
-    def early(t):
-        exits(t, {0: [F(x_1, t)], 1: [F(x_2, t)], 2: [F(x_3, t), F(x_get, t), F(c_max, t), F(c_new, t)],
-                  4: [F(y_a, t + 1)], 5: [F(y_b, t + 1), F(y_c1, t + 1)], 7: [F(y_c2, t + 1)], 8: [neighbours_d] if t == 0 else []})
-        y_c3(t + 1)
-        c_prep(t + 1)
-        penalty(t)
-
-    def late(t):
-        rest = {4: [F(list_1, t - 1), F(signs, t - 1)] + hs_(t, 2, 3, 4, 5, 6, 7) + hv_(t, 0), 5: hv_(t, 1)}
-        if t == R - 1:
-            d_phase(t, {0: [F(places, t - 1)], 3: [F(take_exits, t - 1), F(take_rest, t - 1)]})
-            return {0: [F(list_0, t - 1), F(pool_in, t - 1)] + hs_(t, 0), 3: hs_(t, 1), **rest}
-        d_phase(t, {0: [F(places, t - 1)], 1: [F(take_exits, t - 1)], 2: [F(list_0, t - 1), F(pool_in, t - 1)],
-                    3: [F(take_rest, t - 1)] + hs_(t, 0, 1)})
-        return rest
-
-    def hs_(t, *ks):
-        return [F(h_get, t, k) for k in ks]
-
-    def hv_(t, *ks):
-        return [F(h_max, t, k) for k in ks]
-
-    consts_choice()
-    op("V", cp(T.EU[:], T.EI[:]), r=["EI"], w=["EU0", "EU1"])
-    consts_exits()
-    c_prep(0)
-    y_a(0)
-    h_get(0, 0)
-    y_b(0)
-    y_c1(0)
-    neighbours_a()
-    h_get(0, 1)
-    y_c2(0)
-    h_get(0, 2)
-    h_max(0, 0)
-    h_get(0, 3)
-    y_c3(0)
-    h_max(0, 1)
-    neighbours_b()
-    h_max(0, 2)
-    h_get(0, 4)
-    h_max(0, 3)
-    h_get(0, 5)
-    neighbours_c()
-    h_max(0, 4)
-    flux(0)
-    h_get(0, 6)
-    y_d(0)
-    h_max(0, 5)
-    h_get(0, 7)
-    h_max(0, 6)
-    h_max(0, 7)
-    d_phase(0, {0: [F(choice_a, 0), F(choice_b, 0)], 1: [F(choice_c, 0)], 2: [F(choice_d, 0)], 3: [F(c_bounds, 0), F(slots_ready, 0)]})
-    early(0)
-    slots_ready(1)
-    c_bounds(1)
-    entries_0()
-    y_d(1)
-    exits(1, {**late(1), 7: hv_(1, 2, 3) + [F(flux, 1), F(h_sum, 1, 2)], 8: [F(h_sum, 1, 3)] + hv_(1, 4, 5)})
-    h_max(1, 6)
-    h_max(1, 7)
-    choice_a(1)
-    penalty(1)
-    places(1)
-    choice_b(1)
-    choice_c(1)
-    choice_d(1)
-    x_1(1)
-    x_2(1)
-    x_3(1)
-    x_get(1)
-    c_max(1)
-    y_a(2)
-    c_new(1)
-    c_prep(2)
-    y_b(2)
-    y_c1(2)
-    y_c2(2)
-    take_exits(1)
-    take_rest(1)
-    y_c3(2)
-    list_0(1)
-    pool_in(1)
-    h_get(2, 0)
-    h_get(2, 1)
-    list_1(1)
-    signs(1)
-    for k in H_BY_VECTOR[2]:
-        h_get(2, k)
-    for k in range(8):
-        if k > 1 and k not in H_BY_VECTOR[2]:
-            h_get(2, k)
-        h_max(2, k)
-        if k == 2:
-            y_d(2)
-    flux(2)
-    d_phase(2, {0: [F(choice_a, 2), F(choice_b, 2)], 1: [F(choice_c, 2)], 2: [F(choice_d, 2)], 3: [F(c_bounds, 2), F(slots_ready, 2)]})
-    early(2)
-    y_d(3)
-    slots_ready(3)
-    c_bounds(3)
-    exits(3, {**late(3), 7: [F(flux, 3), F(h_sum, 3, 1)], 8: hv_(3, 2)})
-    h_sum(3, 2)
-    h_max(3, 3)
-    h_sum(3, 3)
-    for k in range(4, 8):
-        h_max(3, k)
-    places(3)
-    choice_a(3)
-    op("V", lambda: V.memset(T.KN[:], float(3 + R - 1)), w=["KN"])
-    t = R - 1
-    choice_b(3)
-    choice_c(3)
-    choice_d(3)
-    x_1(3)
-    x_2(3)
-    x_3(3)
-    x_get(3)
-    take_exits(t)
-    take_rest(t)
-    op("S", act(T.XO[:], T.XB[:, 0:512].indirect(T.LU[:, 96:128]), AF.Copy), r=["X", "LU3"], w=["XO"])
-    dma("Y", [(T.yx[:], T.XO[:])], "ox", r=["XO"])
-    c_max(3)
-    c_new(3)
+    for t in range(R):
+        jump(t)
+        flux(t)
+        for part in (neighbours, entries) if CFG["FOLD"][t] else (entries, neighbours):
+            part(t)
+        choice(t)
+        bounds(t)
+        move(t)
+        exits(t)
+        arrivals(t)
+    dma("Y", [(T.yx[:], T.XB[:])], "ox", r=["X"])
+    dma("Y", [(T.yc[:], T.HW0[:, 4096:4608])], "oc", r=["C0"])
     dma("Y", [(T.yz[:, 1152:1536], T.ZW[:, 3200:3584])], "oz1", r=["L3"])
-    op("V", ts(T.EG[:, 0:64], T.B6[:, 0:64], 2048.0, 2048.0, OP.is_ge, OP.mult), r=["U0"], w=["EGa"], b=[6])
-    op("V", tt(T.EF[:, 0:64], T.B6[:, 0:64], T.EG[:, 0:64], OP.subtract), r=["U0", "EGa"], w=["EFa"], b=[6])
-    dma("Y", [(T.ye[:, 512 * k:512 * k + 512], T.EF[:, 32 * k:32 * k + 32]) for k in range(2)], "oe", r=["EFa"], total=128)
-    signs(t)
-    flux(R)
-    op("V", ts(T.EG[:, 64:256], T.B3[:, 256:448], 2048.0, 2048.0, OP.is_ge, OP.mult), r=["pf"], w=["EGb"], b=[3])
-    op("V", tt(T.EF[:, 64:256], T.B3[:, 256:448], T.EG[:, 64:256], OP.subtract), r=["pf", "EGb"], w=["EFb"], b=[3])
-    dma("Y", [(T.ye[:, 512 * k:512 * k + 512], T.EF[:, 32 * k:32 * k + 32]) for k in range(2, 8)], "oe", r=["EFb"])
-    op("V", cp(T.CO[:], T.HW0[:, 4096:4608].indirect(T.LU[:, 96:128])), r=["C0", "LU3"], w=["CO"])
-    op("S", act(T.NF[:], T.B6[:, 256:512], AF.Copy), r=["n"], w=["NF"], b=[6])
-    dma("S", [(T.yn[:, 512 * k:512 * k + 512], T.NF[:, 32 * k:32 * k + 32]) for k in range(8)], "on", r=["NF"])
-    dma("Y", [(T.yc[:], T.CO[:])], "oc", r=["CO"])
+
+    if "order" not in ORDER:
+        ORDER["order"] = order_calls(calls)
+    for i in ORDER["order"]:
+        issue(calls[i])
     for sem, val in count.items():
         if known["G"].get(sem, 0) < val:
             g.wait_ge(T.sem[sem], val)

@@ -4,13 +4,14 @@ from concourse.mybir import AluOpType as OP, ActivationFunctionType as AF
 R = 4
 BF, F32, I32, U16 = "bfloat16", "float32", "int32", "uint16"
 CFG = {
-    "D": ["CCRC", "CCAC", "CCRC", "CCAC"],
-    "H": ["SSSSSSSS", "SSSSSSEE", "SSSVSSSV", "SSSSSSEE"], "CUTS": [0, 1, 2, 4],
-    "CASES": [(1.0, 1.0, 1.0), (1.3, 1.0, 1.2), (1.0, 1.5, 1.15), (0.9, 0.8, 0.88)], "SEED": 1,
+    "D": ["ACAC", "CACA", "ACAC", "CACA"], "PUT": (1, 1),
+    "H": ["SVSSSVSS", "SSSSSSSS", "SVSSVSSS", "SSSSSSSS"], "CUTS": [0, 1, 2, 4],
+    "CASES": [((1.0, 1.0, 1.0, 1.0), 1.0, 1.0), ((1.4, 1.75, 2.0, 1.0), 1.1, 1.45), ((1.2, 0.9, 1.5, 1.0), 1.4, 1.25), ((1.2, 1.45, 0.7, 1.0), 0.9, 1.15)], "SEED": 1,
     "FOLD": [False, True, False, True],
     "JV": [False, False, False, False],
     "XM": ["direct"] * 4, "XY": ["exits"] * 4,
-    "LC": 8.7, "LC0": 14.3, "exits": 5.5, "direct": 4.2, "HOP": 0.08, "ROUNDS": 1000, "CP": "S", "CM": "S",
+    "XC": ["there"] * 4, "XD": ["exits"] * 4, "XE": ["direct"] * 4, "SPLIT": [[192, 256], [256, 512], [256, 512], [256, 512]],
+    "Lc1": 6.8, "Ld1": 6.8, "Ld0": 7.5, "Le0": 7.0, "LC0": 11.0, "exits": 5.5, "direct": 4.2, "HOP": 0.08, "ROUNDS": 5000, "TICK": 0.02, "PLAN": (1.0, 1.0, 1.0, 1.0), "SLACK": 0.3, "WHOLE": 0.4, "CP": "G", "CM": "P", "Z": "V",
 }
 
 SCRATCH = {
@@ -22,7 +23,7 @@ SCRATCH = {
     "OA": ("sbuf", [128, 512], BF), "CM": ("sbuf", [128, 512], BF), "TM": ("sbuf", [128, 512], BF), "MS": ("sbuf", [128, 512], BF),
     "ONE": ("sbuf", [128, 512], BF),
     "SB": ("sbuf", [128, 896], BF), "YS": ("sbuf", [128, 1536], BF), "VT": ("sbuf", [128, 1536], BF), "VB": ("sbuf", [128, 384], BF),
-    "P1": ("sbuf", [128, 384], BF), "P2": ("sbuf", [128, 384], BF), "S48": ("sbuf", [128, 384], BF),
+    "P1": ("sbuf", [128, 384], BF), "P2": ("sbuf", [128, 384], BF), "S48": ("sbuf", [128, 384], BF), "SE": ("sbuf", [128, 384], BF),
     "META": ("sbuf", [128, 128], U16), "LM": ("sbuf", [128, 128], U16),
     "NBI": ("sbuf", [128, 256], I32), "NX": ("sbuf", [128, 512], BF), "NT": ("sbuf", [128, 512], BF),
     "N1": ("sbuf", [128, 256], I32), "N2": ("sbuf", [128, 256], I32), "N3": ("sbuf", [128, 256], I32),
@@ -39,7 +40,7 @@ SCRATCH = {
     "COL": ("sbuf", [128, 144], F32), "PI": ("sbuf", [128, 8], I32), "PF": ("sbuf", [128, 24], F32),
     "WS": ("sbuf", [128, 10 * 144], BF), "ID": ("sbuf", [128, 128], BF), "NID": ("sbuf", [128, 128], BF), "IH": ("sbuf", [128, 128], BF),
     "I512": ("sbuf", [128, 128], BF), "I16": ("sbuf", [128, 128], BF), "I32": ("sbuf", [128, 128], F32), "IS": ("sbuf", [128, 128], F32),
-    "ZID": ("sbuf", [128, 128], BF), "GRP": ("sbuf", [128, 128], BF), "NUP": ("sbuf", [128, 128], BF),
+    "GRP": ("sbuf", [128, 128], BF), "NUP": ("sbuf", [128, 128], BF),
     "TA": ("sbuf", [128, 128], BF), "TB": ("sbuf", [128, 128], BF), "TC": ("sbuf", [128, 128], BF),
     "LI": ("sbuf", [128, 32], I32), "LJ": ("sbuf", [128, 32], I32), "LU": ("sbuf", [128, 96], U16),
     "EX": ("sbuf", [128, 512], F32), "ET": ("sbuf", [128, 512], F32),
@@ -49,7 +50,7 @@ SCRATCH = {
     "B4": ("psum", [128, 512], F32), "B5": ("psum", [128, 512], F32), "B6": ("psum", [128, 512], F32), "B7": ("psum", [128, 512], F32),
 }
 SEMAPHORES = (["qV", "qS", "qP", "qG", "lcen", "lent", "lown", "lpl", "lwk", "ljt", "lnb", "dew", "dmt", "oz0", "oz1", "oc", "ox", "oe", "on"]
-              + ["%s%s%d" % (a, k, t) for a in "lah" for k in "cmy" for t in range(R)])
+              + ["%s%s%d" % (a, k, t) for a in "lah" for k in "cdemy" for t in range(R)])
 ORDER = {}
 
 
@@ -68,7 +69,7 @@ def deal(engs, n):
 
 
 def plans(T, topo):
-    out = {"first": [], "later": [], "exits": [], "direct": []}
+    out = {"first": [], "later": [], "exits": [], "direct": [], "there": []}
     for c in T.cores:
         mate, plane, far = [], [], []
         for o, d in enumerate(T.cores):
@@ -85,6 +86,7 @@ def plans(T, topo):
         out["first"].append(([], {**two, here: mate + plane[:1], plain: plane[1:]}))
         out["direct"].append((mate + plane + far, {}))
         out["exits"].append(([], {here: mate + far, plain: plane}))
+        out["there"].append(([], {there[0]: mate + far[:1] + plane[:2], there[1]: far[1:] + plane[2:]}))
     return out
 
 
@@ -124,9 +126,9 @@ def dst(topo, c):
 
 
 def pieces(T, kind, t):
-    if kind == "c":
-        ca = T["CA%d" % t]
-        return None, None, lambda q: ca[:, 512 * q:512 * q + 512]
+    if kind in "cde":
+        ca, (a, z) = T["CA%d" % t], columns(kind, t)
+        return None, None, lambda q: ca[:, 512 * q + a:512 * q + z]
     if kind == "m":
         return (T.META[:, 32 * t:32 * t + 24], lambda o: T.META[:, 32 * t + 3 * o:32 * t + 3 * o + 3],
                 lambda q: T.LM[:, 32 * t + 3 * q:32 * t + 3 * q + 3])
@@ -135,93 +137,98 @@ def pieces(T, kind, t):
             lambda q: T.ZW[:, base + 48 * q:base + 48 * q + 48])
 
 
+def columns(kind, t):
+    cuts = [0] + CFG["SPLIT"][t] + [512]
+    return cuts["cde".index(kind)], cuts["cde".index(kind) + 1]
+
+
 def exchange(kind, t):
-    if kind == "c":
-        return "first" if t == 0 else "later", False
+    if kind in "cde":
+        return CFG["X" + kind.upper()][t], False
     return CFG["XM" if kind == "m" else "XY"][t], True
 
 
 def helper_program(g, core, T, topo, pl):
     ends = []
+    turns = [(kind, 0) for kind in "cde"]
     for t in range(R):
-        for kind in "cmy":
-            name, keep = exchange(kind, t)
-            for q in range(len(T.cores)):
-                far = pl[name][q][1].get(core)
-                if not far:
-                    continue
-                whole, part, land = pieces(T, kind, t)
-                ms = helper_masks(T, topo, core, far)
-                g.wait_ge(T.sem["h%s%d" % (kind, t)], counts(T, topo, pl[name], keep)[1][core])
-                g.remote_dma_fused([RemoteDMATransfer(dst_ids=[dst(topo, T.cores[o])], dma_engine_mask=bits(m), remote_sem=T.sem["a%s%d" % (kind, t)],
-                                                      src=part(o) if part else land(q), dst=land(q)) for o, m in zip(far, ms)],
-                                   local_sem=T.sem["l%s%d" % (kind, t)])
-                ends.append(("l%s%d" % (kind, t), sum(len(m) for m in ms)))
+        centres, exits = [(kind, t + 1) for kind in "cde" if t + 1 < R], [("m", t), ("y", t)]
+        turns += exits + centres if CFG["FOLD"][t] else centres + exits
+    for kind, t in turns:
+        name, keep = exchange(kind, t)
+        for q in range(len(T.cores)):
+            far = pl[name][q][1].get(core)
+            if not far or (kind in "cde" and columns(kind, t)[0] == columns(kind, t)[1]):
+                continue
+            whole, part, land = pieces(T, kind, t)
+            ms = helper_masks(T, topo, core, far)
+            g.wait_ge(T.sem["h%s%d" % (kind, t)], counts(T, topo, pl[name], keep)[1][core])
+            g.remote_dma_fused([RemoteDMATransfer(dst_ids=[dst(topo, T.cores[o])], dma_engine_mask=bits(m), remote_sem=T.sem["a%s%d" % (kind, t)],
+                                                  src=part(o) if part else land(q), dst=land(q)) for o, m in zip(far, ms)],
+                               local_sem=T.sem["l%s%d" % (kind, t)])
+            ends.append(("l%s%d" % (kind, t), sum(len(m) for m in ms)))
     for sem, n in ends:
         g.wait_ge(T.sem[sem], n)
 
 
 def place_calls(calls, before, rank, free):
-    hop = CFG["HOP"]
-    start, lines = [None] * len(calls), {}
-
-    def first_after(line, s):
-        lo, hi = 0, len(line)
-        while lo < hi:
-            mid = (lo + hi) // 2
-            if line[mid][1] <= s:
-                lo = mid + 1
-            else:
-                hi = mid
-        return lo
+    hop = ticks(CFG["HOP"])
+    start, end, busy, banks = [None] * len(calls), [0] * len(calls), {}, [{} for _ in range(8)]
 
     def place(i):
-        e, c, s = calls[i]["e"], calls[i]["c"], free[i]
-        for p, delay in before[i].items():
+        e, c, b = calls[i]
+        s = free[i]
+        for p, delay in before[i]:
             if start[p] is None:
                 place(p)
-            s = max(s, start[p] + calls[p]["c"] + delay)
+            if end[p] + delay > s:
+                s = end[p] + delay
         if e is not None:
-            mine = [lines.setdefault(x, []) for x in (e,) + calls[i]["b"]]
-            moved = True
-            while moved:
-                moved = False
-                for n, line in enumerate(mine):
-                    j = first_after(line, s - hop)
-                    while j < len(line) and line[j][0] - hop < s + c:
-                        a, z, ee = line[j]
-                        gap = 0.0 if n == 0 or ee == e else hop
-                        if a - gap < s + c - 1e-9 and z + gap > s + 1e-9:
-                            s, moved = z + gap, True
-                        j += 1
-            for line in mine:
-                line.insert(first_after(line, s), (s, s + c, e))
-        start[i] = s
+            taken = busy.get(e, 0)
+            for x in b:
+                for ee, mask in banks[x].items():
+                    if ee != e:
+                        taken |= mask
+            taken >>= s
+            k = 1
+            while k < c and taken:
+                step = min(k, c - k)
+                taken |= taken >> step
+                k += step
+            s += (~taken & (taken + 1)).bit_length() - 1
+            busy[e] = busy.get(e, 0) | ((1 << c) - 1) << s
+            for x in b:
+                banks[x][e] = banks[x].get(e, 0) | ((1 << c + 2 * hop) - 1) << s >> hop
+        start[i], end[i] = s, s + c
     for i in rank:
         if start[i] is None:
             place(i)
     return start
 
 
-def replay(calls, before, order, work, wire):
+def ticks(t):
+    return int(t / CFG["TICK"] + 0.999)
+
+
+def replay(case, order):
     hop = CFG["HOP"]
-    end, queue, bank, last = [0.0] * len(calls), {}, {}, 0.0
+    end, queue, banks = [0.0] * len(case), {}, [{} for _ in range(8)]
     for i in order:
-        k = calls[i]
-        s = queue.get(k["e"], 0.0)
-        for p, delay in before[i].items():
-            s = max(s, end[p] + (delay * wire if calls[p]["e"] is None else delay))
-        for x in k["b"]:
-            for e, z in bank.setdefault(x, {}).items():
-                if e != k["e"]:
-                    s = max(s, z + hop)
-        end[i] = s + k["c"] * (work if k["e"] in ("V", "S", "P") else 1.0)
-        if k["e"] is not None:
-            queue[k["e"]] = end[i]
-        for x in k["b"]:
-            bank[x][k["e"]] = end[i]
-        last = max(last, end[i] + k["lat"])
-    return last
+        e, c, b, before = case[i]
+        s = queue.get(e, 0.0)
+        for p, delay in before:
+            if end[p] + delay > s:
+                s = end[p] + delay
+        for x in b:
+            for ee, z in banks[x].items():
+                if ee != e and z + hop > s:
+                    s = z + hop
+        end[i] = s = s + c
+        for x in b:
+            banks[x][e] = s
+        if e is not None:
+            queue[e] = s
+    return end
 
 
 def order_calls(calls):
@@ -239,19 +246,34 @@ def order_calls(calls):
         for x in k["w"]:
             wr[x] = i
             rd[x] = []
+    above = [0] * n
+    for i in range(n):
+        for p in before[i]:
+            above[i] |= above[p] | 1 << p
+        for p in [p for p, d in before[i].items() if d <= CFG["HOP"] and any(above[x] >> p & 1 and before[i][x] >= d for x in before[i])]:
+            del before[i][p], after[p][i]
     way = [0.0] * n
     for i in range(n - 1, -1, -1):
         way[i] = calls[i]["c"] + max([way[j] + d for j, d in after[i].items()] + [calls[i]["lat"]])
-    tails = [0.0 if after[i] else k["lat"] for i, k in enumerate(calls)]
+    last = [i for i in range(n) if not after[i]]
+    tails = [0 if after[i] else ticks(k["lat"]) for i, k in enumerate(calls)]
+    plain = [(k["e"], ticks(k["c"] * CFG["PLAN"][k["kind"]]), k["b"]) for k in calls]
+    ahead, behind = ([[(p, ticks(d)) for p, d in x.items()] for x in side] for side in (before, after))
+    cases = [[(k["e"], k["c"] * work[k["kind"]], k["b"], [(p, d * wire if calls[p]["e"] is None else d) for p, d in before[i].items()])
+              for i, k in enumerate(calls)] for work, wire, _ in CFG["CASES"]]
 
     def forward(urgency):
-        start = place_calls(calls, before, sorted(range(n), key=lambda i: (-urgency[i], i)), [0.0] * n)
-        order = sorted(range(n), key=lambda i: (start[i], i))
-        return sum(replay(calls, before, order, a, b) / c for a, b, c in CFG["CASES"]) / len(CFG["CASES"]), urgency, start, order
+        start = place_calls(plain, ahead, sorted(range(n), key=lambda i: -urgency[i]), [0] * n)
+        order = sorted(range(n), key=lambda i: start[i])
+        value = 0.0
+        for case, (_, _, scale) in zip(cases, CFG["CASES"]):
+            end = replay(case, order)
+            value += max(end[i] + calls[i]["lat"] for i in last) / scale / len(cases)
+        return value, urgency, [s * CFG["TICK"] for s in start], order
 
     def backward(start):
-        back = place_calls(calls, after, sorted(range(n), key=lambda i: (-start[i] - calls[i]["c"], -i)), tails)
-        return [back[i] + calls[i]["c"] for i in range(n)]
+        back = place_calls(plain, behind, sorted(range(n - 1, -1, -1), key=lambda i: -start[i] - plain[i][1] * CFG["TICK"]), tails)
+        return [(back[i] + plain[i][1]) * CFG["TICK"] for i in range(n)]
     state = [CFG["SEED"]]
 
     def draw():
@@ -261,12 +283,18 @@ def order_calls(calls):
     for turn in range(CFG["ROUNDS"]):
         urgency = backward(now[2]) if turn % 3 == 2 else now[1]
         a, width, size = draw() * max(now[2]), 3.0 * 10.0 ** draw(), 0.3 * 20.0 ** draw()
-        new = forward([urgency[i] + size * (2 * draw() - 1) if a <= now[2][i] < a + width and draw() < 0.3 else urgency[i] for i in range(n)])
-        if new[0] <= now[0] + 0.15 * draw():
+        if draw() < CFG["WHOLE"]:
+            i0 = int(draw() * n)
+            shift = size * (2 * draw() - 1)
+            new = forward([urgency[i] + shift if calls[i]["part"] == calls[i0]["part"] and i >= i0 - 40 * draw() else urgency[i] for i in range(n)])
+        else:
+            new = forward([urgency[i] + size * (2 * draw() - 1) if a <= now[2][i] < a + width and draw() < 0.3 else urgency[i] for i in range(n)])
+        if new[0] <= now[0] + CFG["SLACK"] * (1.0 - turn / CFG["ROUNDS"]) * draw():
             now = new
         if new[0] < best[0]:
             best = new
-    ORDER["plan"] = (best[0], [(k["e"], best[2][i], k["c"], (k["w"] + k["r"])[0]) for i, k in enumerate(calls)])
+    end = replay(cases[0], best[3])
+    ORDER["plan"] = (best[0], [(k["e"], end[i] - k["c"], k["c"], (k["w"] + k["r"])[0]) for i, k in enumerate(calls)])
     return best[3]
 
 
@@ -280,7 +308,7 @@ def rank_program(g, core, T, topo):
     V, S, PE = g.vector, g.scalar, g.tensor
     known = {e: {} for e in Q}
     count, wr, rd, bank = {}, {}, {}, {}
-    calls = []
+    calls, stage = [], [0]
 
     def need(e, tok):
         sem, val, clock = tok
@@ -324,7 +352,8 @@ def rank_program(g, core, T, topo):
             bank.setdefault(x, {})[e] = tok
 
     def op(e, fc, r=(), w=(), b=(), sem=None, inc=1, total=None, lat=0.0):
-        calls.append(dict(e=e, fn=fc[0], c=fc[1], r=list(r), w=list(w), b=tuple(b), sem=sem, inc=inc, total=total, lat=lat))
+        c, kind = fc[1] if isinstance(fc[1], tuple) else (fc[1], 3 if sem else 0)
+        calls.append(dict(e=e, fn=fc[0], c=c, kind=kind, part=stage[0], r=list(r), w=list(w), b=tuple(b), sem=sem, inc=inc, total=total, lat=lat))
 
     def dma(e, pairs, sem, r=(), w=(), total=None, lat=2.0):
         def fn():
@@ -338,10 +367,10 @@ def rank_program(g, core, T, topo):
         return max(n, 64) * CYC
 
     def got(n):
-        return 0.06 + 1.56 * n * CYC
+        return 0.06 + 1.56 * n * CYC, 1
 
     def put(n):
-        return 0.05 + 3.8 * n * CYC
+        return 0.05 + 3.8 * n * CYC, 2
 
     def ts(out, in0, s1, s2, o0, o1=None, c=us(0)):
         if o1 is None:
@@ -378,6 +407,9 @@ def rank_program(g, core, T, topo):
     def iota(out, pat, base, name, n, ch=0):
         op("G", (lambda: g.iota(out, pat, base, ch, allow_small_or_imprecise_dtypes=True), 0.13 + 2 * n * CYC), w=[name])
 
+    def pass_on(out, a, n):
+        return lambda: g.affine_select(out, a, [[0, n]], OP.is_ge, 0.0, 0, 0), 0.17 + 2 * n * CYC
+
     def wf(j):
         return T.WF[:, 32 * j:32 * j + 32]
 
@@ -403,9 +435,9 @@ def rank_program(g, core, T, topo):
                                 src=src if part is None else part(o), dst=land(q)) for o, m in zip(near, m1)]
         tr += [RemoteDMATransfer(dst_ids=[dst(topo, h)], dma_engine_mask=bits(m), remote_sem=T.sem[h_], src=src if part is None else whole,
                                  dst=land(q) if part is None else whole) for h, m in zip(hs, m2)]
-        chain = ["~c"] if kind == "c" else ["~x"]
+        chain = ["~" + kind] + ["~h%d" % i for i, h in enumerate(topo.cores_of(core)) if h in hs]
         first = kind == "c" and t == 0
-        op("G", (lambda: g.remote_dma_fused(tr, local_sem=T.sem[l]), 3.5 if first else 0.45), r=[name], w=chain + ["~s" + a] + (["~x"] if first else []),
+        op("G", (lambda: g.remote_dma_fused(tr, local_sem=T.sem[l]), 3.5 if first else 0.45), r=[name], w=chain + ["~s" + a] + (["~0"] if kind in "cde" and t == 0 else []),
            sem=l, inc=sum(len(m) for m in m1 + m2))
         total = counts(T, topo, pl[plan], keep)[0][q]
         got_ = ["~s" + a]
@@ -413,17 +445,24 @@ def rank_program(g, core, T, topo):
             total += 16
             dma("Y", [(land(q), part(q))], a, r=[name], w=["~o" + a], total=total)
             got_.append("~o" + a)
-        op(None, (None, 0.0), r=got_, w=[landed], sem=a, total=total, lat=(CFG["LC0"] - 3.5 if first else CFG["LC"] if kind == "c" else CFG[plan]) - 0.45)
+        op(None, (None, 0.0), r=got_, w=[landed], sem=a, total=total, lat=(CFG["LC0"] - 3.05 if first else CFG["L" + kind + str(min(t, 1))] if kind in "cde" else CFG[plan]) - 0.45)
+
+    def parts(t):
+        return [(kind,) + columns(kind, t) for kind in "cde" if columns(kind, t)[0] < columns(kind, t)[1]]
+
+    def centre(p):
+        return ["C%dc" % p, "C%dd" % p]
 
     own0 = CA[0][:, 512 * q:512 * q + 512]
     dma("Y", [(own0, T.cen[:])], "lcen", w=["cen", "~ld"])
     dma("Y", [(T.EI[:], T.ent[:])], "lent", w=["EI", "~ld"], lat=2.3)
-    dma("Y", [(T.XB[:], T.wk[:])], "lwk", w=["X", "~ld"], lat=2.6)
+    dma("Y", [(T.XB[:], T.wk[:])], "lwk", w=["Xc", "Xd", "~ld"], lat=2.6)
     dma("Y", [(T.JT[:], T.jmp[:])], "ljt", w=["JT", "~ld"], lat=2.9)
-    dma("Y", [(T.HW0[:, 4096:4608], T.cen[:])], "lown", w=["C0", "~ld"], lat=3.2)
+    dma("Y", [(T.HW0[:, 4096:4608], T.cen[:])], "lown", w=centre(0) + ["~ld"], lat=3.2)
     dma("Y", [(T.ZW[:, 0:2048], T.pl[:])], "lpl", w=["Z", "~ld"], lat=4.4)
     dma("Y", [(T.NBI[:], T.nb[:])], "lnb", w=["NBI", "~ld"], lat=4.7)
-    send("c", 0, "cen", "CA0", src=own0)
+    for kind, a, z in parts(0):
+        send(kind, 0, "cen", "CA0" + kind, src=CA[0][:, 512 * q + a:512 * q + z])
     op("G", (lambda: g.iota(T.PI[:, 0:1], [[0, 1]], 0, 1), 0.13), w=["PI0"])
     iota(T.COL[:], [[1, 144]], 0, "COL", 144)
     op("G", (lambda: g.iota(T.LI[:], [[1, 16], [0, 2]], 0, 0), 0.19), w=["LI"])
@@ -460,7 +499,6 @@ def rank_program(g, core, T, topo):
     for j, s in ((W1, 1.0), (WM2, -2.0), (W8192, 8192.0), (WM4096, -4096.0), (W4096, 4096.0), (WM1, -1.0)):
         weights(j, s)
     op("V", ts(T.LU[:, 32:48], T.COL[:, 0:16], 32.0, pf(3), OP.mult, OP.add), r=["PF0", "COL"], w=["LU2"])
-    op("V", fill(T.ZID[:], 0.0), w=["ZID"])
     op("V", fill(T.ONE[:], 1.0, us(256)), w=["ONE"])
     op("V", fill(T.M8[:], 1.0, us(256)), w=["M8"])
     op("V", fill(T.M32[:], 1.0, us(128)), w=["M32"])
@@ -479,8 +517,8 @@ def rank_program(g, core, T, topo):
     op("V", ts(wf(1), wf(0), 4608.0, None, OP.add), r=["m"], w=["my"])
     weights(WT, pf(15), ["PF15"])
     weights(WY, pf(16), ["PF16"])
-    op("V", tt(T.GRP[:], T.TA[:], T.TB[:], OP.mult, us(256)), r=["TA", "TB"], w=["GRP"])
-    op("V", tt(T.NUP[:], T.TA[:], T.TC[:], OP.mult, us(256)), r=["TA", "TC"], w=["NUP"])
+    op("V", tt(T.GRP[:], T.TA[:], T.TB[:], OP.mult, us(128)), r=["TA", "TB"], w=["GRP"])
+    op("V", tt(T.NUP[:], T.TA[:], T.TC[:], OP.mult, us(128)), r=["TA", "TC"], w=["NUP"])
     op("V", fill(T.HW0[:, 5120:5136], 0.0), w=["zero0"])
     op("V", fill(T.HW1[:, 5120:5136], 0.0), w=["zero1"])
     op("V", cp(T.NL[:], T.NBI[:], us(256)), r=["NBI"], w=["NL"])
@@ -511,55 +549,54 @@ def rank_program(g, core, T, topo):
     op("V", ts(T.PF[:, 20:24], T.COL[:, 0:4], 3.0, 16.0, OP.mult, OP.add), r=["COL"], w=["PF20"])
     op("V", ts(pf(14), pf(5), 128.0, pf(4), OP.mult, OP.add), r=["PF4"], w=["PF14"])
     op("V", ts(pf(13), pf(1), 16.0, None, OP.mult), r=["PF0"], w=["PF13"])
-    op("V", tt(T.VB[:], T.P1[:], T.P2[:], OP.add, us(768)), r=["P1", "P2"], w=["VB"])
+    op("V", tt(T.VB[:], T.P1[:], T.P2[:], OP.add, us(384)), r=["P1", "P2"], w=["VB"])
     op("V", ts(T.PF[:, 20:24], T.PF[:, 20:24], pf(5), None, OP.mult), r=["PF20", "PF4"], w=["PF20"])
     weights(WE, pf(14), ["PF14"])
     op("V", ts(T.LU[:, 0:32], T.LI[:], pf(13), None, OP.add), r=["PF13", "LI"], w=["LU1"])
+    op("S", act(T.SE[:], T.S48[:], AF.Identity, us(384), bias=pf(19), scale=pf(4)), r=["S48", "PF19", "PF4"], w=["SE"])
     for t in range(R):
         op("S", act(T.VT[:, 384 * t:384 * t + 384], T.VB[:], AF.Identity, us(384), bias=pf(20 + t)), r=["VB", "PF20"], w=["VT%d" % t])
 
     def jump(t):
         H, p = HW[t % 2], t % 2
-        C, Y, c_, y_ = H[:, 4096:4608], H[:, 4608:5120], "C%d" % p, "Y%d" % p
-        op("P", mm(sel(T.B7[:, 0:32], WJ, lambda r: T.XB[:, r:512:16])), r=["X", "WS5"], w=["jP"], b=[7])
+        C, Y, c_, y_ = H[:, 4096:4608], H[:, 4608:5120], centre(p), "Y%d" % p
+        op("P", mm(sel(T.B7[:, 0:32], WJ, lambda r: T.XB[:, r:512:16])), r=["Xc", "Xd", "WS5"], w=["jP"], b=[7])
         op("V", cp(wi_(0), T.B7[:, 0:32]), r=["jP"], w=["ji"], b=[7])
         op("V", ts(wi_(1), wi_(0), 511, None, OP.bitwise_and), r=["ji"], w=["ja"])
         op("V", cp(wu(0), wi_(1)), r=["ja"], w=["ju"])
         if CFG["JV"][t]:
-            op("V", tt(T.JG[:], T.JT[:, 0:512].indirect(wu(0)), T.XB[:], OP.subtract, got(512)), r=["JT", "ju", "X"], w=["JG"])
+            op("V", tt(T.JG[:], T.JT[:, 0:512].indirect(wu(0)), T.XB[:], OP.subtract, got(512)), r=["JT", "ju", "Xc", "Xd"], w=["JG"])
             op("S", act(Y, T.JG[:], AF.Abs, us(512)), r=["JG"], w=[y_])
         else:
             op("S", act(T.JG[:], T.JT[:, 0:512].indirect(wu(0)), AF.Copy, got(512)), r=["JT", "ju"], w=["JG"])
-            op("P", mm([(T.B2[:], T.ID[:], T.XB[:]), (T.B2[:], T.NID[:], T.JG[:])], 512), r=["X", "JG", "ID", "NID"], w=["B2"], b=[2])
+            op("P", mm([(T.B2[:], T.ID[:], T.XB[:]), (T.B2[:], T.NID[:], T.JG[:])], 512), r=["Xc", "Xd", "JG", "ID", "NID"], w=["B2"], b=[2])
             op("S", act(Y, T.B2[:], AF.Abs, us(512)), r=["B2"], w=[y_], b=[2])
-        op("P", mm(sel(T.B7[:, 160:224], W1, lambda r: H[:, 4096 + r:5120:16])), r=[c_, y_, "WS0"], w=["SyP"], b=[7])
-        op("P", mm([(T.B2[:], T.ID[:], C), (T.B2[:], T.NID[:], Y)], 512), r=[c_, y_, "ID", "NID"], w=["B2"], b=[2])
+        op("P", mm(sel(T.B7[:, 160:224], W1, lambda r: H[:, 4096 + r:5120:16])), r=c_ + [y_, "WS0"], w=["SyP"], b=[7])
+        op("P", mm([(T.B2[:], T.ID[:], C), (T.B2[:], T.NID[:], Y)], 512), r=c_ + [y_, "ID", "NID"], w=["B2"], b=[2])
         for j in range(2):
             op("S", act(T.SC2[:, 32 * j:32 * j + 32], T.B7[:, 160:192], AF.Copy), r=["SyP"], w=["SC2%d" % j], b=[7])
             op("S", act(T.SY2[:, 32 * j:32 * j + 32], T.B7[:, 192:224], AF.Copy), r=["SyP"], w=["SY2%d" % j], b=[7])
         op("S", act(T.OA[:], T.B2[:], AF.Abs, us(512)), r=["B2"], w=["OA"], b=[2])
         op("P", mm(sel(T.B7[:, 64:96], W4096, lambda r: T.OA[:, r:512:16])), r=["OA", "WS4"], w=["ownP"], b=[7])
         for j in range(2):
-            op("V", ts(T.THR[:, 32 * j:32 * j + 32], T.B7[:, 64:96], pf(12), None, OP.subtract), r=["ownP", "A"], w=["thr%d" % j], b=[7])
+            op("S", act(T.THR[:, 32 * j:32 * j + 32], T.B7[:, 64:96], AF.Identity, bias=pf(12)), r=["ownP", "A"], w=["thr%d" % j], b=[7])
         op("V", cp(wi_(2), T.SY2[:, 0:32]), r=["SY20"], w=["ui"])
         op("V", ts(wi_(3), wi_(2), 63, None, OP.bitwise_and), r=["ui"], w=["ua"])
         op("V", ts(wf(3), wi_(3), 1.0 / 64, None, OP.mult), r=["ua"], w=["u64"])
 
     def bounds(t):
-        C, c_ = HW[t % 2][:, 4096:4608], "C%d" % (t % 2)
-        if CFG["CM"] == "S":
-            op("S", act(T.CM[:], C, AF.Identity, us(512), bias=-1.0), r=[c_], w=["CM"])
+        C, c_ = HW[t % 2][:, 4096:4608], centre(t % 2)
+        if CFG["CM"] == "P":
+            op("P", mm([(T.B1[:], T.ID[:], C), (T.B1[:], T.NID[:], T.ONE[:])], 512), r=c_ + ["ID", "NID", "ONE"], w=["B1"], b=[1])
+        elif CFG["CM"] == "S":
+            op("S", act(T.CM[:], C, AF.Identity, us(512), bias=-1.0), r=c_, w=["CM"])
         else:
-            op("V", ts(T.CM[:], C, -1.0, None, OP.add, c=us(256)), r=[c_], w=["CM"])
-        op("P", mm([(T.B2[:], T.ID[:], C), (T.B2[:], T.ID[:], T.ONE[:])], 512), r=[c_, "ID", "ONE"], w=["B2"], b=[2])
+            op("V", ts(T.CM[:], C, -1.0, None, OP.add, c=us(256)), r=c_, w=["CM"])
+        op("P", mm([(T.B2[:], T.ID[:], C), (T.B2[:], T.ID[:], T.ONE[:])], 512), r=c_ + ["ID", "ONE"], w=["B2"], b=[2])
 
     def entries(t):
         H, p = HW[t % 2], t % 2
-        op("P", mm([(T.B1[:], T.ID[:], H[:, 4096:4608])], 512), r=["C%d" % p, "ID"], w=["B1"], b=[1])
-        op("P", mm([(T.B5[:, 0:256], T.ZID[:], T.M32[:])], 256, stop=False), r=["ZID", "M32"], w=["G", "Go"], b=[5])
         kinds = CFG["H"][t]
-        op("P", mm([(T.B5[:, 64 * c:64 * c + 64], T.I32[:], T.SC2[:]) for c in range(4) if kinds[2 * c] != "E"], 256, start=False, stop=False),
-           r=["SC20", "SC21", "I32", "Go"], w=["Gc"], b=[5])
         for k in range(8):
             c = k // 2
             src = T.ZW[:, 0:2048 + 384 * t].indirect(T.EU[:, 32 * k:32 * k + 32])
@@ -570,31 +607,32 @@ def rank_program(g, core, T, topo):
             else:
                 op("S", act(s_, src, AF.Copy, got(512)), r=dep, w=[sk, "~S"])
             if kinds[k] == "E":
-                op("P", mm([(T.B0[:], T.ID[:], s_), (T.B0[:], T.NID[:], H[:, 4096:4608])], 512), r=[sk, "C%d" % p, "ID", "NID"], w=["B0"], b=[0])
-                op("S", act(mh, T.B0[:], AF.Abs, us(512)), r=["B0"], w=["MH%d" % k], b=[0])
+                op("P", mm([(T.B2[:], T.ID[:], s_), (T.B2[:], T.NID[:], H[:, 4096:4608])], 512), r=centre(p) + [sk, "ID", "NID"], w=["B2"], b=[2])
+                op("S", act(mh, T.B2[:], AF.Abs, us(512)), r=["B2"], w=["MH%d" % k], b=[2])
             else:
-                op("V", tt(mh, s_, T.B1[:], OP.max, us(512)), r=[sk, "B1"], w=["MH%d" % k], b=[1])
+                op("V", tt(mh, s_, H[:, 4096:4608], OP.max, us(512)), r=[sk] + centre(p), w=["MH%d" % k])
             if k % 2:
-                out = T.B5[:, 64 * c:64 * c + 64]
+                bk = 5 * (c % 2)
+                out, free = T["B%d" % bk][:, 64 * c:64 * c + 64], ["G%d" % ((c + 2) % 4)]
+                sc = []
                 if kinds[k] != "E":
-                    op("P", mm(sel(out, W1, lambda r, c=c: H[:, 1024 * c + r:1024 * c + 1024:16]), start=False, stop=False),
-                       r=["Go", "WS0", "s%d_%d" % (p, k - 1), sk], w=["Ga%d" % c], b=[5])
-                op("P", mm(sel(out, WM1 if kinds[k] == "E" else WM2, lambda r, c=c: T.MH[:, 1024 * c + r:1024 * c + 1024:16]), start=False, stop=False),
-                   r=["Go", "WS1", "WS9", "MH%d" % (k - 1), "MH%d" % k], w=["Gb%d" % c], b=[5])
-        op("P", mm([(T.B5[:, 0:64], T.ZID[:], T.M32[:, 0:64])], start=False), r=["Gc"] + ["G%s%d" % (x, c) for x in "ab" for c in range(4)], w=["G"], b=[5])
+                    sc = [(out, T.I32[:], T.SC2[:])]
+                    op("P", mm(sel(out, W1, lambda r, c=c: H[:, 1024 * c + r:1024 * c + 1024:16]), stop=False),
+                       r=["WS0", "s%d_%d" % (p, k - 1), sk] + free, w=["G%d" % c], b=[bk])
+                op("P", mm(sc + sel(out, WM2 if sc else WM1, lambda r, c=c: T.MH[:, 1024 * c + r:1024 * c + 1024:16]), more=192 * len(sc), start=not sc),
+                   r=["WS1", "WS9", "SC20", "SC21", "I32", "MH%d" % (k - 1), "MH%d" % k] + free, w=["G%d" % c], b=[bk])
+                op("S", act(T.RG[:, 64 * c:64 * c + 64], out, AF.Relu, bias=2047.0), r=["G%d" % c], w=["RG%d" % c], b=[bk])
 
     def flux(t):
         n = T.B6[:, 256:512]
-        items = [(n, T.ID[:], T.ONE[:, 0:256])]
-        for u in range(t):
-            items += [(n, T.IH[:], T.ONE[:, 0:256]), (n, T.IH[:], T.SG[:, 256 * u:256 * u + 256])]
+        items = [(n, T.ID[:], T.ONE[:, 0:256])] * (1 + t // 2) + [(n, T.IH[:], T.ONE[:, 0:256])] * (t % 2)
+        items += [(n, T.IH[:], T.SG[:, 256 * u:256 * u + 256]) for u in range(t)]
         op("P", mm(items, 256), r=["IH", "ID", "ONE"] + ["SG%d" % u for u in range(t)], w=["n"], b=[6])
 
     def neighbours(t):
         H, p = HW[t % 2], t % 2
         Y, y_ = H[:, 4608:5120], "Y%d" % p
-        dep = ["CA%d" % t, "NL", "cen" if t == 0 else "CAown"]
-        op("P", mm([(T.B0[:], T.ID[:], Y)], 512), r=[y_, "ID"], w=["B0"], b=[0])
+        dep = ["CA%dc" % t, "CA%dd" % t, "CA%de" % t, "NL", "cen" if t == 0 else "CAown"]
         for c in range(4):
             kind, bk = CFG["D"][t][c], 3 + c % 2
             out = T["B%d" % bk][:, 64 * c:64 * c + 64]
@@ -605,11 +643,11 @@ def rank_program(g, core, T, topo):
                 ag, mx = T.AG[:, 512 * k:512 * k + 512], T.MX[:, 512 * k:512 * k + 512]
                 if kind == "C":
                     op("S", act(ag, src, AF.Copy, got(512)), r=dep, w=["AG%d" % k, "~S"])
-                    op("V", tt(mx, ag, T.B0[:], OP.max, us(512)), r=["AG%d" % k, "B0"], w=["MX%d" % k], b=[0])
+                    op("V", tt(mx, ag, Y, OP.max, us(512)), r=["AG%d" % k, y_], w=["MX%d" % k])
                 elif kind == "E":
                     op("S", act(ag, src, AF.Copy, got(512)), r=dep, w=["AG%d" % k, "~S"])
-                    op("P", mm([(T.B1[:], T.ID[:], ag), (T.B1[:], T.NID[:], Y)], 512), r=["AG%d" % k, y_, "ID", "NID"], w=["B1"], b=[1])
-                    op("S", act(mx, T.B1[:], AF.Abs, us(512)), r=["B1"], w=["MX%d" % k], b=[1])
+                    op("P", mm([(T.B2[:], T.ID[:], ag), (T.B2[:], T.NID[:], Y)], 512), r=["AG%d" % k, y_, "ID", "NID"], w=["B2"], b=[2])
+                    op("S", act(mx, T.B2[:], AF.Abs, us(512)), r=["B2"], w=["MX%d" % k], b=[2])
                 else:
                     op("V", tt(ag, src, Y, OP.subtract, got(512)), r=dep + [y_], w=["AG%d" % k])
                     if kind == "A":
@@ -627,10 +665,9 @@ def rank_program(g, core, T, topo):
         op("V", tt(wi_(4), T.RUN[:, 0:32], T.RUN[:, 32:64], OP.min), r=["RUN"], w=["kz"])
 
     def choice(t):
-        op("S", act(T.RG[:], T.B5[:, 0:256], AF.Relu, us(256), bias=2047.0), r=["G"], w=["RG"], b=[5])
         for k in range(8):
             op("V", tt(T.G2[:, k:256:8], T.RG[:, 32 * k:32 * k + 32], T.B6[:, 256 + 32 * k:288 + 32 * k], OP.mult),
-               r=["RG", "n"], w=["G2_%d" % k], b=[6])
+               r=["RG%d" % (k // 2), "n"], w=["G2_%d" % k], b=[6])
         op("V", scan(T.PP[:], T.M8[:], T.G2[:], us(256)), r=["M8"] + ["G2_%d" % k for k in range(8)], w=["PP"])
         fold = CFG["FOLD"][t]
         if fold:
@@ -648,7 +685,7 @@ def rank_program(g, core, T, topo):
             op("V", cp(wu(2), out), r=["fP"], w=["xu"], b=[7])
         else:
             op("P", mm(items), r=nc, w=["fP"], b=[7])
-            op("V", ts(wf(5), out, -4608.0, None, OP.add), r=["fP"], w=["fz"], b=[7])
+            op("S", act(wf(5), out, AF.Identity, bias=-4608.0), r=["fP"], w=["fz"], b=[7])
             op("V", tt(T.GO[:], wi_(4), T.THR[:, 0:32], OP.is_lt), r=["kz", "thr0"], w=["go"])
             op("V", tt(wf(7), wf(5), T.GO[:], OP.mult), r=["fz", "go"], w=["x1"])
             op("V", tt(wf(9), wf(7), wf(1), OP.add), r=["x1", "my"], w=["x2"])
@@ -657,22 +694,35 @@ def rank_program(g, core, T, topo):
     def move(t):
         p, pn = t % 2, 1 - t % 2
         src = HW[p][:, 0:5120].indirect(wu(2))
-        dep = ["s%d_%d" % (p, k) for k in range(8)] + ["C%d" % p, "Y%d" % p, "xu"]
+        dep = ["s%d_%d" % (p, k) for k in range(8)] + centre(p) + ["Y%d" % p, "xu"]
         new = HW[pn][:, 4096:4608]
-        op("V", tt(T.TM[:], src, T.CM[:], OP.max, got(512)), r=dep + ["CM"], w=["TM"])
-        op("V", tt(new, T.TM[:], T.B2[:], OP.min, us(512)), r=["TM", "B2"], w=["C%d" % pn], b=[2])
-        op("S", act(T.XB[:], src, AF.Copy, got(512)), r=dep, w=["X"])
-        if t < R - 1:
-            send("c", t + 1, "C%d" % pn, "CA%d" % (t + 1), src=new)
-            own = CA[t + 1][:, 512 * q:512 * q + 512]
-            if CFG["CP"] == "S":
-                op("S", act(own, new, AF.Copy, us(512)), r=["C%d" % pn], w=["CAown"])
+        cut = parts(t + 1) if t < R - 1 else [("c", 0, 512)]
+        for kind, a, z in cut:
+            name = centre(pn) if len(cut) == 1 else ["C%d%s" % (pn, kind)]
+            part = HW[pn][:, 4096 + a:4096 + z]
+            chosen = HW[p][:, 0:5120].indirect(T.WU[:, 64 + a // 16:64 + z // 16])
+            if CFG["CM"] == "P":
+                op("S", act(T.XB[:, a:z], chosen, AF.Copy, got(z - a)), r=dep, w=["Xc", "Xd"] if len(cut) == 1 else ["X" + kind])
+                op("V", tt(T.TM[:, a:z], T.XB[:, a:z], T.B1[:, a:z], OP.max, us(z - a)), r=["X" + kind, "B1"], w=["TM" + kind], b=[1])
             else:
-                op("V", cp(own, new, us(256)), r=["C%d" % pn], w=["CAown"])
+                op("V", tt(T.TM[:, a:z], chosen, T.CM[:, a:z], OP.max, got(z - a)), r=dep + ["CM"], w=["TM" + kind])
+            op("V", tt(part, T.TM[:, a:z], T.B2[:, a:z], OP.min, us(z - a)), r=["TM" + kind, "B2"], w=name, b=[2])
+            if t < R - 1:
+                send(kind, t + 1, name[0], "CA%d%s" % (t + 1, kind), src=part)
+        if CFG["CM"] != "P":
+            op("S", act(T.XB[:], src, AF.Copy, got(512)), r=dep, w=["Xc", "Xd"])
+        if t < R - 1:
+            own = CA[t + 1][:, 512 * q:512 * q + 512]
+            if CFG["CP"] == "G":
+                op("G", pass_on(own, new, 512), r=centre(pn) + ["~c", "~d"], w=["CAown"])
+            elif CFG["CP"] == "S":
+                op("S", act(own, new, AF.Copy, us(512)), r=centre(pn), w=["CAown"])
+            else:
+                op("V", cp(own, new, us(256)), r=centre(pn), w=["CAown"])
 
     def exits(t):
         H, p = HW[t % 2], t % 2
-        op("S", act(T.SB[:, 512:896], T.S48[:], AF.Identity, us(384), bias=pf(19), scale=pf(4)), r=["S48", "PF19", "PF4"], w=["SB"])
+        op("G", pass_on(T.SB[:, 512:896], T.SE[:], 384), r=["SE"], w=["SB"])
         op("V", ts(wi_(5), wi_(4), 2055, None, OP.bitwise_and), r=["kz"], w=["og"])
         op("V", ts(wi_(6), wi_(4), 3, 255, OP.arith_shift_right, OP.bitwise_and), r=["kz"], w=["kc"])
         op("V", ts(wu(1), wi_(6), pf(11), None, OP.add), r=["kc", "PF11"], w=["mu"])
@@ -690,7 +740,9 @@ def rank_program(g, core, T, topo):
         op("V", tt(wf(14), wf(13), wf(12), OP.mult), r=["val", "ar"], w=["v2"])
         op("V", tt(wf(15), wf(14), wf(0), OP.max), r=["v2", "m"], w=["v3"])
         op("V", cp(wu(3), wf(15)), r=["v3"], w=["su"])
-        op("V", cp(T.SB[:, 0:896].indirect(wu(3)), T.MS[:], put(512)), r=["MS", "su"], w=["SB"])
+        n = 512 // CFG["PUT"][0]
+        for a in range(0, 512, n):
+            op("V", cp(T.SB[:, 0:896].indirect(T.WU[:, 96 + a // 16:96 + (a + n) // 16]), T.MS[:, a:a + n], put(n)), r=["MS", "su"], w=["SB"])
         op("P", mm(sel(T.B4[:, 0:24], WT, lambda r: T.SB[:, 512 + r:896:16])), r=["SB", "WS7"], w=["mP"], b=[4])
         op("P", mm(sel(T.B3[:, 256:280], WY, lambda r: T.SB[:, 512 + r:896:16])), r=["SB", "WS8"], w=["pf"], b=[3])
         op("V", cp(T.META[:, 32 * t:32 * t + 24], T.B4[:, 0:24]), r=["mP"], w=["META%d" % t], b=[4])
@@ -703,10 +755,13 @@ def rank_program(g, core, T, topo):
             op("P", mm([(T.B7[:, 224:225], T.ONE[:, 0:128], T.INC[:, 31 + 32 * o:32 + 32 * o]) for o in range(8)]), r=["INC", "ONE"], w=["AP"], b=[7])
             op("V", cp(T.PI[:, 4:5], T.B7[:, 224:225]), r=["AP"], w=["Ai"], b=[7])
             op("V", ts(T.PI[:, 5:6], T.PI[:, 4:5], 63, None, OP.bitwise_and), r=["Ai"], w=["Aa"])
-            op("V", ts(pf(12), T.PI[:, 5:6], 4096.0, None, OP.mult), r=["Aa"], w=["A"])
+            op("V", ts(pf(12), T.PI[:, 5:6], -4096.0, None, OP.mult), r=["Aa"], w=["A"])
 
     def arrivals(t):
-        op("V", cp(T.EW[:, 0:4608].indirect(T.LM[:, 32 * t:32 * t + 24]), T.VT[:, 384 * t:384 * t + 384], put(384)), r=["VT%d" % t, "LM%d" % t], w=["EW"])
+        n = 384 // CFG["PUT"][1]
+        for a in range(0, 384, n):
+            op("V", cp(T.EW[:, 0:4608].indirect(T.LM[:, 32 * t + a // 16:32 * t + (a + n) // 16]), T.VT[:, 384 * t + a:384 * t + a + n], put(n)),
+               r=["VT%d" % t, "LM%d" % t], w=["EW"])
         lim = 0.5 - (2048 + 384 * t)
         if t == R - 1:
             return results(lim)
@@ -716,7 +771,8 @@ def rank_program(g, core, T, topo):
             op("P", mm(sel(u, WE, lambda r, a=a, z=z: T.EW[:, 1024 * a + r:1024 * z:16]), 64 * (z - a)), r=["EW", "WS6"], w=us_ + ["~U"], b=[6])
             op("V", cp(T.EU[:, 64 * a:64 * z], u, us(64 * (z - a))), r=us_, w=["EU%d" % c for c in range(a, z)], b=[6])
         op("S", act(T.SG[:, 256 * t:256 * t + 256], T.B6[:, 0:256], AF.Sign, us(256), bias=lim), r=["U%d" % c for c in range(4)], w=["SG%d" % t], b=[6])
-        op("V", cp(T.ZW[:, 384 * t:384 * t + 384], T.ZW[:, 2048 + 384 * t:2048 + 384 * t + 384], us(192)), r=["L%d" % t], w=["Z"])
+        places, landed = T.ZW[:, 384 * t:384 * t + 384], T.ZW[:, 2048 + 384 * t:2048 + 384 * t + 384]
+        op(CFG["Z"], cp(places, landed, us(192)) if CFG["Z"] == "V" else pass_on(places, landed, 384), r=["L%d" % t], w=["Z"])
         if t == R - 2:
             dma("Y", [(T.yz[:, 0:1152], T.ZW[:, 0:1152]), (T.yz[:, 1536:2048], T.ZW[:, 1536:2048])], "oz0", r=["Z"])
 
@@ -741,17 +797,12 @@ def rank_program(g, core, T, topo):
         dma("S", [(T.yn[:], T.NF[:])], "on", r=["NF0", "NF1"])
 
     for t in range(R):
-        jump(t)
-        flux(t)
-        for part in (neighbours, entries) if CFG["FOLD"][t] else (entries, neighbours):
+        middle = (neighbours, exits, entries, choice, bounds, move) if CFG["FOLD"][t] else (entries, neighbours, choice, bounds, move, exits)
+        for part in (jump, flux) + middle + (arrivals,):
+            stage[0] += 1
             part(t)
-        choice(t)
-        bounds(t)
-        move(t)
-        exits(t)
-        arrivals(t)
-    dma("Y", [(T.yx[:], T.XB[:])], "ox", r=["X"])
-    dma("Y", [(T.yc[:], T.HW0[:, 4096:4608])], "oc", r=["C0"])
+    dma("Y", [(T.yx[:], T.XB[:])], "ox", r=["Xc", "Xd"])
+    dma("Y", [(T.yc[:], T.HW0[:, 4096:4608])], "oc", r=centre(0))
     dma("Y", [(T.yz[:, 1152:1536], T.ZW[:, 3200:3584])], "oz1", r=["L3"])
 
     if "order" not in ORDER:

@@ -4,19 +4,21 @@ from concourse.mybir import AluOpType as OP, ActivationFunctionType as AF
 R = 4
 BF, F32, I32, U16 = "bfloat16", "float32", "int32", "uint16"
 CFG = {
-    "D": ["ACAC", "CACA", "ACAC", "CACA"], "PUT": (1, 1),
-    "H": ["SVSSSVSS", "SSSSSSSS", "SVSSVSSS", "SSSSSSSS"], "CUTS": [0, 1, 2, 4],
-    "CASES": [((1.0, 1.0, 1.0, 1.0), 1.0, 1.0), ((1.4, 1.75, 2.0, 1.0), 1.1, 1.45), ((1.2, 0.9, 1.5, 1.0), 1.4, 1.25), ((1.2, 1.45, 0.7, 1.0), 0.9, 1.15)], "SEED": 1,
+    "D": ["CCAACCAA", "CCAACCAA", "CCAACCAA", "CCAACCAA"], "PUT": (1, 1),
+    "H": ["TTVVTTSS", "TTTTTTSS", "VVTTTTSS", "TTTTTTSS"], "CUTS": [0, 1, 2, 4],
+    "MV": "BBBB", "OWN": "VVVV", "OV": "W", "EWZ": "V", "MTZ": 2, "PB": True, "FX": "V", "GD": (2.5, 1.2, 2.3),
+    "CASES": [((0.96, 0.96, 0.96, 1.0, 1.2, 0.96), 1.03, 1.0), ((1.4, 1.75, 2.0, 1.0, 1.6, 1.4), 1.15, 1.45), ((1.2, 0.9, 1.5, 1.0, 1.5, 1.8), 1.4, 1.25),
+              ((1.2, 1.45, 0.7, 1.0, 1.2, 1.8), 0.95, 1.15)], "SEED": 2,
     "FOLD": [False, True, False, True],
     "JV": [False, False, False, False],
-    "XM": ["direct"] * 4, "XY": ["exits"] * 4,
+    "XM": ["direct"] * 4, "XY": ["exits"] * 4, "CUT": [True, True, True, False], "BOTH": ["", "", "", ""], "KEEP0": True,
     "XC": ["there"] * 4, "XD": ["exits"] * 4, "XE": ["direct"] * 4, "SPLIT": [[192, 256], [256, 512], [256, 512], [256, 512]],
-    "Lc1": 6.8, "Ld1": 6.8, "Ld0": 7.5, "Le0": 7.0, "LC0": 11.0, "exits": 5.5, "direct": 4.2, "HOP": 0.08, "ROUNDS": 5000, "TICK": 0.02, "PLAN": (1.0, 1.0, 1.0, 1.0), "SLACK": 0.3, "WHOLE": 0.4, "CP": "G", "CM": "P", "Z": "V",
+    "four": 4.9, "quad": 4.9, "Lc1": 6.8, "Ld1": 6.8, "Ld0": 7.5, "Le0": 7.0, "LC0": 11.0, "exits": 5.5, "direct": 4.2, "HOP": 0.1, "ROUNDS": 800, "MOVES": 1, "LOOKS": 800, "TRIES": 150, "WIDE": 70, "WARM": 0.1, "COLD": 0.1, "SOON": 0.03, "GIVE": 0.05, "MARK": 0.6, "NEAR": 0.5, "EARLY": 0.02, "LAND": 0.0, "FAR": 0.5, "HEAT": 0.3, "SORT": True, "TICK": 0.02, "PLAN": (1.0, 1.0, 1.0, 1.0, 1.2, 1.2), "SLACK": 0.3, "WHOLE": 0.4, "CP": "G", "CM": "V", "Z": "G",
 }
 
 SCRATCH = {
     "CA0": ("sbuf", [128, 4096], BF), "CA1": ("sbuf", [128, 4096], BF), "CA2": ("sbuf", [128, 4096], BF), "CA3": ("sbuf", [128, 4096], BF),
-    "HW0": ("sbuf", [128, 5136], BF), "HW1": ("sbuf", [128, 5136], BF),
+    "HW0": ("sbuf", [128, 5648], BF), "HW1": ("sbuf", [128, 5136], BF),
     "ZW": ("sbuf", [128, 3584], BF), "EW": ("sbuf", [128, 4608], BF), "MT": ("sbuf", [128, 4096], BF),
     "AG": ("sbuf", [128, 4096], BF), "MX": ("sbuf", [128, 4096], BF), "MH": ("sbuf", [128, 4096], BF),
     "JT": ("sbuf", [128, 512], BF), "XB": ("sbuf", [128, 512], BF), "JG": ("sbuf", [128, 512], BF),
@@ -25,31 +27,32 @@ SCRATCH = {
     "SB": ("sbuf", [128, 896], BF), "YS": ("sbuf", [128, 1536], BF), "VT": ("sbuf", [128, 1536], BF), "VB": ("sbuf", [128, 384], BF),
     "P1": ("sbuf", [128, 384], BF), "P2": ("sbuf", [128, 384], BF), "S48": ("sbuf", [128, 384], BF), "SE": ("sbuf", [128, 384], BF),
     "META": ("sbuf", [128, 128], U16), "LM": ("sbuf", [128, 128], U16),
-    "NBI": ("sbuf", [128, 256], I32), "NX": ("sbuf", [128, 512], BF), "NT": ("sbuf", [128, 512], BF),
-    "N1": ("sbuf", [128, 256], I32), "N2": ("sbuf", [128, 256], I32), "N3": ("sbuf", [128, 256], I32),
-    "NQ": ("sbuf", [128, 256], BF), "NP": ("sbuf", [128, 256], BF),
+    "NBI": ("sbuf", [128, 256], I32), "N1": ("sbuf", [128, 256], I32), "NF": ("sbuf", [128, 256], F32),
     "NL": ("sbuf", [128, 256], U16), "EU": ("sbuf", [128, 256], U16),
-    "EI": ("sbuf", [128, 256], I32), "E1": ("sbuf", [128, 256], I32), "E2": ("sbuf", [128, 256], I32),
+    "EI": ("sbuf", [128, 256], I32), "EWF": ("sbuf", [128, 4608], F32), "VF": ("sbuf", [128, 384], F32), "JF": ("sbuf", [128, 384], F32),
     "ELO": ("sbuf", [128, 256], BF), "EHI": ("sbuf", [128, 256], BF),
-    "KHI": ("sbuf", [128, 256], BF), "KLO": ("sbuf", [128, 256], BF), "TLO": ("sbuf", [128, 256], BF), "THI": ("sbuf", [128, 256], BF),
+    "KHI": ("sbuf", [128, 256], BF), "OWN": ("sbuf", [128, 256], BF), "KLO": ("sbuf", [128, 256], BF), "FN": ("sbuf", [128, 256], BF), "TLO": ("sbuf", [128, 256], BF), "THI": ("sbuf", [128, 256], BF),
+    "PM": ("sbuf", [128, 16], F32), "OG": ("sbuf", [128, 64], I32), "OB": ("sbuf", [128, 64], BF),
+    "D0": ("sbuf", [128, 128], BF), "D1": ("sbuf", [128, 128], BF),
     "CT": ("sbuf", [128, 256], BF), "C8": ("sbuf", [128, 256], BF), "KX": ("sbuf", [128, 256], BF), "RT": ("sbuf", [128, 256], BF),
     "M32": ("sbuf", [128, 256], BF), "M8": ("sbuf", [128, 256], F32),
     "SG": ("sbuf", [128, 1024], BF), "RG": ("sbuf", [128, 256], F32), "G2": ("sbuf", [128, 256], F32), "PP": ("sbuf", [128, 256], F32),
     "NC": ("sbuf", [128, 256], BF), "HIT": ("sbuf", [128, 256], BF), "INC": ("sbuf", [128, 256], BF), "PRD": ("sbuf", [128, 256], BF),
-    "EF": ("sbuf", [128, 256], F32), "EG": ("sbuf", [128, 256], F32), "NF": ("sbuf", [128, 256], BF),
+    "EF": ("sbuf", [128, 256], F32), "EG": ("sbuf", [128, 256], F32),
     "COL": ("sbuf", [128, 144], F32), "PI": ("sbuf", [128, 8], I32), "PF": ("sbuf", [128, 24], F32),
     "WS": ("sbuf", [128, 10 * 144], BF), "ID": ("sbuf", [128, 128], BF), "NID": ("sbuf", [128, 128], BF), "IH": ("sbuf", [128, 128], BF),
     "I512": ("sbuf", [128, 128], BF), "I16": ("sbuf", [128, 128], BF), "I32": ("sbuf", [128, 128], F32), "IS": ("sbuf", [128, 128], F32),
     "GRP": ("sbuf", [128, 128], BF), "NUP": ("sbuf", [128, 128], BF),
-    "TA": ("sbuf", [128, 128], BF), "TB": ("sbuf", [128, 128], BF), "TC": ("sbuf", [128, 128], BF),
-    "LI": ("sbuf", [128, 32], I32), "LJ": ("sbuf", [128, 32], I32), "LU": ("sbuf", [128, 96], U16),
+    "TA": ("sbuf", [128, 128], BF), "TB": ("sbuf", [128, 128], BF),
+    "LJ": ("sbuf", [128, 32], I32), "LU": ("sbuf", [128, 96], U16),
     "EX": ("sbuf", [128, 512], F32), "ET": ("sbuf", [128, 512], F32),
-    "WF": ("sbuf", [128, 640], F32), "WI": ("sbuf", [128, 320], I32), "WU": ("sbuf", [128, 160], U16), "GO": ("sbuf", [128, 32], BF),
-    "SY2": ("sbuf", [128, 64], F32), "SC2": ("sbuf", [128, 64], F32), "RUN": ("sbuf", [128, 64], F32), "THR": ("sbuf", [128, 64], F32),
-    "B0": ("psum", [128, 512], F32), "B1": ("psum", [128, 512], F32), "B2": ("psum", [128, 512], F32), "B3": ("psum", [128, 512], F32),
+    "WF": ("sbuf", [128, 640], F32), "WI": ("sbuf", [128, 320], I32), "WU": ("sbuf", [128, 192], U16), "GO": ("sbuf", [128, 64], BF),
+    "UI": ("sbuf", [128, 80], I32), "UF": ("sbuf", [128, 40], F32),
+    "SC2": ("sbuf", [128, 128], F32), "RUN": ("sbuf", [128, 64], F32), "THR": ("sbuf", [128, 64], F32),
+    "B0": ("psum", [128, 512], F32), "B1": ("psum", [128, 1024], BF) if CFG["PB"] else ("psum", [128, 512], F32), "B2": ("psum", [128, 512], F32), "B3": ("psum", [128, 512], F32),
     "B4": ("psum", [128, 512], F32), "B5": ("psum", [128, 512], F32), "B6": ("psum", [128, 512], F32), "B7": ("psum", [128, 512], F32),
 }
-SEMAPHORES = (["qV", "qS", "qP", "qG", "lcen", "lent", "lown", "lpl", "lwk", "ljt", "lnb", "dew", "dmt", "oz0", "oz1", "oc", "ox", "oe", "on"]
+SEMAPHORES = (["qV", "qS", "qP", "qG", "lcen", "lent", "lown", "lpl", "lwk", "ljt", "lnb", "dew", "dmt", "oz0", "oz1", "oc", "ox", "oe", "on", "gn", "gf"]
               + ["%s%s%d" % (a, k, t) for a in "lah" for k in "cdemy" for t in range(R)])
 ORDER = {}
 
@@ -69,7 +72,7 @@ def deal(engs, n):
 
 
 def plans(T, topo):
-    out = {"first": [], "later": [], "exits": [], "direct": [], "there": []}
+    out = {"first": [], "later": [], "exits": [], "direct": [], "there": [], "four": [], "quad": []}
     for c in T.cores:
         mate, plane, far = [], [], []
         for o, d in enumerate(T.cores):
@@ -87,6 +90,10 @@ def plans(T, topo):
         out["direct"].append((mate + plane + far, {}))
         out["exits"].append(([], {here: mate + far, plain: plane}))
         out["there"].append(([], {there[0]: mate + far[:1] + plane[:2], there[1]: far[1:] + plane[2:]}))
+        other = [h for h in free if topo.die(h) != topo.die(c) and h not in there][0]
+        out["four"].append(([], {there[0]: far[:2], here: mate + far[2:], plain: plane[:2], other: plane[2:]}))
+        others = [h for h in free if topo.die(h) != topo.die(c) and h not in there]
+        out["quad"].append(([], {there[0]: far[:2], there[1]: mate + far[2:], others[0]: plane[:2], others[1]: plane[2:]}))
     return out
 
 
@@ -144,8 +151,9 @@ def columns(kind, t):
 
 def exchange(kind, t):
     if kind in "cde":
-        return CFG["X" + kind.upper()][t], False
-    return CFG["XM" if kind == "m" else "XY"][t], True
+        return CFG["X" + kind.upper()][t], t == 0 and CFG["KEEP0"]
+    name = CFG["XM" if kind == "m" else "XY"][t]
+    return name, name not in ("four", "quad")
 
 
 def helper_program(g, core, T, topo, pl):
@@ -293,8 +301,202 @@ def order_calls(calls):
             now = new
         if new[0] < best[0]:
             best = new
+
+    lands = [i for i in range(n) if calls[i]["e"] is None]
+
+    def measure(order, first, old, most=1e9, part=None):
+        hop, queue, banks, links = CFG["HOP"], {}, [{} for _ in range(8)], []
+        for at, i in enumerate(order):
+            e, _, b = plain[i]
+            if at >= first:
+                links.append((i, queue.get(e), [j for x in b for ee, j in banks[x].items() if ee != e]))
+            for x in b:
+                banks[x][e] = i
+            if e is not None:
+                queue[e] = i
+        value, ends, parts = 0.0, [], []
+        for case, (_, _, scale), was in zip(cases, CFG["CASES"], old):
+            if part and value + sum(part[len(parts):]) > most + CFG["GIVE"]:
+                return None
+            end = was[:]
+            for i, j, met in links:
+                s = end[j] if j is not None else 0.0
+                for p, delay in case[i][3]:
+                    if end[p] + delay > s:
+                        s = end[p] + delay
+                for p in met:
+                    if end[p] + hop > s:
+                        s = end[p] + hop
+                end[i] = s + case[i][1]
+            ends.append(end)
+            parts.append((max(end[i] + calls[i]["lat"] for i in last) + CFG["EARLY"] * sum(end) / n + CFG["LAND"] * sum(end[i] for i in lands) / len(lands)) / scale / len(cases))
+            value += parts[-1]
+        return value, order, ends, parts
+
+    def waits(order, case, end):
+        place = {i: at for at, i in enumerate(order)}
+        i, out = max(last, key=lambda j: end[j] + calls[j]["lat"]), []
+        if draw() < CFG["MARK"]:
+            i = lands[int(draw() * len(lands))]
+        while True:
+            s = end[i] - case[i][1]
+            dep = [p for p, delay in case[i][3] if end[p] + delay > s - 1e-9]
+            if dep:
+                i = dep[int(draw() * len(dep))]
+                continue
+            at = place[i] - 1
+            while at >= 0:
+                j = order[at]
+                if end[j] > s - CFG["HOP"] - 1e-9 and (plain[j][0] == plain[i][0] and end[j] > s - 1e-9 or plain[j][0] != plain[i][0] and set(plain[j][2]) & set(plain[i][2])):
+                    break
+                at -= 1
+            if at < 0 or s < 1e-9:
+                return out, place
+            out.append((order[at], i))
+            i = order[at]
+    top = now = measure(best[3], 0, [[0.0] * n for _ in cases])
+    pairs = None
+    for turn in range(CFG["MOVES"]):
+        if pairs is None or turn % 16 == 0:
+            x = int(draw() * len(cases))
+            pairs, place = waits(now[1], cases[x], now[2][x])
+        if not pairs:
+            pairs = None
+            continue
+        j = int(draw() * len(pairs))
+        if draw() < CFG["NEAR"]:
+            j = int(j * draw() * draw())
+        v, u = pairs[j]
+        while draw() < CFG["FAR"] and j + 1 < len(pairs) and pairs[j + 1][1] == v and not above[u] >> pairs[j + 1][0] & 1:
+            j += 1
+            v = pairs[j][0]
+        if above[u] >> v & 1:
+            continue
+        a, z = place[v], place[u] + 1
+        part = now[1][a:z]
+        if draw() < 0.5:
+            moved = [i for i in part if i == u or above[u] >> i & 1]
+            part = moved + [i for i in part if not (i == u or above[u] >> i & 1)]
+        else:
+            moved = [i for i in part if i == v or above[i] >> v & 1]
+            part = [i for i in part if not (i == v or above[i] >> v & 1)] + moved
+        most = now[0] + CFG["HEAT"] * (1.0 - turn / CFG["MOVES"]) * draw()
+        new = measure(now[1][:a] + part + now[1][z:], a, now[2], most, now[3])
+        if new is None:
+            continue
+        if new[0] <= most:
+            now, pairs = new, None
+            if CFG["SORT"]:
+                c0, e0 = cases[0], now[2][0]
+                at = {i: x for x, i in enumerate(now[1])}
+                now = (now[0], sorted(now[1], key=lambda i: (round(e0[i] - c0[i][1], 6), at[i])), now[2], now[3])
+        if new[0] < top[0]:
+            top = new
+    hop = CFG["HOP"]
+    follow = [[[] for _ in calls] for _ in cases]
+    for case, to in zip(cases, follow):
+        for i in range(n):
+            for p, d in case[i][3]:
+                to[p].append((i, d))
+    weight = [1.0 / scale / len(cases) for _, _, scale in CFG["CASES"]]
+
+    def window(order, a, z, heat):
+        inside = order[a:z]
+        local = {i: x for x, i in enumerate(inside)}
+        frame = []
+        for case, to in zip(cases, follow):
+            end = replay(case, order)
+            tail, queue, banks = {}, {}, [{} for _ in range(8)]
+            for i in reversed(order[z:]):
+                e, c, b, _ = case[i]
+                s = max([calls[i]["lat"] if not to[i] else 0.0, queue.get(e, 0.0)] + [d + tail[j] for j, d in to[i]]
+                        + [hop + x for y in b for ee, x in banks[y].items() if ee != e])
+                tail[i] = s = s + c
+                for y in b:
+                    banks[y][e] = s
+                if e is not None:
+                    queue[e] = s
+            base, q0, b0 = 0.0, {}, [{} for _ in range(8)]
+            for i in order[:a]:
+                base = max([base, end[i] + (calls[i]["lat"] if not to[i] else 0.0)] + [end[i] + d + tail[j] for j, d in to[i] if j in tail])
+                for y in case[i][2]:
+                    b0[y][case[i][0]] = end[i]
+                if case[i][0] is not None:
+                    q0[case[i][0]] = end[i]
+            rows = [(case[i][0], case[i][1], case[i][2], [(local[p], d) for p, d in case[i][3] if p in local],
+                     max([0.0] + [end[p] + d for p, d in case[i][3] if p not in local]),
+                     max([calls[i]["lat"] if not to[i] else -1e9] + [d + tail[j] for j, d in to[i] if j in tail])) for i in inside]
+            frame.append((rows, base, q0, b0, queue, banks))
+
+        def value(seq):
+            total, first = 0.0, None
+            for (rows, base, q0, b0, q1, b1), w in zip(frame, weight):
+                end, queue, banks, most = [0.0] * len(rows), dict(q0), [dict(x) for x in b0], base
+                for x in seq:
+                    e, c, b, deps, s, out = rows[x]
+                    if e in queue and queue[e] > s:
+                        s = queue[e]
+                    for p, d in deps:
+                        if end[p] + d > s:
+                            s = end[p] + d
+                    for y in b:
+                        for ee, u in banks[y].items():
+                            if ee != e and u + hop > s:
+                                s = u + hop
+                    end[x] = s = s + c
+                    for y in b:
+                        banks[y][e] = s
+                    if e is not None:
+                        queue[e] = s
+                    if s + out > most:
+                        most = s + out
+                for e, s in queue.items():
+                    if e in q1 and s + q1[e] > most:
+                        most = s + q1[e]
+                for y in range(8):
+                    for e, s in banks[y].items():
+                        for ee, u in b1[y].items():
+                            if ee != e and s + hop + u > most:
+                                most = s + hop + u
+                total += w * (most + CFG["SOON"] * sum(end) / len(end))
+                first = first or end
+            return total, seq, first
+        laid = []
+        for rows, _, q0, b0, _, _ in frame:
+            t0 = min(r[4] for r in rows)
+            free = [ticks(max([r[4], q0.get(r[0], 0.0)] + [u + hop for y in r[2] for ee, u in b0[y].items() if ee != r[0]]) - t0) for r in rows]
+            laid.append(([(r[0], ticks(r[1]), r[2]) for r in rows], [[(p, ticks(d)) for p, d in r[3]] for r in rows], free))
+        m = len(inside)
+        good = now = value(list(range(m)))
+        for _ in range(CFG["TRIES"]):
+            size, share, i0 = 0.15 * 20.0 ** draw(), 0.4 * draw() ** 2 + 0.02, int(draw() * m)
+            key = [now[2][x] - frame[0][0][x][1] for x in range(m)]
+            if draw() < CFG["WHOLE"]:
+                shift = size * (2 * draw() - 1)
+                key = [key[x] + shift if calls[inside[x]]["part"] == calls[inside[i0]]["part"] and draw() < 0.8 else key[x] for x in range(m)]
+            else:
+                key = [key[x] + size * (2 * draw() - 1) if draw() < share else key[x] for x in range(m)]
+            work, deps, free = laid[int(draw() * len(laid))]
+            start = place_calls(work, deps, sorted(range(m), key=lambda x: key[x]), free)
+            new = value(sorted(range(m), key=lambda x: (start[x], work[x][1] > 0)))
+            if new[0] <= now[0] + heat * draw():
+                now = new
+            if new[0] < good[0]:
+                good = new
+        return order[:a] + [inside[x] for x in (now if heat > CFG["COLD"] else good)[1]] + order[z:]
+    order = top[1]
+    for turn in range(CFG["LOOKS"]):
+        m = int(CFG["WIDE"] * (0.6 + 0.8 * draw()))
+        a = max(0, min(n - m, int(draw() * (n + m // 2)) - m // 2))
+        order = window(order, a, a + m, max(CFG["COLD"], CFG["WARM"] * (1.0 - 1.3 * turn / CFG["LOOKS"])))
+        end = replay(cases[0], order)
+        at = {i: x for x, i in enumerate(order)}
+        order.sort(key=lambda i: (round(end[i] - cases[0][i][1], 6), at[i]))
+    top = measure(order, 0, [[0.0] * n for _ in cases])
+    best = (top[0], None, None, top[1])
     end = replay(cases[0], best[3])
-    ORDER["plan"] = (best[0], [(k["e"], end[i] - k["c"], k["c"], (k["w"] + k["r"])[0]) for i, k in enumerate(calls)])
+    ORDER["plan"] = (best[0], [(k["e"], end[i] - k["c"], k["c"], (k["w"] + k["r"])[0]) for i, k in enumerate(calls)],
+                     [round(max(x[i] + calls[i]["lat"] for i in last), 1) for x in (replay(case, best[3]) for case in cases)])
     return best[3]
 
 
@@ -339,7 +541,8 @@ def rank_program(g, core, T, topo):
         res = k["fn"]()
         if sem is None:
             sem = "q" + e
-            res.then_inc(T.sem[sem], 1)
+            for x in res if isinstance(res, list) else [res]:
+                x.then_inc(T.sem[sem], 1)
         count[sem] = max(count.get(sem, 0) + k["inc"], k["total"] or 0) if k["total"] is None else k["total"]
         tok = (sem, count[sem], dict(known[e]))
         for x in r:
@@ -352,14 +555,22 @@ def rank_program(g, core, T, topo):
             bank.setdefault(x, {})[e] = tok
 
     def op(e, fc, r=(), w=(), b=(), sem=None, inc=1, total=None, lat=0.0):
-        c, kind = fc[1] if isinstance(fc[1], tuple) else (fc[1], 3 if sem else 0)
+        c, kind = fc[1] if isinstance(fc[1], tuple) else (fc[1], 3 if sem else 4 if e == "P" else 0)
         calls.append(dict(e=e, fn=fc[0], c=c, kind=kind, part=stage[0], r=list(r), w=list(w), b=tuple(b), sem=sem, inc=inc, total=total, lat=lat))
+
+    def run(e, fcs, r=(), w=(), b=()):
+        op(e, (lambda: [fc[0]() for fc in fcs], sum(fc[1] for fc in fcs)), r, w, b, inc=len(fcs))
 
     def dma(e, pairs, sem, r=(), w=(), total=None, lat=2.0):
         def fn():
             for o, i in pairs:
                 Q[e].dma_start(o, i).then_inc(T.sem[sem], 16)
         op(e, (fn, 0.1 * len(pairs)), r, w, sem=sem, inc=16 * len(pairs), total=total, lat=lat)
+
+    def rows(out, a, sem, r, w, add=True, first=False):
+        kw = dict(accum_op=OP.add) if add else {}
+        op("G", (lambda: g.dma_start(out, a, max_dma_last_dim=4096, **kw).then_inc(T.sem[sem], 16), CFG["GD"][0 if first else 1]),
+           r, w, sem=sem, inc=16, lat=CFG["GD"][2])
 
     CYC = 0.00087
 
@@ -405,7 +616,7 @@ def rank_program(g, core, T, topo):
         return [(out, T.WS[:, 144 * wi + 15 - r:144 * wi + 143 - r], src(r)) for r in range(16)]
 
     def iota(out, pat, base, name, n, ch=0):
-        op("G", (lambda: g.iota(out, pat, base, ch, allow_small_or_imprecise_dtypes=True), 0.13 + 2 * n * CYC), w=[name])
+        op("G", (lambda: g.iota(out, pat, base, ch, allow_small_or_imprecise_dtypes=True), 0.13 + 2 * n * CYC), r=["~0"] * (name != "COL"), w=[name])
 
     def pass_on(out, a, n):
         return lambda: g.affine_select(out, a, [[0, n]], OP.is_ge, 0.0, 0, 0), 0.17 + 2 * n * CYC
@@ -427,6 +638,7 @@ def rank_program(g, core, T, topo):
 
     def send(kind, t, name, landed, src=None):
         plan, keep = exchange(kind, t)
+        name = name if isinstance(name, list) else [name]
         near, hs = pl[plan][q]
         m1, m2 = masks(T, topo, pl[plan], q, keep)
         whole, part, land = pieces(T, kind, t)
@@ -437,15 +649,15 @@ def rank_program(g, core, T, topo):
                                  dst=land(q) if part is None else whole) for h, m in zip(hs, m2)]
         chain = ["~" + kind] + ["~h%d" % i for i, h in enumerate(topo.cores_of(core)) if h in hs]
         first = kind == "c" and t == 0
-        op("G", (lambda: g.remote_dma_fused(tr, local_sem=T.sem[l]), 3.5 if first else 0.45), r=[name], w=chain + ["~s" + a] + (["~0"] if kind in "cde" and t == 0 else []),
+        op("G", (lambda: g.remote_dma_fused(tr, local_sem=T.sem[l]), 3.5 if first else 0.45), r=name, w=chain + ["~s" + a] + (["~0"] if kind in "cde" and t == 0 else []),
            sem=l, inc=sum(len(m) for m in m1 + m2))
         total = counts(T, topo, pl[plan], keep)[0][q]
         got_ = ["~s" + a]
         if part is not None:
             total += 16
-            dma("Y", [(land(q), part(q))], a, r=[name], w=["~o" + a], total=total)
+            dma("Y", [(land(q), part(q))], a, r=name, w=["~o" + a], total=total)
             got_.append("~o" + a)
-        op(None, (None, 0.0), r=got_, w=[landed], sem=a, total=total, lat=(CFG["LC0"] - 3.05 if first else CFG["L" + kind + str(min(t, 1))] if kind in "cde" else CFG[plan]) - 0.45)
+        op(None, (None, 0.0), r=got_, w=[landed], sem=a, total=total, lat=(CFG["LC0"] - 3.05 if first else CFG["L" + kind + str(min(t, 1))] if kind in "cde" else CFG[plan] + 0.2 * (kind == "y")) - 0.45)
 
     def parts(t):
         return [(kind,) + columns(kind, t) for kind in "cde" if columns(kind, t)[0] < columns(kind, t)[1]]
@@ -457,105 +669,127 @@ def rank_program(g, core, T, topo):
     dma("Y", [(own0, T.cen[:])], "lcen", w=["cen", "~ld"])
     dma("Y", [(T.EI[:], T.ent[:])], "lent", w=["EI", "~ld"], lat=2.3)
     dma("Y", [(T.XB[:], T.wk[:])], "lwk", w=["Xc", "Xd", "~ld"], lat=2.6)
-    dma("Y", [(T.JT[:], T.jmp[:])], "ljt", w=["JT", "~ld"], lat=2.9)
-    dma("Y", [(T.HW0[:, 4096:4608], T.cen[:])], "lown", w=centre(0) + ["~ld"], lat=3.2)
-    dma("Y", [(T.ZW[:, 0:2048], T.pl[:])], "lpl", w=["Z", "~ld"], lat=4.4)
+    dma("Y", [(T.ZW[:, 0:2048], T.pl[:])], "lpl", w=["Z", "~ld"], lat=3.7)
+    dma("Y", [(T.JT[:], T.jmp[:])], "ljt", w=["JT", "~ld"], lat=3.9)
+    dma("Y", [(T.HW0[:, 4096:4608], T.cen[:])], "lown", w=centre(0) + ["~ld"], lat=4.1)
     dma("Y", [(T.NBI[:], T.nb[:])], "lnb", w=["NBI", "~ld"], lat=4.7)
     for kind, a, z in parts(0):
         send(kind, 0, "cen", "CA0" + kind, src=CA[0][:, 512 * q + a:512 * q + z])
     op("G", (lambda: g.iota(T.PI[:, 0:1], [[0, 1]], 0, 1), 0.13), w=["PI0"])
     iota(T.COL[:], [[1, 144]], 0, "COL", 144)
-    op("G", (lambda: g.iota(T.LI[:], [[1, 16], [0, 2]], 0, 0), 0.19), w=["LI"])
     op("G", (lambda: g.iota(T.LJ[:], [[16, 16], [0, 2]], 0, 0), 0.19), w=["LJ"])
+    iota(T.TA[:], [[16, 8], [0, 16]], 0, "TA", 128)
     iota(T.CT[:], [[0, 8], [1, 32]], 0, "CT", 256)
     iota(T.C8[:], [[0, 8], [8, 32]], 0, "C8", 256)
-    iota(T.KX[:], [[4, 4], [-2, 2], [0, 32]], 2, "KX", 256)
+    iota(T.KX[:], [[2, 4], [-1, 2], [0, 32]], 1, "KX", 256)
     iota(T.KHI[:], [[256, 8], [0, 32]], 2048, "KHI", 256)
-    for j in range(4):
-        iota(T.MT[:, 1024 * j:1024 * j + 1024], [[0, 1024]], 0, "MT%d" % j, 1024)
+    for j in range(8):
+        if j < CFG["MTZ"]:
+            op("V", fill(T.MT[:, 512 * j:512 * j + 512], 0.0, us(256)), w=["MT%d" % j])
+        else:
+            iota(T.MT[:, 512 * j:512 * j + 512], [[0, 512]], 0, "MT%d" % j, 512)
     iota(T.S48[:], [[0, 8], [1, 48]], 0, "S48", 384)
     iota(T.P1[:], [[0, 3], [1, 128]], 0, "P1", 384)
-    iota(T.P2[:], [[1, 3], [0, 128]], 0, "P2", 384)
-    for j in range(4):
-        op("V", fill(T.EW[:, 1024 * j:1024 * j + 1024], 0.0, us(512)), w=["EW%d" % j])
+    iota(T.P2[:], [[128, 3], [0, 128]], 0, "P2", 384)
+    iota(T.JF[:], [[1, 384]], 0, "JF", 384)
+    for j in range(8):
+        if CFG["EWZ"] == "V":
+            op("V", fill(T.EW[:, 512 * j:512 * j + 512], 0.0, us(256)), w=["EW%d" % j])
+        else:
+            iota(T.EW[:, 512 * j:512 * j + 512], [[0, 512]], 0, "EW%d" % j, 512)
 
-    op("V", ts(T.PI[:, 1:2], T.PI[:, 0:1], 15, None, OP.bitwise_and), r=["PI0"], w=["PI1"])
-    op("V", ts(T.PI[:, 2:3], T.PI[:, 0:1], 112, None, OP.bitwise_and), r=["PI0"], w=["PI2"])
-    op("V", ts(T.PI[:, 3:4], T.PI[:, 0:1], 31, None, OP.bitwise_and), r=["PI0"], w=["PI3"])
-    op("V", cp(T.PF[:, 0:4], T.PI[:, 0:4]), r=["PI0", "PI1", "PI2", "PI3"], w=["PF0"])
-    op("V", fill(pf(12), 0.0), w=["A"])
-    op("V", ts(pf(10), pf(2), 15.0, None, OP.add), r=["PF0"], w=["PF10"])
-    op("V", ts(pf(9), pf(1), 2.0, 1.0, OP.mult, OP.add), r=["PF0"], w=["PF9"])
-    op("V", ts(T.PF[:, 4:8], T.COL[:, 0:4], pf(1), None, OP.is_equal), r=["PF0", "COL"], w=["PF4"])
+    def pm(j):
+        return T.PM[:, j:j + 1]
+    run("V", [ts(T.PI[:, j:j + 1], T.PI[:, 0:1], x, None, OP.bitwise_and) for j, x in ((1, 15), (2, 112), (3, 31))], r=["PI0"], w=["PI1"])
+    op("V", cp(T.PF[:, 0:4], T.PI[:, 0:4]), r=["PI0", "PI1"], w=["PF0"])
+    run("V", [fill(T.B7[:, 224:225], 0.0), fill(T.THR[:, 32:64], 2.0 ** 25), fill(T.GO[:, 32:64], -9.0), fill(T.HW0[:, 5120:5136], 0.0),
+              fill(T.HW1[:, 5120:5136], 0.0)], w=["AP", "thr1", "nine", "zero0", "zero1"], b=[7])
+    run("V", [ts(pf(10), pf(2), 15.0, None, OP.add), ts(pf(9), pf(1), 2.0, 1.0, OP.mult, OP.add)], r=["PF0"], w=["PF10", "PF9"])
+    op("V", ts(T.PM[:], T.COL[:, 0:16], pf(1), None, OP.is_equal), r=["PF0", "COL"], w=["PM"])
+    op("V", ts(T.WS[:, 0:144], T.COL[:], pf(10), None, OP.is_equal, c=us(144)), r=["PF10", "COL"], w=["WS0"])
+    op("V", ts(T.ID[:], T.COL[:, 0:128], pf(0), None, OP.is_equal, c=us(128)), r=["PF0", "COL"], w=["ID"])
 
     def weights(j, s, deps=()):
-        op("V", ts(T.WS[:, 144 * j:144 * j + 144], T.COL[:], pf(10), s, OP.is_equal, OP.mult, c=us(144)), r=["PF10", "COL"] + list(deps), w=["WS%d" % j])
+        op("V", ts(T.WS[:, 144 * j:144 * j + 144], T.WS[:, 0:144], s, None, OP.mult, c=us(72)), r=["WS0"] + list(deps), w=["WS%d" % j])
 
-    def scaled_identity(name, s):
-        op("V", ts(T[name][:], T.COL[:, 0:128], pf(0), s, OP.is_equal, OP.mult, c=us(128)), r=["PF0", "COL"], w=[name])
-    for name, s in (("ID", 1.0), ("NID", -1.0), ("I32", 1.0), ("IS", -4096.0), ("IH", 0.5), ("I512", 512.0), ("I16", 16.0)):
+    def scaled_identity(name, s, deps=()):
+        op("V", ts(T[name][:], T.ID[:], s, None, OP.mult, c=us(128 if SCRATCH[name][2] == F32 else 64)), r=["ID"] + list(deps), w=[name])
+    for name, s in (("NID", -1.0), ("I32", 1.0), ("IS", -4096.0), ("IH", 0.5), ("I512", 512.0), ("I16", 16.0)):
         scaled_identity(name, s)
+    scaled_identity("D0", pm(0), ["PM"])
+    scaled_identity("D1", pm(1), ["PM"])
     weights(WJ, pf(9), ["PF9"])
-    for j, s in ((W1, 1.0), (WM2, -2.0), (W8192, 8192.0), (WM4096, -4096.0), (W4096, 4096.0), (WM1, -1.0)):
+    for j, s in ((WM2, -2.0), (W8192, 8192.0), (WM4096, -4096.0), (W4096, 4096.0)):
         weights(j, s)
-    op("V", ts(T.LU[:, 32:48], T.COL[:, 0:16], 32.0, pf(3), OP.mult, OP.add), r=["PF0", "COL"], w=["LU2"])
     op("V", fill(T.ONE[:], 1.0, us(256)), w=["ONE"])
     op("V", fill(T.M8[:], 1.0, us(256)), w=["M8"])
     op("V", fill(T.M32[:], 1.0, us(128)), w=["M32"])
     op("V", fill(T.M8[:, 0:256:8], 0.0), w=["M8"])
     op("V", fill(T.M32[:, 0:256:32], 0.0), w=["M32"])
     op("V", ts(pf(11), pf(1), 256.0, None, OP.mult), r=["PF0"], w=["PF11"])
-    op("V", ts(pf(15), pf(5), 256.0, pf(4), OP.mult, OP.add), r=["PF4"], w=["PF15"])
-    op("V", ts(pf(16), pf(7), 16.0, pf(6), OP.mult, OP.add), r=["PF4"], w=["PF16"])
-    op("V", ts(pf(17), pf(4), float(64 * (q & 3)), None, OP.mult), r=["PF4"], w=["PF17"])
+    op("V", ts(pf(4), pf(1), 2.0, None, OP.is_lt), r=["PF0"], w=["PF4"])
+    op("V", ts(pf(5), pm(2), -512.0, pf(4), OP.mult, OP.add), r=["PF4", "PM"], w=["PF5"])
+    op("V", ts(pf(15), pm(3), 512.0, pf(5), OP.mult, OP.add), r=["PF5", "PM"], w=["PF15"])
+    op("V", ts(pf(16), pm(5), 16.0, pm(4), OP.mult, OP.add), r=["PM"], w=["PF16"])
+    op("V", ts(pf(14), pm(2), 2048.0, pf(4), OP.mult, OP.add), r=["PF4", "PM"], w=["PF14"])
+    op("V", ts(pf(17), pm(1), float(64 * q), None, OP.mult), r=["PM"], w=["PF17"])
+    op("V", ts(pf(18), pm(3), 8.0, pf(17), OP.mult, OP.add), r=["PM", "PF17"], w=["PF18"])
+    op("V", ts(pf(19), pm(5), 32.0, pf(18), OP.mult, OP.add), r=["PM", "PF18"], w=["PF19"])
     op("V", ts(wf(0), T.COL[:, 0:32], 16.0, pf(1), OP.mult, OP.add), r=["PF0", "COL"], w=["m"])
-    op("V", ts(pf(18), pf(5), float(16 + (q >> 2)), pf(17), OP.mult, OP.add), r=["PF4", "PF17"], w=["PF18"])
-    op("V", ts(T.TA[:], T.COL[:, 0:128], pf(2), None, OP.is_ge, c=us(128)), r=["PF0", "COL"], w=["TA"])
-    op("V", ts(T.TB[:], T.COL[:, 0:128], pf(10), None, OP.is_le, c=us(128)), r=["PF10", "COL"], w=["TB"])
-    op("V", ts(T.TC[:], T.COL[:, 0:128], pf(0), -1.0, OP.is_lt, OP.mult, c=us(128)), r=["PF0", "COL"], w=["TC"])
-    op("V", ts(pf(19), pf(7), 32.0, pf(18), OP.mult, OP.add), r=["PF4", "PF18"], w=["PF19"])
     op("V", ts(wf(1), wf(0), 4608.0, None, OP.add), r=["m"], w=["my"])
     weights(WT, pf(15), ["PF15"])
     weights(WY, pf(16), ["PF16"])
-    op("V", tt(T.GRP[:], T.TA[:], T.TB[:], OP.mult, us(128)), r=["TA", "TB"], w=["GRP"])
-    op("V", tt(T.NUP[:], T.TA[:], T.TC[:], OP.mult, us(128)), r=["TA", "TC"], w=["NUP"])
-    op("V", fill(T.HW0[:, 5120:5136], 0.0), w=["zero0"])
-    op("V", fill(T.HW1[:, 5120:5136], 0.0), w=["zero1"])
+    weights(WE, pf(14), ["PF14"])
+    op("V", ts(T.GRP[:], T.TA[:], pf(2), None, OP.is_equal), r=["TA", "PF0"], w=["GRP"])
+    op("V", ts(T.TB[:], T.TA[:], pf(2), -1.0, OP.is_equal, OP.mult), r=["TA", "PF0"], w=["TB"])
+    op("G", (lambda: g.affine_select(T.NUP[:], T.TB[:], [[-1, 128]], OP.is_ge, 0.0, 0, 1), 0.17 + 256 * CYC), r=["TB"], w=["NUP"])
+
+    def two_parts(whole, name, lo, hi):
+        op("S", act(T[lo][:], whole, AF.Copy, us(256)), r=[name], w=[lo])
+        op("P", mm([(T.B7[:, 256:512], T.I32[:], whole), (T.B7[:, 256:512], T.NID[:], T[lo][:])], 256, more=768), r=[name, lo, "I32", "NID"], w=["left"], b=[7])
+        op("S", act(T[hi][:], T.B7[:, 256:512], AF.Copy, us(256)), r=["left"], w=[hi], b=[7])
     op("V", cp(T.NL[:], T.NBI[:], us(256)), r=["NBI"], w=["NL"])
     op("V", ts(T.N1[:], T.NBI[:], 9, None, OP.arith_shift_right, c=us(256)), r=["NBI"], w=["N1"])
-    op("V", ts(T.N2[:], T.NBI[:], 255, None, OP.bitwise_and, c=us(256)), r=["NBI"], w=["N2"])
-    op("V", tt(T.KLO[:], T.N1[:], T.C8[:], OP.add, us(512)), r=["N1", "C8"], w=["KLO"])
-    op("V", ts(T.N3[:], T.NBI[:], 8, 1, OP.arith_shift_right, OP.bitwise_and, c=us(256)), r=["NBI"], w=["N3"])
-    op("V", cp(T.TLO[:], T.N2[:], us(256)), r=["N2"], w=["TLO"])
-    op("V", tt(T.THI[:], T.N3[:], T.KX[:], OP.add, us(512)), r=["N3", "KX"], w=["THI"])
+    op("V", cp(T.OWN[:], T.N1[:], us(256)), r=["N1"], w=["OWN"])
+    op("V", tt(T.KLO[:], T.OWN[:], T.C8[:], OP.add, us(256)), r=["OWN", "C8"], w=["KLO"])
+    op("V", cp(T.NF[:], T.NBI[:], us(256)), r=["NBI"], w=["NF"])
+    two_parts(T.NF[:], "NF", "TLO", "THI")
     op("S", act(T.RT[:], T.CT[:], AF.Identity, us(256), bias=pf(1), scale=0.0), r=["CT", "PF0"], w=["RT"])
-    dma("Y", [(T.MT[f:128:16, :], x[:]) for f, x in enumerate((T.TLO, T.THI, T.RT, T.CT))], "dmt",
-        r=["TLO", "THI", "RT", "CT"], w=["MT"] + ["MT%d" % j for j in range(4)], lat=2.6)
+    dma("Y", [(T.MT[f:128:16, :], x[:]) for f, x in enumerate((T.TLO, T.THI, T.OWN, T.KX, T.RT, T.CT))], "dmt",
+        r=["TLO", "THI", "OWN", "KX", "RT", "CT"], w=["MT"] + ["MT%d" % j for j in range(8)], lat=2.6)
     op("V", ts(T.LU[:, 48:80], T.LJ[:], pf(1), None, OP.add), r=["PF0", "LJ"], w=["LU3"])
     op("V", ts(pf(8), pf(1), 31.0, pf(3), OP.mult, OP.add), r=["PF0"], w=["PF8"])
     op("V", ts(T.LU[:, 80:96], T.COL[:, 0:16], pf(8), None, OP.add), r=["PF8", "COL"], w=["LU4"])
-    op("V", cp(T.EX[:], T.EI[:, 0:256].indirect(T.LU[:, 48:80]), got(512)), r=["EI", "LU3"], w=["EX"])
-    op("V", (lambda: V.transpose(T.ET[:], T.EX[:]), us(512)), r=["EX"], w=["ET"])
-    op("V", cp(T.EG[:], T.ET[:, 0:512].indirect(T.LU[:, 80:96]), got(256)), r=["ET", "LU4"], w=["EG0", "EG1"])
-    op("V", cp(T.EU[:], T.EG[:], us(256)), r=["EG0", "EG1"], w=["EU%d" % c for c in range(4)])
-    op("V", ts(T.E1[:], T.EI[:], 127, None, OP.bitwise_and, c=us(256)), r=["EI"], w=["E1"])
-    op("V", ts(T.E2[:], T.EI[:], 7, None, OP.arith_shift_right, c=us(256)), r=["EI"], w=["E2"])
-    op("V", cp(T.ELO[:], T.E1[:], us(256)), r=["E1"], w=["ELO"])
-    op("V", cp(T.EHI[:], T.E2[:], us(256)), r=["E2"], w=["EHI"])
+    op("V", cp(T.EF[:], T.EI[:], us(256)), r=["EI"], w=["EF"])
+    op("V", cp(T.EX[:, 0:256], T.EI[:, 0:256].indirect(T.LU[:, 48:64]), got(256)), r=["EI", "LU3"], w=["EX0"])
+    op("S", act(T.EX[:, 256:512], T.EF[:, 0:256].indirect(T.LU[:, 64:80]), AF.Copy, got(256)), r=["EF", "LU3"], w=["EX1"])
+    for j in range(2):
+        op("V", (lambda j=j: V.transpose(T.ET[:, 256 * j:256 * j + 256], T.EX[:, 256 * j:256 * j + 256]), us(256)), r=["EX%d" % j], w=["ET%d" % j])
+    for a, z in ((0, 2), (2, 4)):
+        op("V", cp(T.EG[:, 64 * a:64 * z], T.ET[:, 0:512].indirect(T.LU[:, 80 + 4 * a:80 + 4 * z]), got(128)), r=["ET0", "ET1", "LU4"], w=["EG%d" % a])
+        op("V", cp(T.EU[:, 64 * a:64 * z], T.EG[:, 64 * a:64 * z], us(128)), r=["EG%d" % a], w=["EU%d" % c for c in range(a, z)])
+    two_parts(T.EF[:], "EF", "ELO", "EHI")
     dma("Y", [(T.EW[0:128:16, 0:4096], T.ELO[:]), (T.EW[1:128:16, 0:4096], T.EHI[:])], "dew", r=["ELO", "EHI"],
-        w=["EW"] + ["EW%d" % j for j in range(4)], lat=2.6)
-    op("V", ts(T.P1[:], T.P1[:], pf(4), None, OP.mult, c=us(192)), r=["P1", "PF4"], w=["P1"])
-    op("V", ts(T.P2[:], T.P2[:], pf(5), None, OP.mult, c=us(192)), r=["P2", "PF4"], w=["P2"])
-    op("V", ts(T.PF[:, 20:24], T.COL[:, 0:4], 3.0, 16.0, OP.mult, OP.add), r=["COL"], w=["PF20"])
-    op("V", ts(pf(14), pf(5), 128.0, pf(4), OP.mult, OP.add), r=["PF4"], w=["PF14"])
-    op("V", ts(pf(13), pf(1), 16.0, None, OP.mult), r=["PF0"], w=["PF13"])
-    op("V", tt(T.VB[:], T.P1[:], T.P2[:], OP.add, us(384)), r=["P1", "P2"], w=["VB"])
-    op("V", ts(T.PF[:, 20:24], T.PF[:, 20:24], pf(5), None, OP.mult), r=["PF20", "PF4"], w=["PF20"])
-    weights(WE, pf(14), ["PF14"])
-    op("V", ts(T.LU[:, 0:32], T.LI[:], pf(13), None, OP.add), r=["PF13", "LI"], w=["LU1"])
-    op("S", act(T.SE[:], T.S48[:], AF.Identity, us(384), bias=pf(19), scale=pf(4)), r=["S48", "PF19", "PF4"], w=["SE"])
-    for t in range(R):
-        op("S", act(T.VT[:, 384 * t:384 * t + 384], T.VB[:], AF.Identity, us(384), bias=pf(20 + t)), r=["VB", "PF20"], w=["VT%d" % t])
+        w=["EW"] + ["EW%d" % j for j in range(8)], lat=2.6)
+    dma("Y", [(T.yn[:], T.ONE[:, 0:256])], "on", r=["ONE"], w=["yn"])
+    op("V", ts(T.PF[:, 20:23], T.COL[:, 0:3], 384.0, pm(1), OP.mult, OP.mult), r=["COL", "PM"], w=["PF20"])
+    op("V", tt(T.PF[:, 20:23], T.PF[:, 20:23], T.PM[:, 3:6], OP.add), r=["PF20", "PM"], w=["PF20"])
+    op("V", ts(T.PF[:, 20:23], T.PF[:, 20:23], pm(2), None, OP.add), r=["PF20", "PM"], w=["PF20"])
+    op("V", ts(pf(23), pm(0), 384.0 * (R - 1), pm(8), OP.mult, OP.add), r=["PM"], w=["PF23"])
+    op("S", act(T.SE[:], T.S48[:], AF.Identity, us(384), bias=pf(19), scale=pm(0)), r=["S48", "PF19", "PM"], w=["SE"])
+    op("S", act(T.VF[:], T.JF[:], AF.Identity, us(384), bias=pf(23), scale=pm(0)), r=["JF", "PF23", "PM"], w=["VT%d" % (R - 1)])
+
+    def values():
+        op("P", mm([(T.B2[:, 0:384], T.D0[:], T.P1[:]), (T.B2[:, 0:384], T.D1[:], T.P2[:])], 384), r=["D0", "D1", "P1", "P2"], w=["B2"], b=[2])
+        op("S", act(T.VB[:], T.B2[:, 0:384], AF.Copy, us(384)), r=["B2"], w=["VB"], b=[2])
+        for t in range(R - 1):
+            op("V", ts(T.VT[:, 384 * t:384 * t + 384], T.VB[:], pf(20 + t), None, OP.add, c=us(192)), r=["VB", "PF20"], w=["VT%d" % t])
+
+    def most(out, a, b, j, r, w):
+        if CFG["PB"]:
+            op("V", tt(out, a, T.B1[:, 512 * j:512 * j + 512], OP.max, (us(256), 5)), r=r + [("Cp", "Yp")[j]], w=[w], b=[1])
+        else:
+            op("V", tt(out, a, b, OP.max, us(512)), r=r, w=[w])
 
     def jump(t):
         H, p = HW[t % 2], t % 2
@@ -571,28 +805,40 @@ def rank_program(g, core, T, topo):
             op("S", act(T.JG[:], T.JT[:, 0:512].indirect(wu(0)), AF.Copy, got(512)), r=["JT", "ju"], w=["JG"])
             op("P", mm([(T.B2[:], T.ID[:], T.XB[:]), (T.B2[:], T.NID[:], T.JG[:])], 512), r=["Xc", "Xd", "JG", "ID", "NID"], w=["B2"], b=[2])
             op("S", act(Y, T.B2[:], AF.Abs, us(512)), r=["B2"], w=[y_], b=[2])
+        if CFG["PB"]:
+            op("V", cp(T.B1[:, 0:512], C, us(256)), r=c_, w=["Cp"], b=[1])
+            op("V", cp(T.B1[:, 512:1024], Y, us(256)), r=[y_], w=["Yp"], b=[1])
         op("P", mm(sel(T.B7[:, 160:224], W1, lambda r: H[:, 4096 + r:5120:16])), r=c_ + [y_, "WS0"], w=["SyP"], b=[7])
-        op("P", mm([(T.B2[:], T.ID[:], C), (T.B2[:], T.NID[:], Y)], 512), r=c_ + [y_, "ID", "NID"], w=["B2"], b=[2])
-        for j in range(2):
-            op("S", act(T.SC2[:, 32 * j:32 * j + 32], T.B7[:, 160:192], AF.Copy), r=["SyP"], w=["SC2%d" % j], b=[7])
-            op("S", act(T.SY2[:, 32 * j:32 * j + 32], T.B7[:, 192:224], AF.Copy), r=["SyP"], w=["SY2%d" % j], b=[7])
-        op("S", act(T.OA[:], T.B2[:], AF.Abs, us(512)), r=["B2"], w=["OA"], b=[2])
-        op("P", mm(sel(T.B7[:, 64:96], W4096, lambda r: T.OA[:, r:512:16])), r=["OA", "WS4"], w=["ownP"], b=[7])
-        for j in range(2):
-            op("S", act(T.THR[:, 32 * j:32 * j + 32], T.B7[:, 64:96], AF.Identity, bias=pf(12)), r=["ownP", "A"], w=["thr%d" % j], b=[7])
-        op("V", cp(wi_(2), T.SY2[:, 0:32]), r=["SY20"], w=["ui"])
-        op("V", ts(wi_(3), wi_(2), 63, None, OP.bitwise_and), r=["ui"], w=["ua"])
-        op("V", ts(wf(3), wi_(3), 1.0 / 64, None, OP.mult), r=["ua"], w=["u64"])
-
-    def bounds(t):
-        C, c_ = HW[t % 2][:, 4096:4608], centre(t % 2)
-        if CFG["CM"] == "P":
-            op("P", mm([(T.B1[:], T.ID[:], C), (T.B1[:], T.NID[:], T.ONE[:])], 512), r=c_ + ["ID", "NID", "ONE"], w=["B1"], b=[1])
-        elif CFG["CM"] == "S":
-            op("S", act(T.CM[:], C, AF.Identity, us(512), bias=-1.0), r=c_, w=["CM"])
+        run("S", [act(T.SC2[:, 32:96], T.B7[:, 160:224], AF.Copy), act(T.SC2[:, 0:32], T.B7[:, 160:192], AF.Copy),
+                  act(T.SC2[:, 96:128], T.B7[:, 192:224], AF.Copy)], r=["SyP"], w=["SC"], b=[7])
+        if CFG["OWN"][t] in "SW":
+            if CFG["OWN"][t] == "W":
+                op("V", tt(T.CM[:], Y, T.B1[:, 0:512], OP.subtract, (us(256), 5)), r=["Cp", y_], w=["CMc", "CMd"], b=[1])
+                op("S", act(T.OA[:], T.CM[:], AF.Abs, us(512)), r=["CMc"], w=["OA"])
+            else:
+                op("P", mm([(T.B2[:], T.ID[:], C), (T.B2[:], T.NID[:], Y)], 512), r=c_ + [y_, "ID", "NID"], w=["B2"], b=[2])
+                op("S", act(T.OA[:], T.B2[:], AF.Abs, us(512)), r=["B2"], w=["OA"], b=[2])
+            op("P", mm([(T.B7[:, 64:96], T.ID[:], T.C8[:, 0:32])] + sel(T.B7[:, 64:96], W4096, lambda r: T.OA[:, r:512:16])), r=["OA", "WS4", "C8", "ID"], w=["ownP"], b=[7])
         else:
-            op("V", ts(T.CM[:], C, -1.0, None, OP.add, c=us(256)), r=c_, w=["CM"])
-        op("P", mm([(T.B2[:], T.ID[:], C), (T.B2[:], T.ID[:], T.ONE[:])], 512), r=c_ + ["ID", "ONE"], w=["B2"], b=[2])
+            most(T.OA[:], Y, C, 0, c_ + [y_], "OA")
+            sums = [(T.B7[:, 64:96], T.IS[:], T.SC2[:, 32:64]), (T.B7[:, 64:96], T.IS[:], T.SC2[:, 64:96])]
+            op("P", mm(sums + sel(T.B7[:, 64:96], W8192, lambda r: T.OA[:, r:512:16]), more=384), r=["OA", "WS2", "IS", "SC"], w=["ownP"], b=[7])
+        op("V", cp(T.UI[:, 0:33], T.B7[:, 192:225]), r=["SyP", "AP"], w=["ui"], b=[7])
+        op("V", ts(T.UI[:, 40:73], T.UI[:, 0:33], 63, None, OP.bitwise_and), r=["ui"], w=["ua"])
+        op("V", ts(T.UF[:, 0:33], T.UI[:, 40:73], 1.0 / 64, None, OP.mult), r=["ua"], w=["u64"])
+        op("S", act(pf(12), T.UF[:, 32:33], AF.Copy, scale=-4096.0 * 64), r=["u64"], w=["A"])
+        op("S", act(T.THR[:, 0:32], T.B7[:, 64:96], AF.Identity, bias=pf(12)), r=["ownP", "A"], w=["thr0"], b=[7])
+
+    wide = [0]
+
+    def difference(a, b, r):
+        wide[0] = bk = 2 if CFG["PB"] else 3 - wide[0] if wide[0] else 1
+        out = T["B%d" % bk][:]
+        op("P", mm([(out, T.ID[:], a), (out, T.NID[:], b)], 512), r=r + ["ID", "NID"], w=["B%d" % bk], b=[bk])
+        return out, "B%d" % bk, bk
+
+    def span(c, ks):
+        return 512 * ks[0], 512 * ks[-1] + 512, 32 * ks[0], 32 * ks[-1] + 32
 
     def entries(t):
         H, p = HW[t % 2], t % 2
@@ -602,28 +848,39 @@ def rank_program(g, core, T, topo):
             src = T.ZW[:, 0:2048 + 384 * t].indirect(T.EU[:, 32 * k:32 * k + 32])
             dep = ["Z", "EU%d" % c] + ["L%d" % u for u in range(t)]
             s_, sk, mh = H[:, 512 * k:512 * k + 512], "s%d_%d" % (p, k), T.MH[:, 512 * k:512 * k + 512]
+            both = kinds[2 * c:2 * c + 2] == "TT"
             if kinds[k] == "V":
                 op("V", cp(s_, src, got(512)), r=dep, w=[sk])
-            else:
-                op("S", act(s_, src, AF.Copy, got(512)), r=dep, w=[sk, "~S"])
+            elif both and k % 2 == 0:
+                op("S", act(H[:, 512 * k:512 * k + 1024], T.ZW[:, 0:2048 + 384 * t].indirect(T.EU[:, 32 * k:32 * k + 64]), AF.Copy, got(1024)),
+                   r=dep, w=[sk, "s%d_%d" % (p, k + 1)])
+            elif not both:
+                op("S", act(s_, src, AF.Copy, got(512)), r=dep, w=[sk])
             if kinds[k] == "E":
-                op("P", mm([(T.B2[:], T.ID[:], s_), (T.B2[:], T.NID[:], H[:, 4096:4608])], 512), r=centre(p) + [sk, "ID", "NID"], w=["B2"], b=[2])
-                op("S", act(mh, T.B2[:], AF.Abs, us(512)), r=["B2"], w=["MH%d" % k], b=[2])
+                d, d_, bk = difference(s_, H[:, 4096:4608], centre(p) + [sk])
+                op("S", act(mh, d, AF.Abs, us(512), scale=0.5), r=[d_], w=["MH%d" % k], b=[bk])
             else:
-                op("V", tt(mh, s_, H[:, 4096:4608], OP.max, us(512)), r=[sk] + centre(p), w=["MH%d" % k])
+                most(mh, s_, H[:, 4096:4608], 0, [sk] + centre(p), "MH%d" % k)
             if k % 2:
                 bk = 5 * (c % 2)
-                out, free = T["B%d" % bk][:, 64 * c:64 * c + 64], ["G%d" % ((c + 2) % 4)]
-                sc = []
-                if kinds[k] != "E":
-                    sc = [(out, T.I32[:], T.SC2[:])]
-                    op("P", mm(sel(out, W1, lambda r, c=c: H[:, 1024 * c + r:1024 * c + 1024:16]), stop=False),
-                       r=["WS0", "s%d_%d" % (p, k - 1), sk] + free, w=["G%d" % c], b=[bk])
-                op("P", mm(sc + sel(out, WM2 if sc else WM1, lambda r, c=c: T.MH[:, 1024 * c + r:1024 * c + 1024:16]), more=192 * len(sc), start=not sc),
-                   r=["WS1", "WS9", "SC20", "SC21", "I32", "MH%d" % (k - 1), "MH%d" % k] + free, w=["G%d" % c], b=[bk])
-                op("S", act(T.RG[:, 64 * c:64 * c + 64], out, AF.Relu, bias=2047.0), r=["G%d" % c], w=["RG%d" % c], b=[bk])
+                B, free = T["B%d" % bk], ["G%d" % ((c + 2) % 4)]
+                out = B[:, 64 * c:64 * c + 64]
+                ks = [x for x in (k - 1, k) if kinds[x] != "E"]
+                if ks:
+                    a, z, x0, x1 = span(c, ks)
+                    head = [(out, T.NID[:], T.ONE[:, 0:64])] if len(ks) == 1 else []
+                    op("P", mm(head + sel(B[:, x0:x1], W1, lambda r, a=a, z=z: H[:, a + r:z:16]), stop=False),
+                       r=["WS0", "NID", "ONE"] + ["s%d_%d" % (p, x) for x in ks] + free, w=["G%d" % c], b=[bk])
+                sc = [(B[:, x0:x1], T.I32[:], T.SC2[:, 64 - 32 * len(ks):64])] if ks else []
+                op("P", mm(sc + sel(out, WM2, lambda r, c=c: T.MH[:, 1024 * c + r:1024 * c + 1024:16]), more=192 * len(sc), start=not ks),
+                   r=["WS1", "SC", "SC0", "I32", "MH%d" % (k - 1), "MH%d" % k] + free, w=["G%d" % c], b=[bk])
+                op("S", act(T.RG[:, 64 * c:64 * c + 64], out, AF.Relu, bias=2047.0 + (len(ks) == 1)), r=["G%d" % c], w=["RG%d" % c], b=[bk])
 
     def flux(t):
+        if CFG["FX"] == "V":
+            if t:
+                op("V", tt(T.FN[:], T.FN[:] if t > 1 else T.ONE[:, 0:256], T.SG[:, 0:256], OP.add, us(256)), r=["n", "ONE", "SG%d" % (t - 1)], w=["n"])
+            return
         n = T.B6[:, 256:512]
         items = [(n, T.ID[:], T.ONE[:, 0:256])] * (1 + t // 2) + [(n, T.IH[:], T.ONE[:, 0:256])] * (t % 2)
         items += [(n, T.IH[:], T.SG[:, 256 * u:256 * u + 256]) for u in range(t)]
@@ -634,83 +891,121 @@ def rank_program(g, core, T, topo):
         Y, y_ = H[:, 4608:5120], "Y%d" % p
         dep = ["CA%dc" % t, "CA%dd" % t, "CA%de" % t, "NL", "cen" if t == 0 else "CAown"]
         for c in range(4):
-            kind, bk = CFG["D"][t][c], 3 + c % 2
-            out = T["B%d" % bk][:, 64 * c:64 * c + 64]
-            head = [(out, T.ID[:], T.KHI[:, 64 * c:64 * c + 64]), (out, T.ID[:], T.KLO[:, 64 * c:64 * c + 64])]
+            bk = 3 + c % 2
+            B = T["B%d" % bk]
+            out = B[:, 64 * c:64 * c + 64]
+            head, tail = ([(out, T.ID[:], x[:, 64 * c:64 * c + 64])] for x in (T.KHI, T.KLO))
             free = ["KD%d" % (c - 2)] if c > 1 else ["pf", "mP"]
             for k in (2 * c, 2 * c + 1):
+                kind = CFG["D"][t][k]
                 src = CA[t][:, 0:4096].indirect(T.NL[:, 32 * k:32 * k + 32])
                 ag, mx = T.AG[:, 512 * k:512 * k + 512], T.MX[:, 512 * k:512 * k + 512]
-                if kind == "C":
-                    op("S", act(ag, src, AF.Copy, got(512)), r=dep, w=["AG%d" % k, "~S"])
-                    op("V", tt(mx, ag, Y, OP.max, us(512)), r=["AG%d" % k, y_], w=["MX%d" % k])
+                if kind in "CT":
+                    if kind == "C":
+                        op("S", act(ag, src, AF.Copy, got(512)), r=dep, w=["AG%d" % k])
+                    elif k % 2 == 0:
+                        op("S", act(T.AG[:, 512 * k:512 * k + 1024], CA[t][:, 0:4096].indirect(T.NL[:, 32 * k:32 * k + 64]), AF.Copy, got(1024)),
+                           r=dep, w=["AG%d" % k, "AG%d" % (k + 1)])
+                    most(mx, ag, Y, 1, ["AG%d" % k, y_], "MX%d" % k)
                 elif kind == "E":
-                    op("S", act(ag, src, AF.Copy, got(512)), r=dep, w=["AG%d" % k, "~S"])
-                    op("P", mm([(T.B2[:], T.ID[:], ag), (T.B2[:], T.NID[:], Y)], 512), r=["AG%d" % k, y_, "ID", "NID"], w=["B2"], b=[2])
-                    op("S", act(mx, T.B2[:], AF.Abs, us(512)), r=["B2"], w=["MX%d" % k], b=[2])
+                    op("S", act(ag, src, AF.Copy, got(512)), r=dep, w=["AG%d" % k])
+                    d, d_, db = difference(ag, Y, ["AG%d" % k, y_])
+                    op("S", act(mx, d, AF.Abs, us(512), scale=0.5), r=[d_], w=["MX%d" % k], b=[db])
                 else:
                     op("V", tt(ag, src, Y, OP.subtract, got(512)), r=dep + [y_], w=["AG%d" % k])
                     if kind == "A":
-                        op("S", act(mx, ag, AF.Abs, us(512)), r=["AG%d" % k], w=["MX%d" % k])
+                        op("S", act(mx, ag, AF.Abs, us(512), scale=0.5), r=["AG%d" % k], w=["MX%d" % k])
                     else:
                         op("V", ts(mx, ag, 0.0, None, OP.max, c=us(256)), r=["AG%d" % k], w=["MX%d" % k])
-            ags, mxs = ["AG%d" % (2 * c), "AG%d" % (2 * c + 1)], ["MX%d" % (2 * c), "MX%d" % (2 * c + 1)]
-            if kind not in "AE":
-                sy = [(out, T.IS[:], T.SY2[:])] if kind == "C" else []
-                op("P", mm(sy + sel(out, WM4096, lambda r, c=c: T.AG[:, 1024 * c + r:1024 * c + 1024:16]), more=192 * len(sy), stop=False),
-                   r=["IS", "SY20", "SY21", "WS3"] + ags + free, w=["KD%d" % c], b=[bk])
-            op("P", mm(sel(out, W4096 if kind in "AE" else W8192, lambda r, c=c: T.MX[:, 1024 * c + r:1024 * c + 1024:16]) + head, start=kind in "AE"),
-               r=["WS2", "WS4", "KHI", "KLO", "ID"] + mxs + free, w=["KD%d" % c], b=[bk])
+            mxs = ["MX%d" % (2 * c), "MX%d" % (2 * c + 1)]
+            ks = [k for k in (2 * c, 2 * c + 1) if CFG["D"][t][k] in "CTR"]
+            if ks:
+                a, z, x0, x1 = span(c, ks)
+                cs = [k for k in ks if CFG["D"][t][k] in "CT"]
+                sy = [(B[:, 32 * cs[0]:32 * cs[-1] + 32], T.IS[:], T.SC2[:, 64:64 + 32 * len(cs)])] if cs else []
+                op("P", mm(head + sy + sel(B[:, x0:x1], WM4096, lambda r, a=a, z=z: T.AG[:, a + r:z:16]), more=192 * len(sy), stop=False),
+                   r=["IS", "SC", "SC3", "WS3", "KHI", "C8", "ID"] + ["AG%d" % k for k in ks] + free, w=["KD%d" % c], b=[bk])
+                head = []
+            op("P", mm(head + sel(out, W8192, lambda r, c=c: T.MX[:, 1024 * c + r:1024 * c + 1024:16]) + tail, start=not ks),
+               r=["WS2", "KHI", "KLO", "ID"] + mxs + free, w=["KD%d" % c], b=[bk])
             op("V", tt(T.RUN[:], T.THR[:] if c == 0 else T.RUN[:], out, OP.min), r=["thr0", "thr1", "RUN", "KD%d" % c], w=["RUN"], b=[bk])
         op("V", tt(wi_(4), T.RUN[:, 0:32], T.RUN[:, 32:64], OP.min), r=["RUN"], w=["kz"])
 
     def choice(t):
-        for k in range(8):
-            op("V", tt(T.G2[:, k:256:8], T.RG[:, 32 * k:32 * k + 32], T.B6[:, 256 + 32 * k:288 + 32 * k], OP.mult),
-               r=["RG%d" % (k // 2), "n"], w=["G2_%d" % k], b=[6])
-        op("V", scan(T.PP[:], T.M8[:], T.G2[:], us(256)), r=["M8"] + ["G2_%d" % k for k in range(8)], w=["PP"])
+        n, at = (T.B6, 256) if CFG["FX"] == "P" else (T.FN if t else T.ONE, 0)
+        for c in range(4):
+            run("V", [tt(T.G2[:, k:256:8], T.RG[:, 32 * k:32 * k + 32], n[:, at + 32 * k:at + 32 * k + 32], OP.mult) for k in (2 * c, 2 * c + 1)],
+                r=["RG%d" % c, "n", "ONE"], w=["G2_%d" % c], b=[6] * (at > 0))
+        op("V", scan(T.PP[:], T.M8[:], T.G2[:], us(256)), r=["M8"] + ["G2_%d" % c for c in range(4)], w=["PP"])
         fold = CFG["FOLD"][t]
         if fold:
-            op("V", tt(T.GO[:], wi_(4), T.THR[:, 0:32], OP.is_ge), r=["kz", "thr0"], w=["go"])
-            op("V", tt(wf(2), wf(3), T.GO[:], OP.max), r=["u64", "go"], w=["uf"])
-        op("V", tt(wf(4), T.PP[:, 7:256:8], wf(2) if fold else wf(3), OP.mult), r=["PP", "u64", "uf"], w=["th2"])
-        for k in range(8):
-            op("V", tt(T.NC[:, 32 * k:32 * k + 32], T.PP[:, k:256:8], wf(4), OP.is_le), r=["PP", "th2"], w=["NC%d" % k])
+            op("V", tt(T.GO[:, 0:32], wi_(4), T.THR[:, 0:32], OP.is_ge), r=["kz", "thr0"], w=["go"])
+            op("V", tt(wf(2), T.UF[:, 0:32], T.GO[:, 0:32], OP.max), r=["u64", "go"], w=["uf"])
+        run("V", [tt(T.B0[:, 256 + j:320:2], T.PP[:, 7:256:8], wf(2) if fold else T.UF[:, 0:32], OP.mult) for j in range(2)], r=["PP", "u64", "uf"], w=["th"], b=[0])
+        run("V", [tt(T.NC[:, 64 * k:64 * k + 64], T.PP[:, k:256:4], T.B0[:, 256:320], OP.is_le) for k in range(4)], r=["PP", "th"], w=["NC"], b=[0])
         out = T.B7[:, 96:128]
-        items = [(out, T.I512[:], T.NC[:, 32 * k:32 * k + 32]) for k in range(8)]
-        nc = ["NC%d" % k for k in range(8)] + ["I512"]
+        items = [(out, T.I512[:], T.NC[:, 64 * k + j:64 * k + 64:2]) for k in range(4) for j in range(2)]
+        nc = ["NC", "I512"]
         if fold:
-            items = [(out, T.I512[:], T.GO[:]), (out, T.I16[:], T.CT[:, 0:32]), (out, T.ID[:], T.RT[:, 0:32])] + items
+            items = [(out, T.I512[:], T.GO[:, 0:32]), (out, T.I16[:], T.CT[:, 0:32]), (out, T.ID[:], T.RT[:, 0:32])] + items
             op("P", mm(items), r=nc + ["go", "I16", "CT", "ID", "RT"], w=["fP"], b=[7])
             op("V", cp(wu(2), out), r=["fP"], w=["xu"], b=[7])
+        elif CFG["BOTH"][t]:
+            op("P", mm([(out, T.I16[:], T.CT[:, 0:32]), (out, T.ID[:], T.RT[:, 0:32])] + items), r=nc + ["I16", "CT", "ID", "RT"], w=["fP"], b=[7])
+            op("V", cp(wu(5), out), r=["fP"], w=["zu"], b=[7])
+            op("V", ts(wi_(7), wi_(4), 3, 256 + 31, OP.arith_shift_right, OP.bitwise_and), r=["kz"], w=["gc"])
+            op("V", ts(wu(2), wi_(7), 16.0, pf(1), OP.mult, OP.add), r=["gc", "PF0"], w=["xu"])
         else:
-            op("P", mm(items), r=nc, w=["fP"], b=[7])
-            op("S", act(wf(5), out, AF.Identity, bias=-4608.0), r=["fP"], w=["fz"], b=[7])
-            op("V", tt(T.GO[:], wi_(4), T.THR[:, 0:32], OP.is_lt), r=["kz", "thr0"], w=["go"])
-            op("V", tt(wf(7), wf(5), T.GO[:], OP.mult), r=["fz", "go"], w=["x1"])
+            op("P", mm([(out, T.I512[:], T.GO[:, 32:64])] + items), r=nc + ["nine"], w=["fP"], b=[7])
+            op("V", tt(T.GO[:, 0:32], wi_(4), T.THR[:, 0:32], OP.is_lt), r=["kz", "thr0"], w=["go"])
+            op("V", tt(wf(7), out, T.GO[:, 0:32], OP.mult), r=["fP", "go"], w=["x1"], b=[7])
             op("V", tt(wf(9), wf(7), wf(1), OP.add), r=["x1", "my"], w=["x2"])
             op("V", cp(wu(2), wf(9)), r=["x2"], w=["xu"])
 
     def move(t):
         p, pn = t % 2, 1 - t % 2
-        src = HW[p][:, 0:5120].indirect(wu(2))
+        if CFG["MV"][t] == "B" and not CFG["PB"]:
+            for B, sign, bk in ((T.B1, T.NID, 1), (T.B2, T.ID, 2)):
+                op("P", mm([(B[:], T.ID[:], HW[p][:, 4096:4608]), (B[:], sign[:], T.ONE[:])], 512), r=centre(p) + ["ID", "NID", "ONE"], w=["B%d" % bk], b=[bk])
         dep = ["s%d_%d" % (p, k) for k in range(8)] + centre(p) + ["Y%d" % p, "xu"]
         new = HW[pn][:, 4096:4608]
-        cut = parts(t + 1) if t < R - 1 else [("c", 0, 512)]
+        cut = [("c", 0, 256), ("d", 256, 512)] if CFG["CUT"][t] else [("c", 0, 512)]
+        if CFG["BOTH"][t]:
+            H, s_ = HW[p], ["s%d_%d" % (p, k) for k in range(8)]
+            op("S", act(H[:, 5136:5648], H[:, 0:4608].indirect(wu(5)), AF.Copy, got(512)), r=s_ + centre(p) + ["zu"], w=["XZ"])
+            op("V", tt(T.CM[:], H[:, 4608:5120], T.B1[:], OP.max, us(512)), r=["Y%d" % p, "B1"], w=["CM"], b=[1])
+            op("V", tt(T.CM[:], T.CM[:], T.B2[:], OP.min, us(512)), r=["CM", "B2"], w=["CM"], b=[2])
+            op("V", cp(H[:, 0:512], T.CM[:], us(256)), r=["CM"], w=s_[:1])
+            op("G", pass_on(H[:, 1040:1552], H[:, 4608:5120], 512), r=["Y%d" % p], w=s_[2:4])
+            op("V", tt(T.TM[:], H[:, 5136:5648], T.B1[:], OP.max, us(512)), r=["XZ", "B1"], w=["TMc", "TMd"], b=[1])
+            op("V", tt(H[:, 4096:4608], T.TM[:], T.B2[:], OP.min, us(512)), r=["TMc", "B2"], w=centre(p), b=[2])
+            for e, (kind, a, z) in zip(CFG["BOTH"][t], cut):
+                part, chosen = HW[pn][:, 4096 + a:4096 + z], H[:, 0:4608].indirect(T.WU[:, 64 + a // 16:64 + z // 16])
+                op(e, act(part, chosen, AF.Copy, got(z - a)) if e == "S" else cp(part, chosen, got(z - a)), r=dep, w=["C%d%s" % (pn, kind)])
+            op("S", act(T.XB[:], H[:, 1040:5648].indirect(wu(2)), AF.Copy, got(512)), r=dep + ["XZ", "zero%d" % p], w=["Xc", "Xd"])
+            cut = []
         for kind, a, z in cut:
             name = centre(pn) if len(cut) == 1 else ["C%d%s" % (pn, kind)]
             part = HW[pn][:, 4096 + a:4096 + z]
             chosen = HW[p][:, 0:5120].indirect(T.WU[:, 64 + a // 16:64 + z // 16])
-            if CFG["CM"] == "P":
-                op("S", act(T.XB[:, a:z], chosen, AF.Copy, got(z - a)), r=dep, w=["Xc", "Xd"] if len(cut) == 1 else ["X" + kind])
-                op("V", tt(T.TM[:, a:z], T.XB[:, a:z], T.B1[:, a:z], OP.max, us(z - a)), r=["X" + kind, "B1"], w=["TM" + kind], b=[1])
+            C = HW[p][:, 4096 + a:4096 + z]
+            op("S", act(T.XB[:, a:z], chosen, AF.Copy, got(z - a)), r=dep, w=["Xc", "Xd"] if len(cut) == 1 else ["X" + kind])
+            if CFG["PB"]:
+                half = us((z - a) // 2)
+                op("V", tt(T.CM[:, a:z], T.XB[:, a:z], T.B1[:, a:z], OP.subtract, (half, 5)), r=["X" + kind, "Cp"], w=["CM" + kind], b=[1])
+                op("V", ts(T.TM[:, a:z], T.CM[:, a:z], -1.0, 1.0, OP.max, OP.min, c=half), r=["CM" + kind], w=["TM" + kind])
+                op("V", tt(part, T.TM[:, a:z], T.B1[:, a:z], OP.add, (half, 5)), r=["TM" + kind, "Cp"], w=name, b=[1])
+            elif CFG["MV"][t] == "S":
+                bk = 1 + (kind == "d")
+                d = T["B%d" % bk][:, a:z]
+                op("P", mm([(d, T.NID[:], C), (d, T.ID[:], T.XB[:, a:z])], z - a), r=centre(p) + ["X" + kind, "ID", "NID"], w=["B%d" % bk], b=[bk])
+                op("S", act(T.TM[:, a:z], d, AF.Sign, us(z - a)), r=["B%d" % bk], w=["TM" + kind], b=[bk])
+                op("V", tt(part, T.TM[:, a:z], C, OP.add, us(z - a)), r=["TM" + kind] + centre(p), w=name)
             else:
-                op("V", tt(T.TM[:, a:z], chosen, T.CM[:, a:z], OP.max, got(z - a)), r=dep + ["CM"], w=["TM" + kind])
-            op("V", tt(part, T.TM[:, a:z], T.B2[:, a:z], OP.min, us(z - a)), r=["TM" + kind, "B2"], w=name, b=[2])
-            if t < R - 1:
-                send(kind, t + 1, name[0], "CA%d%s" % (t + 1, kind), src=part)
-        if CFG["CM"] != "P":
-            op("S", act(T.XB[:], src, AF.Copy, got(512)), r=dep, w=["Xc", "Xd"])
+                op("V", tt(T.TM[:, a:z], T.XB[:, a:z], T.B1[:, a:z], OP.max, us(z - a)), r=["X" + kind, "B1"], w=["TM" + kind], b=[1])
+                op("V", tt(part, T.TM[:, a:z], T.B2[:, a:z], OP.min, us(z - a)), r=["TM" + kind, "B2"], w=name, b=[2])
+        for kind, a, z in parts(t + 1) if t < R - 1 else []:
+            send(kind, t + 1, centre(pn)[a // 256:(z + 255) // 256], "CA%d%s" % (t + 1, kind), src=HW[pn][:, 4096 + a:4096 + z])
         if t < R - 1:
             own = CA[t + 1][:, 512 * q:512 * q + 512]
             if CFG["CP"] == "G":
@@ -723,22 +1018,32 @@ def rank_program(g, core, T, topo):
     def exits(t):
         H, p = HW[t % 2], t % 2
         op("G", pass_on(T.SB[:, 512:896], T.SE[:], 384), r=["SE"], w=["SB"])
-        op("V", ts(wi_(5), wi_(4), 2055, None, OP.bitwise_and), r=["kz"], w=["og"])
+        op("V", ts(T.OG[:, 0:32], wi_(4), 2055, None, OP.bitwise_and), r=["kz"], w=["og"])
+        op("V", ts(T.OG[:, 32:64], T.OG[:, 0:32], -4.0, None, OP.add), r=["og"], w=["og4"])
         op("V", ts(wi_(6), wi_(4), 3, 255, OP.arith_shift_right, OP.bitwise_and), r=["kz"], w=["kc"])
         op("V", ts(wu(1), wi_(6), pf(11), None, OP.add), r=["kc", "PF11"], w=["mu"])
         op("S", act(T.MS[:], T.MT[:, 0:4096].indirect(wu(1)), AF.Copy, got(512)), r=["MT", "mu"], w=["MS"])
-        for o in range(8):
-            op("V", ts(T.HIT[:, 32 * o:32 * o + 32], wi_(5), float(2048 + o), None, OP.is_equal), r=["og"], w=["HIT%d" % o])
-        hit = ["HIT%d" % o for o in range(8)]
+        run("V", [ts(T.HIT[:, 64 * o:64 * o + 64], T.OG[:], float(2048 + o), None, OP.is_equal) for o in range(4)], r=["og", "og4"], w=["HIT"])
+        hit = ["HIT"]
         op("V", scan(T.INC[:], T.M32[:], T.HIT[:], us(128)), r=["M32"] + hit, w=["INC"])
         op("P", mm([(T.B3[:, 256:512], T.NUP[:], T.HIT[:]), (T.B3[:, 256:512], T.GRP[:], T.INC[:])], 256), r=hit + ["INC", "GRP", "NUP"], w=["pf"], b=[3])
-        op("V", ts(wf(11), wi_(5), 48.0, 511.0 - 48.0 * 2048, OP.mult, OP.add), r=["og"], w=["t1"])
+        op("V", ts(T.OB[:, 0:32], T.OG[:, 0:32], 48.0, 512.0 - 48.0 * 2048, OP.mult, OP.add), r=["og"], w=["ob"])
         op("V", tt(T.PRD[:], T.B3[:, 256:512], T.HIT[:], OP.mult, us(256)), r=["pf"] + hit, w=["PRD"], b=[3])
         op("P", mm([(T.B7[:, 128:160], T.ID[:], T.PRD[:, 32 * o:32 * o + 32]) for o in range(8)]), r=["PRD", "ID"], w=["cnt"], b=[7])
-        op("V", ts(wf(12), T.B7[:, 128:160], 48.0, None, OP.is_le), r=["cnt"], w=["ar"], b=[7])
-        op("V", tt(wf(13), T.B7[:, 128:160], wf(11), OP.add), r=["cnt", "t1"], w=["val"], b=[7])
-        op("V", tt(wf(14), wf(13), wf(12), OP.mult), r=["val", "ar"], w=["v2"])
-        op("V", tt(wf(15), wf(14), wf(0), OP.max), r=["v2", "m"], w=["v3"])
+        val = T.B4[:, 256:288]
+        if CFG["OV"] == "W":
+            run("V", [ts(wf(12), T.B7[:, 128:160], 48.0, -2048.0, OP.is_ge, OP.mult), tt(wf(13), T.B7[:, 128:160], T.OB[:, 0:32], OP.add)], r=["cnt", "ob"], w=["ov"], b=[7])
+            op("V", tt(wf(14), wf(13), wf(12), OP.add), r=["ov"], w=["val"])
+            op("V", tt(wf(15), wf(14), wf(0), OP.max), r=["val", "m"], w=["v3"])
+        else:
+            op("P", mm([(val, T.ID[:], T.OB[:, 0:32])] + [(val, T.ID[:], T.PRD[:, 32 * o:32 * o + 32]) for o in range(8)], stop=False),
+               r=["PRD", "ID", "ob"], w=["val", "mP"], b=[4])
+            if CFG["OV"] == "S":
+                op("S", act(T.OB[:, 32:64], T.B7[:, 128:160], AF.Relu, bias=-47.0 * 1024, scale=1024.0), r=["cnt"], w=["ov"], b=[7])
+            else:
+                op("V", ts(T.OB[:, 32:64], T.B7[:, 128:160], 48.0, 2048.0, OP.is_ge, OP.mult), r=["cnt"], w=["ov"], b=[7])
+            op("P", mm([(val, T.NID[:], T.OB[:, 32:64])], start=False), r=["ov", "NID"], w=["val", "mP"], b=[4])
+            op("V", tt(wf(15), val, wf(0), OP.max), r=["val", "m"], w=["v3"], b=[4])
         op("V", cp(wu(3), wf(15)), r=["v3"], w=["su"])
         n = 512 // CFG["PUT"][0]
         for a in range(0, 512, n):
@@ -753,51 +1058,37 @@ def rank_program(g, core, T, topo):
         send("y", t, "YS%d" % t, "L%d" % t)
         if t < R - 1:
             op("P", mm([(T.B7[:, 224:225], T.ONE[:, 0:128], T.INC[:, 31 + 32 * o:32 + 32 * o]) for o in range(8)]), r=["INC", "ONE"], w=["AP"], b=[7])
-            op("V", cp(T.PI[:, 4:5], T.B7[:, 224:225]), r=["AP"], w=["Ai"], b=[7])
-            op("V", ts(T.PI[:, 5:6], T.PI[:, 4:5], 63, None, OP.bitwise_and), r=["Ai"], w=["Aa"])
-            op("V", ts(pf(12), T.PI[:, 5:6], -4096.0, None, OP.mult), r=["Aa"], w=["A"])
 
     def arrivals(t):
-        n = 384 // CFG["PUT"][1]
-        for a in range(0, 384, n):
-            op("V", cp(T.EW[:, 0:4608].indirect(T.LM[:, 32 * t + a // 16:32 * t + (a + n) // 16]), T.VT[:, 384 * t + a:384 * t + a + n], put(n)),
-               r=["VT%d" % t, "LM%d" % t], w=["EW"])
-        lim = 0.5 - (2048 + 384 * t)
         if t == R - 1:
-            return results(lim)
+            op("V", cp(T.EWF[:, 0:4608].indirect(T.LM[:, 32 * t:32 * t + 24]), T.VF[:], put(384)), r=["VT%d" % t, "LM%d" % t], w=["EWF"])
+            dma("Y", [(T.ye[:], T.EWF[0:128:16, 0:4096])], "oe", r=["EWF"], lat=2.3)
+            rows(T.yn[:], T.EWF[8:128:16, 0:4096], "gn", ["EWF"], ["yn"])
+            return
+        if t == 0:
+            values()
+        op("V", cp(T.EW[:, 0:4608].indirect(T.LM[:, 32 * t:32 * t + 24]), T.VT[:, 384 * t:384 * t + 384], put(384)), r=["VT%d" % t, "LM%d" % t], w=["EW"])
+        rows(T.yn[:], T.EW[3 + t:128:16, 0:4096], "gn", ["EW"], ["yn"], first=t == 0)
+        if t == R - 2:
+            rows(T.EWF[0:128:8, 0:4096], T.EW[0:128:8, 0:4096], "gf", ["EW"], ["EWF"], add=False)
+            rows(T.EWF[0:128:16, 0:4096], T.EW[1:128:16, 0:4096], "gf", ["EW"], ["EWF"])
+        lim = 0.5 - (2048 + 384 * t)
         cuts = CFG["CUTS"]
         for a, z in zip(cuts, cuts[1:]):
             u, us_ = T.B6[:, 64 * a:64 * z], ["U%d" % c for c in range(a, z)]
             op("P", mm(sel(u, WE, lambda r, a=a, z=z: T.EW[:, 1024 * a + r:1024 * z:16]), 64 * (z - a)), r=["EW", "WS6"], w=us_ + ["~U"], b=[6])
             op("V", cp(T.EU[:, 64 * a:64 * z], u, us(64 * (z - a))), r=us_, w=["EU%d" % c for c in range(a, z)], b=[6])
-        op("S", act(T.SG[:, 256 * t:256 * t + 256], T.B6[:, 0:256], AF.Sign, us(256), bias=lim), r=["U%d" % c for c in range(4)], w=["SG%d" % t], b=[6])
+        if CFG["FX"] == "V":
+            op("V", ts(T.SG[:, 0:256], T.EU[:], -lim, None, OP.is_ge, c=us(128)), r=["EU%d" % c for c in range(4)] + ["n"], w=["SG%d" % t])
+        else:
+            op("S", act(T.SG[:, 256 * t:256 * t + 256], T.B6[:, 0:256], AF.Sign, us(256), bias=lim), r=["U%d" % c for c in range(4)], w=["SG%d" % t], b=[6])
         places, landed = T.ZW[:, 384 * t:384 * t + 384], T.ZW[:, 2048 + 384 * t:2048 + 384 * t + 384]
-        op(CFG["Z"], cp(places, landed, us(192)) if CFG["Z"] == "V" else pass_on(places, landed, 384), r=["L%d" % t], w=["Z"])
+        op(CFG["Z"], {"V": cp(places, landed, us(192)), "G": pass_on(places, landed, 384), "S": act(places, landed, AF.Copy, us(384))}[CFG["Z"]], r=["L%d" % t], w=["Z"])
         if t == R - 2:
             dma("Y", [(T.yz[:, 0:1152], T.ZW[:, 0:1152]), (T.yz[:, 1536:2048], T.ZW[:, 1536:2048])], "oz0", r=["Z"])
 
-    def results(lim):
-        op("S", act(T.NQ[:], T.B6[:, 256:512], AF.Copy, us(256)), r=["n"], w=["NQ"], b=[6])
-        op("S", act(T.NX[:], T.NQ[:, 0:256].indirect(T.LU[:, 0:32]), AF.Copy, got(512)), r=["NQ", "LU1"], w=["NX"])
-        op("V", (lambda: V.transpose(T.NT[:], T.NX[:]), us(256)), r=["NX"], w=["NT"])
-        op("S", act(T.NP[:], T.NT[:, 0:512].indirect(T.LU[:, 32:48]), AF.Copy, got(256)), r=["NT", "LU2"], w=["NP"])
-        for x, bk in ((0, 6), (1, 4)):
-            part = slice(128 * x, 128 * x + 128)
-            u, n = T["B%d" % bk][:, 0:128], T["B%d" % bk][:, 128:256]
-            names = ["U0", "U1", "U2", "U3"] if bk == 6 else ["mP", "KD1", "KD3"]
-            op("P", mm(sel(u, WE, lambda r, x=x: T.EW[:, 256 * r + 128 * x:256 * r + 128 * x + 128]), 128), r=["EW", "WS6"], w=names + ["~U"], b=[bk])
-            op("V", ts(T.EG[:, part], u, 2048.0, 2048.0, OP.is_ge, OP.mult, c=us(128)), r=names, w=["EG%d" % x], b=[bk])
-            op("V", tt(T.EF[:, part], u, T.EG[:, part], OP.subtract, us(128)), r=names + ["EG%d" % x], w=["EF%d" % x], b=[bk])
-            sg = T.SG[:, 768 + 128 * x:896 + 128 * x]
-            op("S", act(sg, u, AF.Sign, us(128), bias=lim), r=names, w=["SGx%d" % x], b=[bk])
-            op("P", mm([(n, T.ID[:], T.NP[:, part]), (n, T.IH[:], T.ONE[:, 0:128]), (n, T.IH[:], sg)], 128),
-               r=["NP", "ID", "IH", "ONE", "SGx%d" % x], w=["nx%d" % x], b=[bk])
-            op("S", act(T.NF[:, part], n, AF.Copy, us(128)), r=["nx%d" % x], w=["NF%d" % x], b=[bk])
-        dma("Y", [(T.ye[:], T.EF[:])], "oe", r=["EF0", "EF1"])
-        dma("S", [(T.yn[:], T.NF[:])], "on", r=["NF0", "NF1"])
-
     for t in range(R):
-        middle = (neighbours, exits, entries, choice, bounds, move) if CFG["FOLD"][t] else (entries, neighbours, choice, bounds, move, exits)
+        middle = (neighbours, exits, entries, choice, move) if CFG["FOLD"][t] else (entries, neighbours, choice, move, exits)
         for part in (jump, flux) + middle + (arrivals,):
             stage[0] += 1
             part(t)

from concourse.bass import DstId, RemoteDMATransfer
from concourse.mybir import AluOpType as OP, ActivationFunctionType as AF

R = 4
BF, F32, I32, U16 = "bfloat16", "float32", "int32", "uint16"
CFG = {
    "D": ["CCAACCAA", "CCAACCAA", "CCAACCAA", "CCAACCAA"], "PUT": (1, 1),
    "H": ["TTVVTTSS", "TTTTTTSS", "VVTTTTSS", "TTTTTTSS"], "CUTS": [0, 1, 2, 4],
    "MV": "BBBB", "OWN": "VVVV", "OV": "W", "EWZ": "V", "MTZ": 2, "PB": True, "FX": "V", "GD": (2.5, 1.2, 2.3),
    "CASES": [((0.96, 0.96, 0.96, 1.0, 1.2, 0.96), 1.03, 1.0), ((1.4, 1.75, 2.0, 1.0, 1.6, 1.4), 1.15, 1.45), ((1.2, 0.9, 1.5, 1.0, 1.5, 1.8), 1.4, 1.25),
              ((1.2, 1.45, 0.7, 1.0, 1.2, 1.8), 0.95, 1.15)], "SEED": 2,
    "FOLD": [False, True, False, True],
    "JV": [False, False, False, False],
    "XM": ["direct"] * 4, "XY": ["exits"] * 4, "CUT": [True, True, True, False], "BOTH": ["", "", "", ""], "KEEP0": True,
    "XC": ["there"] * 4, "XD": ["exits"] * 4, "XE": ["direct"] * 4, "SPLIT": [[192, 256], [256, 512], [256, 512], [256, 512]],
    "four": 4.9, "quad": 4.9, "Lc1": 6.8, "Ld1": 6.8, "Ld0": 7.5, "Le0": 7.0, "LC0": 11.0, "exits": 5.5, "direct": 4.2, "HOP": 0.1, "ROUNDS": 800, "MOVES": 1, "LOOKS": 800, "TRIES": 150, "WIDE": 70, "WARM": 0.1, "COLD": 0.1, "SOON": 0.03, "GIVE": 0.05, "MARK": 0.6, "NEAR": 0.5, "EARLY": 0.02, "LAND": 0.0, "FAR": 0.5, "HEAT": 0.3, "SORT": True, "TICK": 0.02, "PLAN": (1.0, 1.0, 1.0, 1.0, 1.2, 1.2), "SLACK": 0.3, "WHOLE": 0.4, "CP": "G", "CM": "V", "Z": "G",
}

SCRATCH = {
    "CA0": ("sbuf", [128, 4096], BF), "CA1": ("sbuf", [128, 4096], BF), "CA2": ("sbuf", [128, 4096], BF), "CA3": ("sbuf", [128, 4096], BF),
    "HW0": ("sbuf", [128, 5648], BF), "HW1": ("sbuf", [128, 5136], BF),
    "ZW": ("sbuf", [128, 3584], BF), "EW": ("sbuf", [128, 4608], BF), "MT": ("sbuf", [128, 4096], BF),
    "AG": ("sbuf", [128, 4096], BF), "MX": ("sbuf", [128, 4096], BF), "MH": ("sbuf", [128, 4096], BF),
    "JT": ("sbuf", [128, 512], BF), "XB": ("sbuf", [128, 512], BF), "JG": ("sbuf", [128, 512], BF),
    "OA": ("sbuf", [128, 512], BF), "CM": ("sbuf", [128, 512], BF), "TM": ("sbuf", [128, 512], BF), "MS": ("sbuf", [128, 512], BF),
    "ONE": ("sbuf", [128, 512], BF),
    "SB": ("sbuf", [128, 896], BF), "YS": ("sbuf", [128, 1536], BF), "VT": ("sbuf", [128, 1536], BF), "VB": ("sbuf", [128, 384], BF),
    "P1": ("sbuf", [128, 384], BF), "P2": ("sbuf", [128, 384], BF), "S48": ("sbuf", [128, 384], BF), "SE": ("sbuf", [128, 384], BF),
    "META": ("sbuf", [128, 128], U16), "LM": ("sbuf", [128, 128], U16),
    "NBI": ("sbuf", [128, 256], I32), "N1": ("sbuf", [128, 256], I32), "NF": ("sbuf", [128, 256], F32),
    "NL": ("sbuf", [128, 256], U16), "EU": ("sbuf", [128, 256], U16),
    "EI": ("sbuf", [128, 256], I32), "EWF": ("sbuf", [128, 4608], F32), "VF": ("sbuf", [128, 384], F32), "JF": ("sbuf", [128, 384], F32),
    "ELO": ("sbuf", [128, 256], BF), "EHI": ("sbuf", [128, 256], BF),
    "KHI": ("sbuf", [128, 256], BF), "OWN": ("sbuf", [128, 256], BF), "KLO": ("sbuf", [128, 256], BF), "FN": ("sbuf", [128, 256], BF), "TLO": ("sbuf", [128, 256], BF), "THI": ("sbuf", [128, 256], BF),
    "PM": ("sbuf", [128, 16], F32), "OG": ("sbuf", [128, 64], I32), "OB": ("sbuf", [128, 64], BF),
    "D0": ("sbuf", [128, 128], BF), "D1": ("sbuf", [128, 128], BF),
    "CT": ("sbuf", [128, 256], BF), "C8": ("sbuf", [128, 256], BF), "KX": ("sbuf", [128, 256], BF), "RT": ("sbuf", [128, 256], BF),
    "M32": ("sbuf", [128, 256], BF), "M8": ("sbuf", [128, 256], F32),
    "SG": ("sbuf", [128, 1024], BF), "RG": ("sbuf", [128, 256], F32), "G2": ("sbuf", [128, 256], F32), "PP": ("sbuf", [128, 256], F32),
    "NC": ("sbuf", [128, 256], BF), "HIT": ("sbuf", [128, 256], BF), "INC": ("sbuf", [128, 256], BF), "PRD": ("sbuf", [128, 256], BF),
    "EF": ("sbuf", [128, 256], F32), "EG": ("sbuf", [128, 256], F32),
    "COL": ("sbuf", [128, 144], F32), "PI": ("sbuf", [128, 8], I32), "PF": ("sbuf", [128, 24], F32),
    "WS": ("sbuf", [128, 10 * 144], BF), "ID": ("sbuf", [128, 128], BF), "NID": ("sbuf", [128, 128], BF), "IH": ("sbuf", [128, 128], BF),
    "I512": ("sbuf", [128, 128], BF), "I16": ("sbuf", [128, 128], BF), "I32": ("sbuf", [128, 128], F32), "IS": ("sbuf", [128, 128], F32),
    "GRP": ("sbuf", [128, 128], BF), "NUP": ("sbuf", [128, 128], BF),
    "TA": ("sbuf", [128, 128], BF), "TB": ("sbuf", [128, 128], BF),
    "LJ": ("sbuf", [128, 32], I32), "LU": ("sbuf", [128, 96], U16),
    "EX": ("sbuf", [128, 512], F32), "ET": ("sbuf", [128, 512], F32),
    "WF": ("sbuf", [128, 640], F32), "WI": ("sbuf", [128, 320], I32), "WU": ("sbuf", [128, 192], U16), "GO": ("sbuf", [128, 64], BF),
    "UI": ("sbuf", [128, 80], I32), "UF": ("sbuf", [128, 40], F32),
    "SC2": ("sbuf", [128, 128], F32), "RUN": ("sbuf", [128, 64], F32), "THR": ("sbuf", [128, 64], F32),
    "B0": ("psum", [128, 512], F32), "B1": ("psum", [128, 1024], BF) if CFG["PB"] else ("psum", [128, 512], F32), "B2": ("psum", [128, 512], F32), "B3": ("psum", [128, 512], F32),
    "B4": ("psum", [128, 512], F32), "B5": ("psum", [128, 512], F32), "B6": ("psum", [128, 512], F32), "B7": ("psum", [128, 512], F32),
}
SEMAPHORES = (["qV", "qS", "qP", "qG", "lcen", "lent", "lown", "lpl", "lwk", "ljt", "lnb", "dew", "dmt", "oz0", "oz1", "oc", "ox", "oe", "on", "gn", "gf"]
              + ["%s%s%d" % (a, k, t) for a in "lah" for k in "cdemy" for t in range(R)])
ORDER = {}


def bits(engs):
    m = 0
    for e in engs:
        m |= 1 << e
    return m


def deal(engs, n):
    w = 1
    while 2 * w * n <= len(engs):
        w *= 2
    return [engs[i * w:(i + 1) * w] for i in range(n)]


def plans(T, topo):
    out = {"first": [], "later": [], "exits": [], "direct": [], "there": [], "four": [], "quad": []}
    for c in T.cores:
        mate, plane, far = [], [], []
        for o, d in enumerate(T.cores):
            if d != c:
                a, b = topo.chip(c), topo.chip(d)
                (mate if topo.mates(a, b) else plane if topo.same_plane(a, b) else far).append(o)
        free = [h for h in topo.cores_of(c) if h not in T.cores]
        port = [h for h in free if all(topo.may_write(h, T.cores[o]) for o in mate + far)]
        there = [h for h in port if topo.die(h) != topo.die(c)][:2]
        here = [h for h in port if topo.die(h) == topo.die(c)][0]
        plain = [h for h in free if topo.die(h) == topo.die(c) and h != here][0]
        two = {h: far[i::len(there)] for i, h in enumerate(there)}
        out["later"].append((mate + plane, two))
        out["first"].append(([], {**two, here: mate + plane[:1], plain: plane[1:]}))
        out["direct"].append((mate + plane + far, {}))
        out["exits"].append(([], {here: mate + far, plain: plane}))
        out["there"].append(([], {there[0]: mate + far[:1] + plane[:2], there[1]: far[1:] + plane[2:]}))
        other = [h for h in free if topo.die(h) != topo.die(c) and h not in there][0]
        out["four"].append(([], {there[0]: far[:2], here: mate + far[2:], plain: plane[:2], other: plane[2:]}))
        others = [h for h in free if topo.die(h) != topo.die(c) and h not in there]
        out["quad"].append(([], {there[0]: far[:2], there[1]: mate + far[2:], others[0]: plane[:2], others[1]: plane[2:]}))
    return out


def masks(T, topo, plan, q, keep):
    c = T.cores[q]
    near, hs = plan[q]
    off = topo.engines(c, T.cores[(q + 1) % len(T.cores)])
    if not hs:
        return deal(off, len(near)), []
    on = topo.engines(c, list(hs)[0])
    if near or keep:
        on = [e for e in on if e not in off]
    return (deal(off, len(near)) if near else []), deal(on, len(hs))


def helper_masks(T, topo, h, far):
    return deal(topo.engines(h, T.cores[far[0]]), len(far))


def counts(T, topo, plan, keep):
    cnt, hc = [0] * len(T.cores), {}
    for q in range(len(T.cores)):
        near, hs = plan[q]
        m1, m2 = masks(T, topo, plan, q, keep)
        for o, m in zip(near, m1):
            cnt[o] += len(m)
        for h, m in zip(hs, m2):
            hc[h] = len(m)
            for o, m3 in zip(hs[h], helper_masks(T, topo, h, hs[h])):
                cnt[o] += len(m3)
    return cnt, hc


def dst(topo, c):
    a = topo.addr(c)
    return DstId(rid=a[0], pnc=a[1])


def pieces(T, kind, t):
    if kind in "cde":
        ca, (a, z) = T["CA%d" % t], columns(kind, t)
        return None, None, lambda q: ca[:, 512 * q + a:512 * q + z]
    if kind == "m":
        return (T.META[:, 32 * t:32 * t + 24], lambda o: T.META[:, 32 * t + 3 * o:32 * t + 3 * o + 3],
                lambda q: T.LM[:, 32 * t + 3 * q:32 * t + 3 * q + 3])
    base = 2048 + 384 * t
    return (T.YS[:, 384 * t:384 * t + 384], lambda o: T.YS[:, 384 * t + 48 * o:384 * t + 48 * o + 48],
            lambda q: T.ZW[:, base + 48 * q:base + 48 * q + 48])


def columns(kind, t):
    cuts = [0] + CFG["SPLIT"][t] + [512]
    return cuts["cde".index(kind)], cuts["cde".index(kind) + 1]


def exchange(kind, t):
    if kind in "cde":
        return CFG["X" + kind.upper()][t], t == 0 and CFG["KEEP0"]
    name = CFG["XM" if kind == "m" else "XY"][t]
    return name, name not in ("four", "quad")


def helper_program(g, core, T, topo, pl):
    ends = []
    turns = [(kind, 0) for kind in "cde"]
    for t in range(R):
        centres, exits = [(kind, t + 1) for kind in "cde" if t + 1 < R], [("m", t), ("y", t)]
        turns += exits + centres if CFG["FOLD"][t] else centres + exits
    for kind, t in turns:
        name, keep = exchange(kind, t)
        for q in range(len(T.cores)):
            far = pl[name][q][1].get(core)
            if not far or (kind in "cde" and columns(kind, t)[0] == columns(kind, t)[1]):
                continue
            whole, part, land = pieces(T, kind, t)
            ms = helper_masks(T, topo, core, far)
            g.wait_ge(T.sem["h%s%d" % (kind, t)], counts(T, topo, pl[name], keep)[1][core])
            g.remote_dma_fused([RemoteDMATransfer(dst_ids=[dst(topo, T.cores[o])], dma_engine_mask=bits(m), remote_sem=T.sem["a%s%d" % (kind, t)],
                                                  src=part(o) if part else land(q), dst=land(q)) for o, m in zip(far, ms)],
                               local_sem=T.sem["l%s%d" % (kind, t)])
            ends.append(("l%s%d" % (kind, t), sum(len(m) for m in ms)))
    for sem, n in ends:
        g.wait_ge(T.sem[sem], n)


def place_calls(calls, before, rank, free):
    hop = ticks(CFG["HOP"])
    start, end, busy, banks = [None] * len(calls), [0] * len(calls), {}, [{} for _ in range(8)]

    def place(i):
        e, c, b = calls[i]
        s = free[i]
        for p, delay in before[i]:
            if start[p] is None:
                place(p)
            if end[p] + delay > s:
                s = end[p] + delay
        if e is not None:
            taken = busy.get(e, 0)
            for x in b:
                for ee, mask in banks[x].items():
                    if ee != e:
                        taken |= mask
            taken >>= s
            k = 1
            while k < c and taken:
                step = min(k, c - k)
                taken |= taken >> step
                k += step
            s += (~taken & (taken + 1)).bit_length() - 1
            busy[e] = busy.get(e, 0) | ((1 << c) - 1) << s
            for x in b:
                banks[x][e] = banks[x].get(e, 0) | ((1 << c + 2 * hop) - 1) << s >> hop
        start[i], end[i] = s, s + c
    for i in rank:
        if start[i] is None:
            place(i)
    return start


def ticks(t):
    return int(t / CFG["TICK"] + 0.999)


def replay(case, order):
    hop = CFG["HOP"]
    end, queue, banks = [0.0] * len(case), {}, [{} for _ in range(8)]
    for i in order:
        e, c, b, before = case[i]
        s = queue.get(e, 0.0)
        for p, delay in before:
            if end[p] + delay > s:
                s = end[p] + delay
        for x in b:
            for ee, z in banks[x].items():
                if ee != e and z + hop > s:
                    s = z + hop
        end[i] = s = s + c
        for x in b:
            banks[x][e] = s
        if e is not None:
            queue[e] = s
    return end


def order_calls(calls):
    n = len(calls)
    before, after = [{} for _ in calls], [{} for _ in calls]
    wr, rd = {}, {}
    for i, k in enumerate(calls):
        met = [(wr[x], x) for x in k["r"] + k["w"] if x in wr] + [(p, x) for x in k["w"] for p in rd.get(x, ())]
        for p, x in met:
            if p != i:
                delay = 0.0 if x[0] == "~" or k["e"] == calls[p]["e"] == "P" else calls[p]["lat"] + CFG["HOP"]
                before[i][p] = after[p][i] = max(delay, before[i].get(p, 0.0))
        for x in k["r"]:
            rd.setdefault(x, []).append(i)
        for x in k["w"]:
            wr[x] = i
            rd[x] = []
    above = [0] * n
    for i in range(n):
        for p in before[i]:
            above[i] |= above[p] | 1 << p
        for p in [p for p, d in before[i].items() if d <= CFG["HOP"] and any(above[x] >> p & 1 and before[i][x] >= d for x in before[i])]:
            del before[i][p], after[p][i]
    way = [0.0] * n
    for i in range(n - 1, -1, -1):
        way[i] = calls[i]["c"] + max([way[j] + d for j, d in after[i].items()] + [calls[i]["lat"]])
    last = [i for i in range(n) if not after[i]]
    tails = [0 if after[i] else ticks(k["lat"]) for i, k in enumerate(calls)]
    plain = [(k["e"], ticks(k["c"] * CFG["PLAN"][k["kind"]]), k["b"]) for k in calls]
    ahead, behind = ([[(p, ticks(d)) for p, d in x.items()] for x in side] for side in (before, after))
    cases = [[(k["e"], k["c"] * work[k["kind"]], k["b"], [(p, d * wire if calls[p]["e"] is None else d) for p, d in before[i].items()])
              for i, k in enumerate(calls)] for work, wire, _ in CFG["CASES"]]

    def forward(urgency):
        start = place_calls(plain, ahead, sorted(range(n), key=lambda i: -urgency[i]), [0] * n)
        order = sorted(range(n), key=lambda i: start[i])
        value = 0.0
        for case, (_, _, scale) in zip(cases, CFG["CASES"]):
            end = replay(case, order)
            value += max(end[i] + calls[i]["lat"] for i in last) / scale / len(cases)
        return value, urgency, [s * CFG["TICK"] for s in start], order

    def backward(start):
        back = place_calls(plain, behind, sorted(range(n - 1, -1, -1), key=lambda i: -start[i] - plain[i][1] * CFG["TICK"]), tails)
        return [(back[i] + plain[i][1]) * CFG["TICK"] for i in range(n)]
    state = [CFG["SEED"]]

    def draw():
        state[0] = (state[0] * 6364136223846793005 + 1442695040888963407) % (1 << 64)
        return (state[0] >> 11) / float(1 << 53)
    best = now = forward(way)
    for turn in range(CFG["ROUNDS"]):
        urgency = backward(now[2]) if turn % 3 == 2 else now[1]
        a, width, size = draw() * max(now[2]), 3.0 * 10.0 ** draw(), 0.3 * 20.0 ** draw()
        if draw() < CFG["WHOLE"]:
            i0 = int(draw() * n)
            shift = size * (2 * draw() - 1)
            new = forward([urgency[i] + shift if calls[i]["part"] == calls[i0]["part"] and i >= i0 - 40 * draw() else urgency[i] for i in range(n)])
        else:
            new = forward([urgency[i] + size * (2 * draw() - 1) if a <= now[2][i] < a + width and draw() < 0.3 else urgency[i] for i in range(n)])
        if new[0] <= now[0] + CFG["SLACK"] * (1.0 - turn / CFG["ROUNDS"]) * draw():
            now = new
        if new[0] < best[0]:
            best = new

    lands = [i for i in range(n) if calls[i]["e"] is None]

    def measure(order, first, old, most=1e9, part=None):
        hop, queue, banks, links = CFG["HOP"], {}, [{} for _ in range(8)], []
        for at, i in enumerate(order):
            e, _, b = plain[i]
            if at >= first:
                links.append((i, queue.get(e), [j for x in b for ee, j in banks[x].items() if ee != e]))
            for x in b:
                banks[x][e] = i
            if e is not None:
                queue[e] = i
        value, ends, parts = 0.0, [], []
        for case, (_, _, scale), was in zip(cases, CFG["CASES"], old):
            if part and value + sum(part[len(parts):]) > most + CFG["GIVE"]:
                return None
            end = was[:]
            for i, j, met in links:
                s = end[j] if j is not None else 0.0
                for p, delay in case[i][3]:
                    if end[p] + delay > s:
                        s = end[p] + delay
                for p in met:
                    if end[p] + hop > s:
                        s = end[p] + hop
                end[i] = s + case[i][1]
            ends.append(end)
            parts.append((max(end[i] + calls[i]["lat"] for i in last) + CFG["EARLY"] * sum(end) / n + CFG["LAND"] * sum(end[i] for i in lands) / len(lands)) / scale / len(cases))
            value += parts[-1]
        return value, order, ends, parts

    def waits(order, case, end):
        place = {i: at for at, i in enumerate(order)}
        i, out = max(last, key=lambda j: end[j] + calls[j]["lat"]), []
        if draw() < CFG["MARK"]:
            i = lands[int(draw() * len(lands))]
        while True:
            s = end[i] - case[i][1]
            dep = [p for p, delay in case[i][3] if end[p] + delay > s - 1e-9]
            if dep:
                i = dep[int(draw() * len(dep))]
                continue
            at = place[i] - 1
            while at >= 0:
                j = order[at]
                if end[j] > s - CFG["HOP"] - 1e-9 and (plain[j][0] == plain[i][0] and end[j] > s - 1e-9 or plain[j][0] != plain[i][0] and set(plain[j][2]) & set(plain[i][2])):
                    break
                at -= 1
            if at < 0 or s < 1e-9:
                return out, place
            out.append((order[at], i))
            i = order[at]
    top = now = measure(best[3], 0, [[0.0] * n for _ in cases])
    pairs = None
    for turn in range(CFG["MOVES"]):
        if pairs is None or turn % 16 == 0:
            x = int(draw() * len(cases))
            pairs, place = waits(now[1], cases[x], now[2][x])
        if not pairs:
            pairs = None
            continue
        j = int(draw() * len(pairs))
        if draw() < CFG["NEAR"]:
            j = int(j * draw() * draw())
        v, u = pairs[j]
        while draw() < CFG["FAR"] and j + 1 < len(pairs) and pairs[j + 1][1] == v and not above[u] >> pairs[j + 1][0] & 1:
            j += 1
            v = pairs[j][0]
        if above[u] >> v & 1:
            continue
        a, z = place[v], place[u] + 1
        part = now[1][a:z]
        if draw() < 0.5:
            moved = [i for i in part if i == u or above[u] >> i & 1]
            part = moved + [i for i in part if not (i == u or above[u] >> i & 1)]
        else:
            moved = [i for i in part if i == v or above[i] >> v & 1]
            part = [i for i in part if not (i == v or above[i] >> v & 1)] + moved
        most = now[0] + CFG["HEAT"] * (1.0 - turn / CFG["MOVES"]) * draw()
        new = measure(now[1][:a] + part + now[1][z:], a, now[2], most, now[3])
        if new is None:
            continue
        if new[0] <= most:
            now, pairs = new, None
            if CFG["SORT"]:
                c0, e0 = cases[0], now[2][0]
                at = {i: x for x, i in enumerate(now[1])}
                now = (now[0], sorted(now[1], key=lambda i: (round(e0[i] - c0[i][1], 6), at[i])), now[2], now[3])
        if new[0] < top[0]:
            top = new
    hop = CFG["HOP"]
    follow = [[[] for _ in calls] for _ in cases]
    for case, to in zip(cases, follow):
        for i in range(n):
            for p, d in case[i][3]:
                to[p].append((i, d))
    weight = [1.0 / scale / len(cases) for _, _, scale in CFG["CASES"]]

    def window(order, a, z, heat):
        inside = order[a:z]
        local = {i: x for x, i in enumerate(inside)}
        frame = []
        for case, to in zip(cases, follow):
            end = replay(case, order)
            tail, queue, banks = {}, {}, [{} for _ in range(8)]
            for i in reversed(order[z:]):
                e, c, b, _ = case[i]
                s = max([calls[i]["lat"] if not to[i] else 0.0, queue.get(e, 0.0)] + [d + tail[j] for j, d in to[i]]
                        + [hop + x for y in b for ee, x in banks[y].items() if ee != e])
                tail[i] = s = s + c
                for y in b:
                    banks[y][e] = s
                if e is not None:
                    queue[e] = s
            base, q0, b0 = 0.0, {}, [{} for _ in range(8)]
            for i in order[:a]:
                base = max([base, end[i] + (calls[i]["lat"] if not to[i] else 0.0)] + [end[i] + d + tail[j] for j, d in to[i] if j in tail])
                for y in case[i][2]:
                    b0[y][case[i][0]] = end[i]
                if case[i][0] is not None:
                    q0[case[i][0]] = end[i]
            rows = [(case[i][0], case[i][1], case[i][2], [(local[p], d) for p, d in case[i][3] if p in local],
                     max([0.0] + [end[p] + d for p, d in case[i][3] if p not in local]),
                     max([calls[i]["lat"] if not to[i] else -1e9] + [d + tail[j] for j, d in to[i] if j in tail])) for i in inside]
            frame.append((rows, base, q0, b0, queue, banks))

        def value(seq):
            total, first = 0.0, None
            for (rows, base, q0, b0, q1, b1), w in zip(frame, weight):
                end, queue, banks, most = [0.0] * len(rows), dict(q0), [dict(x) for x in b0], base
                for x in seq:
                    e, c, b, deps, s, out = rows[x]
                    if e in queue and queue[e] > s:
                        s = queue[e]
                    for p, d in deps:
                        if end[p] + d > s:
                            s = end[p] + d
                    for y in b:
                        for ee, u in banks[y].items():
                            if ee != e and u + hop > s:
                                s = u + hop
                    end[x] = s = s + c
                    for y in b:
                        banks[y][e] = s
                    if e is not None:
                        queue[e] = s
                    if s + out > most:
                        most = s + out
                for e, s in queue.items():
                    if e in q1 and s + q1[e] > most:
                        most = s + q1[e]
                for y in range(8):
                    for e, s in banks[y].items():
                        for ee, u in b1[y].items():
                            if ee != e and s + hop + u > most:
                                most = s + hop + u
                total += w * (most + CFG["SOON"] * sum(end) / len(end))
                first = first or end
            return total, seq, first
        laid = []
        for rows, _, q0, b0, _, _ in frame:
            t0 = min(r[4] for r in rows)
            free = [ticks(max([r[4], q0.get(r[0], 0.0)] + [u + hop for y in r[2] for ee, u in b0[y].items() if ee != r[0]]) - t0) for r in rows]
            laid.append(([(r[0], ticks(r[1]), r[2]) for r in rows], [[(p, ticks(d)) for p, d in r[3]] for r in rows], free))
        m = len(inside)
        good = now = value(list(range(m)))
        for _ in range(CFG["TRIES"]):
            size, share, i0 = 0.15 * 20.0 ** draw(), 0.4 * draw() ** 2 + 0.02, int(draw() * m)
            key = [now[2][x] - frame[0][0][x][1] for x in range(m)]
            if draw() < CFG["WHOLE"]:
                shift = size * (2 * draw() - 1)
                key = [key[x] + shift if calls[inside[x]]["part"] == calls[inside[i0]]["part"] and draw() < 0.8 else key[x] for x in range(m)]
            else:
                key = [key[x] + size * (2 * draw() - 1) if draw() < share else key[x] for x in range(m)]
            work, deps, free = laid[int(draw() * len(laid))]
            start = place_calls(work, deps, sorted(range(m), key=lambda x: key[x]), free)
            new = value(sorted(range(m), key=lambda x: (start[x], work[x][1] > 0)))
            if new[0] <= now[0] + heat * draw():
                now = new
            if new[0] < good[0]:
                good = new
        return order[:a] + [inside[x] for x in (now if heat > CFG["COLD"] else good)[1]] + order[z:]
    order = top[1]
    for turn in range(CFG["LOOKS"]):
        m = int(CFG["WIDE"] * (0.6 + 0.8 * draw()))
        a = max(0, min(n - m, int(draw() * (n + m // 2)) - m // 2))
        order = window(order, a, a + m, max(CFG["COLD"], CFG["WARM"] * (1.0 - 1.3 * turn / CFG["LOOKS"])))
        end = replay(cases[0], order)
        at = {i: x for x, i in enumerate(order)}
        order.sort(key=lambda i: (round(end[i] - cases[0][i][1], 6), at[i]))
    top = measure(order, 0, [[0.0] * n for _ in cases])
    best = (top[0], None, None, top[1])
    end = replay(cases[0], best[3])
    ORDER["plan"] = (best[0], [(k["e"], end[i] - k["c"], k["c"], (k["w"] + k["r"])[0]) for i, k in enumerate(calls)],
                     [round(max(x[i] + calls[i]["lat"] for i in last), 1) for x in (replay(case, best[3]) for case in cases)])
    return best[3]


def rank_program(g, core, T, topo):
    pl = plans(T, topo)
    q = T.rank_of(core)
    if q is None:
        helper_program(g, core, T, topo, pl)
        return
    Q = {"V": g.vector, "S": g.scalar, "P": g.tensor, "G": g, "Y": g.sync}
    V, S, PE = g.vector, g.scalar, g.tensor
    known = {e: {} for e in Q}
    count, wr, rd, bank = {}, {}, {}, {}
    calls, stage = [], [0]

    def need(e, tok):
        sem, val, clock = tok
        if known[e].get(sem, 0) >= val:
            return
        Q[e].wait_ge(T.sem[sem], val)
        known[e][sem] = val
        for s, v in clock.items():
            if known[e].get(s, 0) < v:
                known[e][s] = v

    def issue(k):
        e, r, w, b, sem = k["e"], k["r"], k["w"], k["b"], k["sem"]
        if e is None:
            count[sem] = k["total"]
            for x in w:
                wr[x] = (sem, k["total"], {})
            return
        toks = [wr[x] for x in r if x in wr] + [wr[x] for x in w if x in wr]
        for x in w:
            toks += rd.get(x, [])
        for x in b:
            toks += [tk for ee, tk in bank.get(x, {}).items() if ee != e]
        toks.sort(key=lambda tk: -tk[1])
        for tk in toks:
            if not (e == "P" and tk[0] == "qP"):
                need(e, tk)
        res = k["fn"]()
        if sem is None:
            sem = "q" + e
            for x in res if isinstance(res, list) else [res]:
                x.then_inc(T.sem[sem], 1)
        count[sem] = max(count.get(sem, 0) + k["inc"], k["total"] or 0) if k["total"] is None else k["total"]
        tok = (sem, count[sem], dict(known[e]))
        for x in r:
            rd.setdefault(x, []).append(tok)
        for x in w:
            if x[0] != "~":
                wr[x] = tok
                rd[x] = []
        for x in b:
            bank.setdefault(x, {})[e] = tok

    def op(e, fc, r=(), w=(), b=(), sem=None, inc=1, total=None, lat=0.0):
        c, kind = fc[1] if isinstance(fc[1], tuple) else (fc[1], 3 if sem else 4 if e == "P" else 0)
        calls.append(dict(e=e, fn=fc[0], c=c, kind=kind, part=stage[0], r=list(r), w=list(w), b=tuple(b), sem=sem, inc=inc, total=total, lat=lat))

    def run(e, fcs, r=(), w=(), b=()):
        op(e, (lambda: [fc[0]() for fc in fcs], sum(fc[1] for fc in fcs)), r, w, b, inc=len(fcs))

    def dma(e, pairs, sem, r=(), w=(), total=None, lat=2.0):
        def fn():
            for o, i in pairs:
                Q[e].dma_start(o, i).then_inc(T.sem[sem], 16)
        op(e, (fn, 0.1 * len(pairs)), r, w, sem=sem, inc=16 * len(pairs), total=total, lat=lat)

    def rows(out, a, sem, r, w, add=True, first=False):
        kw = dict(accum_op=OP.add) if add else {}
        op("G", (lambda: g.dma_start(out, a, max_dma_last_dim=4096, **kw).then_inc(T.sem[sem], 16), CFG["GD"][0 if first else 1]),
           r, w, sem=sem, inc=16, lat=CFG["GD"][2])

    CYC = 0.00087

    def us(n):
        return max(n, 64) * CYC

    def got(n):
        return 0.06 + 1.56 * n * CYC, 1

    def put(n):
        return 0.05 + 3.8 * n * CYC, 2

    def ts(out, in0, s1, s2, o0, o1=None, c=us(0)):
        if o1 is None:
            return lambda: V.tensor_scalar(out, in0, s1, None, o0), c
        return lambda: V.tensor_scalar(out, in0, s1, s2, o0, o1), c

    def tt(out, a, b, o, c=us(0)):
        return lambda: V.tensor_tensor(out, a, b, o), c

    def cp(out, a, c=us(0)):
        return lambda: V.tensor_copy(out, a), c

    def fill(out, x, c=us(0)):
        return lambda: V.memset(out, x), c

    def scan(out, a, b, c):
        return lambda: V.tensor_tensor_scan(out, a, b, 0.0, OP.mult, OP.add), c

    def act(out, a, f, c=us(0), **kw):
        return lambda: S.activation(out, a, f, **kw), c

    def mm(items, n=64, more=0, start=True, stop=True):
        def fn():
            for j, (o, l, x) in enumerate(items):
                res = PE.matmul(o, l, x, start and j == 0, stop and j == len(items) - 1)
            return res
        return fn, (len(items) * max(n, 64) + more) * CYC / 2

    W1, WM2, W8192, WM4096, W4096, WJ, WE, WT, WY, WM1 = range(10)

    def sel(out, wi, src):
        return [(out, T.WS[:, 144 * wi + 15 - r:144 * wi + 143 - r], src(r)) for r in range(16)]

    def iota(out, pat, base, name, n, ch=0):
        op("G", (lambda: g.iota(out, pat, base, ch, allow_small_or_imprecise_dtypes=True), 0.13 + 2 * n * CYC), r=["~0"] * (name != "COL"), w=[name])

    def pass_on(out, a, n):
        return lambda: g.affine_select(out, a, [[0, n]], OP.is_ge, 0.0, 0, 0), 0.17 + 2 * n * CYC

    def wf(j):
        return T.WF[:, 32 * j:32 * j + 32]

    def wi_(j):
        return T.WI[:, 32 * j:32 * j + 32]

    def wu(j):
        return T.WU[:, 32 * j:32 * j + 32]

    def pf(j):
        return T.PF[:, j:j + 1]

    HW = [T.HW0, T.HW1]
    CA = [T["CA%d" % t] for t in range(R)]

    def send(kind, t, name, landed, src=None):
        plan, keep = exchange(kind, t)
        name = name if isinstance(name, list) else [name]
        near, hs = pl[plan][q]
        m1, m2 = masks(T, topo, pl[plan], q, keep)
        whole, part, land = pieces(T, kind, t)
        a, h_, l = ("%s%s%d" % (x, kind, t) for x in "ahl")
        tr = [RemoteDMATransfer(dst_ids=[dst(topo, T.cores[o])], dma_engine_mask=bits(m), remote_sem=T.sem[a],
                                src=src if part is None else part(o), dst=land(q)) for o, m in zip(near, m1)]
        tr += [RemoteDMATransfer(dst_ids=[dst(topo, h)], dma_engine_mask=bits(m), remote_sem=T.sem[h_], src=src if part is None else whole,
                                 dst=land(q) if part is None else whole) for h, m in zip(hs, m2)]
        chain = ["~" + kind] + ["~h%d" % i for i, h in enumerate(topo.cores_of(core)) if h in hs]
        first = kind == "c" and t == 0
        op("G", (lambda: g.remote_dma_fused(tr, local_sem=T.sem[l]), 3.5 if first else 0.45), r=name, w=chain + ["~s" + a] + (["~0"] if kind in "cde" and t == 0 else []),
           sem=l, inc=sum(len(m) for m in m1 + m2))
        total = counts(T, topo, pl[plan], keep)[0][q]
        got_ = ["~s" + a]
        if part is not None:
            total += 16
            dma("Y", [(land(q), part(q))], a, r=name, w=["~o" + a], total=total)
            got_.append("~o" + a)
        op(None, (None, 0.0), r=got_, w=[landed], sem=a, total=total, lat=(CFG["LC0"] - 3.05 if first else CFG["L" + kind + str(min(t, 1))] if kind in "cde" else CFG[plan] + 0.2 * (kind == "y")) - 0.45)

    def parts(t):
        return [(kind,) + columns(kind, t) for kind in "cde" if columns(kind, t)[0] < columns(kind, t)[1]]

    def centre(p):
        return ["C%dc" % p, "C%dd" % p]

    own0 = CA[0][:, 512 * q:512 * q + 512]
    dma("Y", [(own0, T.cen[:])], "lcen", w=["cen", "~ld"])
    dma("Y", [(T.EI[:], T.ent[:])], "lent", w=["EI", "~ld"], lat=2.3)
    dma("Y", [(T.XB[:], T.wk[:])], "lwk", w=["Xc", "Xd", "~ld"], lat=2.6)
    dma("Y", [(T.ZW[:, 0:2048], T.pl[:])], "lpl", w=["Z", "~ld"], lat=3.7)
    dma("Y", [(T.JT[:], T.jmp[:])], "ljt", w=["JT", "~ld"], lat=3.9)
    dma("Y", [(T.HW0[:, 4096:4608], T.cen[:])], "lown", w=centre(0) + ["~ld"], lat=4.1)
    dma("Y", [(T.NBI[:], T.nb[:])], "lnb", w=["NBI", "~ld"], lat=4.7)
    for kind, a, z in parts(0):
        send(kind, 0, "cen", "CA0" + kind, src=CA[0][:, 512 * q + a:512 * q + z])
    op("G", (lambda: g.iota(T.PI[:, 0:1], [[0, 1]], 0, 1), 0.13), w=["PI0"])
    iota(T.COL[:], [[1, 144]], 0, "COL", 144)
    op("G", (lambda: g.iota(T.LJ[:], [[16, 16], [0, 2]], 0, 0), 0.19), w=["LJ"])
    iota(T.TA[:], [[16, 8], [0, 16]], 0, "TA", 128)
    iota(T.CT[:], [[0, 8], [1, 32]], 0, "CT", 256)
    iota(T.C8[:], [[0, 8], [8, 32]], 0, "C8", 256)
    iota(T.KX[:], [[2, 4], [-1, 2], [0, 32]], 1, "KX", 256)
    iota(T.KHI[:], [[256, 8], [0, 32]], 2048, "KHI", 256)
    for j in range(8):
        if j < CFG["MTZ"]:
            op("V", fill(T.MT[:, 512 * j:512 * j + 512], 0.0, us(256)), w=["MT%d" % j])
        else:
            iota(T.MT[:, 512 * j:512 * j + 512], [[0, 512]], 0, "MT%d" % j, 512)
    iota(T.S48[:], [[0, 8], [1, 48]], 0, "S48", 384)
    iota(T.P1[:], [[0, 3], [1, 128]], 0, "P1", 384)
    iota(T.P2[:], [[128, 3], [0, 128]], 0, "P2", 384)
    iota(T.JF[:], [[1, 384]], 0, "JF", 384)
    for j in range(8):
        if CFG["EWZ"] == "V":
            op("V", fill(T.EW[:, 512 * j:512 * j + 512], 0.0, us(256)), w=["EW%d" % j])
        else:
            iota(T.EW[:, 512 * j:512 * j + 512], [[0, 512]], 0, "EW%d" % j, 512)

    def pm(j):
        return T.PM[:, j:j + 1]
    run("V", [ts(T.PI[:, j:j + 1], T.PI[:, 0:1], x, None, OP.bitwise_and) for j, x in ((1, 15), (2, 112), (3, 31))], r=["PI0"], w=["PI1"])
    op("V", cp(T.PF[:, 0:4], T.PI[:, 0:4]), r=["PI0", "PI1"], w=["PF0"])
    run("V", [fill(T.B7[:, 224:225], 0.0), fill(T.THR[:, 32:64], 2.0 ** 25), fill(T.GO[:, 32:64], -9.0), fill(T.HW0[:, 5120:5136], 0.0),
              fill(T.HW1[:, 5120:5136], 0.0)], w=["AP", "thr1", "nine", "zero0", "zero1"], b=[7])
    run("V", [ts(pf(10), pf(2), 15.0, None, OP.add), ts(pf(9), pf(1), 2.0, 1.0, OP.mult, OP.add)], r=["PF0"], w=["PF10", "PF9"])
    op("V", ts(T.PM[:], T.COL[:, 0:16], pf(1), None, OP.is_equal), r=["PF0", "COL"], w=["PM"])
    op("V", ts(T.WS[:, 0:144], T.COL[:], pf(10), None, OP.is_equal, c=us(144)), r=["PF10", "COL"], w=["WS0"])
    op("V", ts(T.ID[:], T.COL[:, 0:128], pf(0), None, OP.is_equal, c=us(128)), r=["PF0", "COL"], w=["ID"])

    def weights(j, s, deps=()):
        op("V", ts(T.WS[:, 144 * j:144 * j + 144], T.WS[:, 0:144], s, None, OP.mult, c=us(72)), r=["WS0"] + list(deps), w=["WS%d" % j])

    def scaled_identity(name, s, deps=()):
        op("V", ts(T[name][:], T.ID[:], s, None, OP.mult, c=us(128 if SCRATCH[name][2] == F32 else 64)), r=["ID"] + list(deps), w=[name])
    for name, s in (("NID", -1.0), ("I32", 1.0), ("IS", -4096.0), ("IH", 0.5), ("I512", 512.0), ("I16", 16.0)):
        scaled_identity(name, s)
    scaled_identity("D0", pm(0), ["PM"])
    scaled_identity("D1", pm(1), ["PM"])
    weights(WJ, pf(9), ["PF9"])
    for j, s in ((WM2, -2.0), (W8192, 8192.0), (WM4096, -4096.0), (W4096, 4096.0)):
        weights(j, s)
    op("V", fill(T.ONE[:], 1.0, us(256)), w=["ONE"])
    op("V", fill(T.M8[:], 1.0, us(256)), w=["M8"])
    op("V", fill(T.M32[:], 1.0, us(128)), w=["M32"])
    op("V", fill(T.M8[:, 0:256:8], 0.0), w=["M8"])
    op("V", fill(T.M32[:, 0:256:32], 0.0), w=["M32"])
    op("V", ts(pf(11), pf(1), 256.0, None, OP.mult), r=["PF0"], w=["PF11"])
    op("V", ts(pf(4), pf(1), 2.0, None, OP.is_lt), r=["PF0"], w=["PF4"])
    op("V", ts(pf(5), pm(2), -512.0, pf(4), OP.mult, OP.add), r=["PF4", "PM"], w=["PF5"])
    op("V", ts(pf(15), pm(3), 512.0, pf(5), OP.mult, OP.add), r=["PF5", "PM"], w=["PF15"])
    op("V", ts(pf(16), pm(5), 16.0, pm(4), OP.mult, OP.add), r=["PM"], w=["PF16"])
    op("V", ts(pf(14), pm(2), 2048.0, pf(4), OP.mult, OP.add), r=["PF4", "PM"], w=["PF14"])
    op("V", ts(pf(17), pm(1), float(64 * q), None, OP.mult), r=["PM"], w=["PF17"])
    op("V", ts(pf(18), pm(3), 8.0, pf(17), OP.mult, OP.add), r=["PM", "PF17"], w=["PF18"])
    op("V", ts(pf(19), pm(5), 32.0, pf(18), OP.mult, OP.add), r=["PM", "PF18"], w=["PF19"])
    op("V", ts(wf(0), T.COL[:, 0:32], 16.0, pf(1), OP.mult, OP.add), r=["PF0", "COL"], w=["m"])
    op("V", ts(wf(1), wf(0), 4608.0, None, OP.add), r=["m"], w=["my"])
    weights(WT, pf(15), ["PF15"])
    weights(WY, pf(16), ["PF16"])
    weights(WE, pf(14), ["PF14"])
    op("V", ts(T.GRP[:], T.TA[:], pf(2), None, OP.is_equal), r=["TA", "PF0"], w=["GRP"])
    op("V", ts(T.TB[:], T.TA[:], pf(2), -1.0, OP.is_equal, OP.mult), r=["TA", "PF0"], w=["TB"])
    op("G", (lambda: g.affine_select(T.NUP[:], T.TB[:], [[-1, 128]], OP.is_ge, 0.0, 0, 1), 0.17 + 256 * CYC), r=["TB"], w=["NUP"])

    def two_parts(whole, name, lo, hi):
        op("S", act(T[lo][:], whole, AF.Copy, us(256)), r=[name], w=[lo])
        op("P", mm([(T.B7[:, 256:512], T.I32[:], whole), (T.B7[:, 256:512], T.NID[:], T[lo][:])], 256, more=768), r=[name, lo, "I32", "NID"], w=["left"], b=[7])
        op("S", act(T[hi][:], T.B7[:, 256:512], AF.Copy, us(256)), r=["left"], w=[hi], b=[7])
    op("V", cp(T.NL[:], T.NBI[:], us(256)), r=["NBI"], w=["NL"])
    op("V", ts(T.N1[:], T.NBI[:], 9, None, OP.arith_shift_right, c=us(256)), r=["NBI"], w=["N1"])
    op("V", cp(T.OWN[:], T.N1[:], us(256)), r=["N1"], w=["OWN"])
    op("V", tt(T.KLO[:], T.OWN[:], T.C8[:], OP.add, us(256)), r=["OWN", "C8"], w=["KLO"])
    op("V", cp(T.NF[:], T.NBI[:], us(256)), r=["NBI"], w=["NF"])
    two_parts(T.NF[:], "NF", "TLO", "THI")
    op("S", act(T.RT[:], T.CT[:], AF.Identity, us(256), bias=pf(1), scale=0.0), r=["CT", "PF0"], w=["RT"])
    dma("Y", [(T.MT[f:128:16, :], x[:]) for f, x in enumerate((T.TLO, T.THI, T.OWN, T.KX, T.RT, T.CT))], "dmt",
        r=["TLO", "THI", "OWN", "KX", "RT", "CT"], w=["MT"] + ["MT%d" % j for j in range(8)], lat=2.6)
    op("V", ts(T.LU[:, 48:80], T.LJ[:], pf(1), None, OP.add), r=["PF0", "LJ"], w=["LU3"])
    op("V", ts(pf(8), pf(1), 31.0, pf(3), OP.mult, OP.add), r=["PF0"], w=["PF8"])
    op("V", ts(T.LU[:, 80:96], T.COL[:, 0:16], pf(8), None, OP.add), r=["PF8", "COL"], w=["LU4"])
    op("V", cp(T.EF[:], T.EI[:], us(256)), r=["EI"], w=["EF"])
    op("V", cp(T.EX[:, 0:256], T.EI[:, 0:256].indirect(T.LU[:, 48:64]), got(256)), r=["EI", "LU3"], w=["EX0"])
    op("S", act(T.EX[:, 256:512], T.EF[:, 0:256].indirect(T.LU[:, 64:80]), AF.Copy, got(256)), r=["EF", "LU3"], w=["EX1"])
    for j in range(2):
        op("V", (lambda j=j: V.transpose(T.ET[:, 256 * j:256 * j + 256], T.EX[:, 256 * j:256 * j + 256]), us(256)), r=["EX%d" % j], w=["ET%d" % j])
    for a, z in ((0, 2), (2, 4)):
        op("V", cp(T.EG[:, 64 * a:64 * z], T.ET[:, 0:512].indirect(T.LU[:, 80 + 4 * a:80 + 4 * z]), got(128)), r=["ET0", "ET1", "LU4"], w=["EG%d" % a])
        op("V", cp(T.EU[:, 64 * a:64 * z], T.EG[:, 64 * a:64 * z], us(128)), r=["EG%d" % a], w=["EU%d" % c for c in range(a, z)])
    two_parts(T.EF[:], "EF", "ELO", "EHI")
    dma("Y", [(T.EW[0:128:16, 0:4096], T.ELO[:]), (T.EW[1:128:16, 0:4096], T.EHI[:])], "dew", r=["ELO", "EHI"],
        w=["EW"] + ["EW%d" % j for j in range(8)], lat=2.6)
    dma("Y", [(T.yn[:], T.ONE[:, 0:256])], "on", r=["ONE"], w=["yn"])
    op("V", ts(T.PF[:, 20:23], T.COL[:, 0:3], 384.0, pm(1), OP.mult, OP.mult), r=["COL", "PM"], w=["PF20"])
    op("V", tt(T.PF[:, 20:23], T.PF[:, 20:23], T.PM[:, 3:6], OP.add), r=["PF20", "PM"], w=["PF20"])
    op("V", ts(T.PF[:, 20:23], T.PF[:, 20:23], pm(2), None, OP.add), r=["PF20", "PM"], w=["PF20"])
    op("V", ts(pf(23), pm(0), 384.0 * (R - 1), pm(8), OP.mult, OP.add), r=["PM"], w=["PF23"])
    op("S", act(T.SE[:], T.S48[:], AF.Identity, us(384), bias=pf(19), scale=pm(0)), r=["S48", "PF19", "PM"], w=["SE"])
    op("S", act(T.VF[:], T.JF[:], AF.Identity, us(384), bias=pf(23), scale=pm(0)), r=["JF", "PF23", "PM"], w=["VT%d" % (R - 1)])

    def values():
        op("P", mm([(T.B2[:, 0:384], T.D0[:], T.P1[:]), (T.B2[:, 0:384], T.D1[:], T.P2[:])], 384), r=["D0", "D1", "P1", "P2"], w=["B2"], b=[2])
        op("S", act(T.VB[:], T.B2[:, 0:384], AF.Copy, us(384)), r=["B2"], w=["VB"], b=[2])
        for t in range(R - 1):
            op("V", ts(T.VT[:, 384 * t:384 * t + 384], T.VB[:], pf(20 + t), None, OP.add, c=us(192)), r=["VB", "PF20"], w=["VT%d" % t])

    def most(out, a, b, j, r, w):
        if CFG["PB"]:
            op("V", tt(out, a, T.B1[:, 512 * j:512 * j + 512], OP.max, (us(256), 5)), r=r + [("Cp", "Yp")[j]], w=[w], b=[1])
        else:
            op("V", tt(out, a, b, OP.max, us(512)), r=r, w=[w])

    def jump(t):
        H, p = HW[t % 2], t % 2
        C, Y, c_, y_ = H[:, 4096:4608], H[:, 4608:5120], centre(p), "Y%d" % p
        op("P", mm(sel(T.B7[:, 0:32], WJ, lambda r: T.XB[:, r:512:16])), r=["Xc", "Xd", "WS5"], w=["jP"], b=[7])
        op("V", cp(wi_(0), T.B7[:, 0:32]), r=["jP"], w=["ji"], b=[7])
        op("V", ts(wi_(1), wi_(0), 511, None, OP.bitwise_and), r=["ji"], w=["ja"])
        op("V", cp(wu(0), wi_(1)), r=["ja"], w=["ju"])
        if CFG["JV"][t]:
            op("V", tt(T.JG[:], T.JT[:, 0:512].indirect(wu(0)), T.XB[:], OP.subtract, got(512)), r=["JT", "ju", "Xc", "Xd"], w=["JG"])
            op("S", act(Y, T.JG[:], AF.Abs, us(512)), r=["JG"], w=[y_])
        else:
            op("S", act(T.JG[:], T.JT[:, 0:512].indirect(wu(0)), AF.Copy, got(512)), r=["JT", "ju"], w=["JG"])
            op("P", mm([(T.B2[:], T.ID[:], T.XB[:]), (T.B2[:], T.NID[:], T.JG[:])], 512), r=["Xc", "Xd", "JG", "ID", "NID"], w=["B2"], b=[2])
            op("S", act(Y, T.B2[:], AF.Abs, us(512)), r=["B2"], w=[y_], b=[2])
        if CFG["PB"]:
            op("V", cp(T.B1[:, 0:512], C, us(256)), r=c_, w=["Cp"], b=[1])
            op("V", cp(T.B1[:, 512:1024], Y, us(256)), r=[y_], w=["Yp"], b=[1])
        op("P", mm(sel(T.B7[:, 160:224], W1, lambda r: H[:, 4096 + r:5120:16])), r=c_ + [y_, "WS0"], w=["SyP"], b=[7])
        run("S", [act(T.SC2[:, 32:96], T.B7[:, 160:224], AF.Copy), act(T.SC2[:, 0:32], T.B7[:, 160:192], AF.Copy),
                  act(T.SC2[:, 96:128], T.B7[:, 192:224], AF.Copy)], r=["SyP"], w=["SC"], b=[7])
        if CFG["OWN"][t] in "SW":
            if CFG["OWN"][t] == "W":
                op("V", tt(T.CM[:], Y, T.B1[:, 0:512], OP.subtract, (us(256), 5)), r=["Cp", y_], w=["CMc", "CMd"], b=[1])
                op("S", act(T.OA[:], T.CM[:], AF.Abs, us(512)), r=["CMc"], w=["OA"])
            else:
                op("P", mm([(T.B2[:], T.ID[:], C), (T.B2[:], T.NID[:], Y)], 512), r=c_ + [y_, "ID", "NID"], w=["B2"], b=[2])
                op("S", act(T.OA[:], T.B2[:], AF.Abs, us(512)), r=["B2"], w=["OA"], b=[2])
            op("P", mm([(T.B7[:, 64:96], T.ID[:], T.C8[:, 0:32])] + sel(T.B7[:, 64:96], W4096, lambda r: T.OA[:, r:512:16])), r=["OA", "WS4", "C8", "ID"], w=["ownP"], b=[7])
        else:
            most(T.OA[:], Y, C, 0, c_ + [y_], "OA")
            sums = [(T.B7[:, 64:96], T.IS[:], T.SC2[:, 32:64]), (T.B7[:, 64:96], T.IS[:], T.SC2[:, 64:96])]
            op("P", mm(sums + sel(T.B7[:, 64:96], W8192, lambda r: T.OA[:, r:512:16]), more=384), r=["OA", "WS2", "IS", "SC"], w=["ownP"], b=[7])
        op("V", cp(T.UI[:, 0:33], T.B7[:, 192:225]), r=["SyP", "AP"], w=["ui"], b=[7])
        op("V", ts(T.UI[:, 40:73], T.UI[:, 0:33], 63, None, OP.bitwise_and), r=["ui"], w=["ua"])
        op("V", ts(T.UF[:, 0:33], T.UI[:, 40:73], 1.0 / 64, None, OP.mult), r=["ua"], w=["u64"])
        op("S", act(pf(12), T.UF[:, 32:33], AF.Copy, scale=-4096.0 * 64), r=["u64"], w=["A"])
        op("S", act(T.THR[:, 0:32], T.B7[:, 64:96], AF.Identity, bias=pf(12)), r=["ownP", "A"], w=["thr0"], b=[7])

    wide = [0]

    def difference(a, b, r):
        wide[0] = bk = 2 if CFG["PB"] else 3 - wide[0] if wide[0] else 1
        out = T["B%d" % bk][:]
        op("P", mm([(out, T.ID[:], a), (out, T.NID[:], b)], 512), r=r + ["ID", "NID"], w=["B%d" % bk], b=[bk])
        return out, "B%d" % bk, bk

    def span(c, ks):
        return 512 * ks[0], 512 * ks[-1] + 512, 32 * ks[0], 32 * ks[-1] + 32

    def entries(t):
        H, p = HW[t % 2], t % 2
        kinds = CFG["H"][t]
        for k in range(8):
            c = k // 2
            src = T.ZW[:, 0:2048 + 384 * t].indirect(T.EU[:, 32 * k:32 * k + 32])
            dep = ["Z", "EU%d" % c] + ["L%d" % u for u in range(t)]
            s_, sk, mh = H[:, 512 * k:512 * k + 512], "s%d_%d" % (p, k), T.MH[:, 512 * k:512 * k + 512]
            both = kinds[2 * c:2 * c + 2] == "TT"
            if kinds[k] == "V":
                op("V", cp(s_, src, got(512)), r=dep, w=[sk])
            elif both and k % 2 == 0:
                op("S", act(H[:, 512 * k:512 * k + 1024], T.ZW[:, 0:2048 + 384 * t].indirect(T.EU[:, 32 * k:32 * k + 64]), AF.Copy, got(1024)),
                   r=dep, w=[sk, "s%d_%d" % (p, k + 1)])
            elif not both:
                op("S", act(s_, src, AF.Copy, got(512)), r=dep, w=[sk])
            if kinds[k] == "E":
                d, d_, bk = difference(s_, H[:, 4096:4608], centre(p) + [sk])
                op("S", act(mh, d, AF.Abs, us(512), scale=0.5), r=[d_], w=["MH%d" % k], b=[bk])
            else:
                most(mh, s_, H[:, 4096:4608], 0, [sk] + centre(p), "MH%d" % k)
            if k % 2:
                bk = 5 * (c % 2)
                B, free = T["B%d" % bk], ["G%d" % ((c + 2) % 4)]
                out = B[:, 64 * c:64 * c + 64]
                ks = [x for x in (k - 1, k) if kinds[x] != "E"]
                if ks:
                    a, z, x0, x1 = span(c, ks)
                    head = [(out, T.NID[:], T.ONE[:, 0:64])] if len(ks) == 1 else []
                    op("P", mm(head + sel(B[:, x0:x1], W1, lambda r, a=a, z=z: H[:, a + r:z:16]), stop=False),
                       r=["WS0", "NID", "ONE"] + ["s%d_%d" % (p, x) for x in ks] + free, w=["G%d" % c], b=[bk])
                sc = [(B[:, x0:x1], T.I32[:], T.SC2[:, 64 - 32 * len(ks):64])] if ks else []
                op("P", mm(sc + sel(out, WM2, lambda r, c=c: T.MH[:, 1024 * c + r:1024 * c + 1024:16]), more=192 * len(sc), start=not ks),
                   r=["WS1", "SC", "SC0", "I32", "MH%d" % (k - 1), "MH%d" % k] + free, w=["G%d" % c], b=[bk])
                op("S", act(T.RG[:, 64 * c:64 * c + 64], out, AF.Relu, bias=2047.0 + (len(ks) == 1)), r=["G%d" % c], w=["RG%d" % c], b=[bk])

    def flux(t):
        if CFG["FX"] == "V":
            if t:
                op("V", tt(T.FN[:], T.FN[:] if t > 1 else T.ONE[:, 0:256], T.SG[:, 0:256], OP.add, us(256)), r=["n", "ONE", "SG%d" % (t - 1)], w=["n"])
            return
        n = T.B6[:, 256:512]
        items = [(n, T.ID[:], T.ONE[:, 0:256])] * (1 + t // 2) + [(n, T.IH[:], T.ONE[:, 0:256])] * (t % 2)
        items += [(n, T.IH[:], T.SG[:, 256 * u:256 * u + 256]) for u in range(t)]
        op("P", mm(items, 256), r=["IH", "ID", "ONE"] + ["SG%d" % u for u in range(t)], w=["n"], b=[6])

    def neighbours(t):
        H, p = HW[t % 2], t % 2
        Y, y_ = H[:, 4608:5120], "Y%d" % p
        dep = ["CA%dc" % t, "CA%dd" % t, "CA%de" % t, "NL", "cen" if t == 0 else "CAown"]
        for c in range(4):
            bk = 3 + c % 2
            B = T["B%d" % bk]
            out = B[:, 64 * c:64 * c + 64]
            head, tail = ([(out, T.ID[:], x[:, 64 * c:64 * c + 64])] for x in (T.KHI, T.KLO))
            free = ["KD%d" % (c - 2)] if c > 1 else ["pf", "mP"]
            for k in (2 * c, 2 * c + 1):
                kind = CFG["D"][t][k]
                src = CA[t][:, 0:4096].indirect(T.NL[:, 32 * k:32 * k + 32])
                ag, mx = T.AG[:, 512 * k:512 * k + 512], T.MX[:, 512 * k:512 * k + 512]
                if kind in "CT":
                    if kind == "C":
                        op("S", act(ag, src, AF.Copy, got(512)), r=dep, w=["AG%d" % k])
                    elif k % 2 == 0:
                        op("S", act(T.AG[:, 512 * k:512 * k + 1024], CA[t][:, 0:4096].indirect(T.NL[:, 32 * k:32 * k + 64]), AF.Copy, got(1024)),
                           r=dep, w=["AG%d" % k, "AG%d" % (k + 1)])
                    most(mx, ag, Y, 1, ["AG%d" % k, y_], "MX%d" % k)
                elif kind == "E":
                    op("S", act(ag, src, AF.Copy, got(512)), r=dep, w=["AG%d" % k])
                    d, d_, db = difference(ag, Y, ["AG%d" % k, y_])
                    op("S", act(mx, d, AF.Abs, us(512), scale=0.5), r=[d_], w=["MX%d" % k], b=[db])
                else:
                    op("V", tt(ag, src, Y, OP.subtract, got(512)), r=dep + [y_], w=["AG%d" % k])
                    if kind == "A":
                        op("S", act(mx, ag, AF.Abs, us(512), scale=0.5), r=["AG%d" % k], w=["MX%d" % k])
                    else:
                        op("V", ts(mx, ag, 0.0, None, OP.max, c=us(256)), r=["AG%d" % k], w=["MX%d" % k])
            mxs = ["MX%d" % (2 * c), "MX%d" % (2 * c + 1)]
            ks = [k for k in (2 * c, 2 * c + 1) if CFG["D"][t][k] in "CTR"]
            if ks:
                a, z, x0, x1 = span(c, ks)
                cs = [k for k in ks if CFG["D"][t][k] in "CT"]
                sy = [(B[:, 32 * cs[0]:32 * cs[-1] + 32], T.IS[:], T.SC2[:, 64:64 + 32 * len(cs)])] if cs else []
                op("P", mm(head + sy + sel(B[:, x0:x1], WM4096, lambda r, a=a, z=z: T.AG[:, a + r:z:16]), more=192 * len(sy), stop=False),
                   r=["IS", "SC", "SC3", "WS3", "KHI", "C8", "ID"] + ["AG%d" % k for k in ks] + free, w=["KD%d" % c], b=[bk])
                head = []
            op("P", mm(head + sel(out, W8192, lambda r, c=c: T.MX[:, 1024 * c + r:1024 * c + 1024:16]) + tail, start=not ks),
               r=["WS2", "KHI", "KLO", "ID"] + mxs + free, w=["KD%d" % c], b=[bk])
            op("V", tt(T.RUN[:], T.THR[:] if c == 0 else T.RUN[:], out, OP.min), r=["thr0", "thr1", "RUN", "KD%d" % c], w=["RUN"], b=[bk])
        op("V", tt(wi_(4), T.RUN[:, 0:32], T.RUN[:, 32:64], OP.min), r=["RUN"], w=["kz"])

    def choice(t):
        n, at = (T.B6, 256) if CFG["FX"] == "P" else (T.FN if t else T.ONE, 0)
        for c in range(4):
            run("V", [tt(T.G2[:, k:256:8], T.RG[:, 32 * k:32 * k + 32], n[:, at + 32 * k:at + 32 * k + 32], OP.mult) for k in (2 * c, 2 * c + 1)],
                r=["RG%d" % c, "n", "ONE"], w=["G2_%d" % c], b=[6] * (at > 0))
        op("V", scan(T.PP[:], T.M8[:], T.G2[:], us(256)), r=["M8"] + ["G2_%d" % c for c in range(4)], w=["PP"])
        fold = CFG["FOLD"][t]
        if fold:
            op("V", tt(T.GO[:, 0:32], wi_(4), T.THR[:, 0:32], OP.is_ge), r=["kz", "thr0"], w=["go"])
            op("V", tt(wf(2), T.UF[:, 0:32], T.GO[:, 0:32], OP.max), r=["u64", "go"], w=["uf"])
        run("V", [tt(T.B0[:, 256 + j:320:2], T.PP[:, 7:256:8], wf(2) if fold else T.UF[:, 0:32], OP.mult) for j in range(2)], r=["PP", "u64", "uf"], w=["th"], b=[0])
        run("V", [tt(T.NC[:, 64 * k:64 * k + 64], T.PP[:, k:256:4], T.B0[:, 256:320], OP.is_le) for k in range(4)], r=["PP", "th"], w=["NC"], b=[0])
        out = T.B7[:, 96:128]
        items = [(out, T.I512[:], T.NC[:, 64 * k + j:64 * k + 64:2]) for k in range(4) for j in range(2)]
        nc = ["NC", "I512"]
        if fold:
            items = [(out, T.I512[:], T.GO[:, 0:32]), (out, T.I16[:], T.CT[:, 0:32]), (out, T.ID[:], T.RT[:, 0:32])] + items
            op("P", mm(items), r=nc + ["go", "I16", "CT", "ID", "RT"], w=["fP"], b=[7])
            op("V", cp(wu(2), out), r=["fP"], w=["xu"], b=[7])
        elif CFG["BOTH"][t]:
            op("P", mm([(out, T.I16[:], T.CT[:, 0:32]), (out, T.ID[:], T.RT[:, 0:32])] + items), r=nc + ["I16", "CT", "ID", "RT"], w=["fP"], b=[7])
            op("V", cp(wu(5), out), r=["fP"], w=["zu"], b=[7])
            op("V", ts(wi_(7), wi_(4), 3, 256 + 31, OP.arith_shift_right, OP.bitwise_and), r=["kz"], w=["gc"])
            op("V", ts(wu(2), wi_(7), 16.0, pf(1), OP.mult, OP.add), r=["gc", "PF0"], w=["xu"])
        else:
            op("P", mm([(out, T.I512[:], T.GO[:, 32:64])] + items), r=nc + ["nine"], w=["fP"], b=[7])
            op("V", tt(T.GO[:, 0:32], wi_(4), T.THR[:, 0:32], OP.is_lt), r=["kz", "thr0"], w=["go"])
            op("V", tt(wf(7), out, T.GO[:, 0:32], OP.mult), r=["fP", "go"], w=["x1"], b=[7])
            op("V", tt(wf(9), wf(7), wf(1), OP.add), r=["x1", "my"], w=["x2"])
            op("V", cp(wu(2), wf(9)), r=["x2"], w=["xu"])

    def move(t):
        p, pn = t % 2, 1 - t % 2
        if CFG["MV"][t] == "B" and not CFG["PB"]:
            for B, sign, bk in ((T.B1, T.NID, 1), (T.B2, T.ID, 2)):
                op("P", mm([(B[:], T.ID[:], HW[p][:, 4096:4608]), (B[:], sign[:], T.ONE[:])], 512), r=centre(p) + ["ID", "NID", "ONE"], w=["B%d" % bk], b=[bk])
        dep = ["s%d_%d" % (p, k) for k in range(8)] + centre(p) + ["Y%d" % p, "xu"]
        new = HW[pn][:, 4096:4608]
        cut = [("c", 0, 256), ("d", 256, 512)] if CFG["CUT"][t] else [("c", 0, 512)]
        if CFG["BOTH"][t]:
            H, s_ = HW[p], ["s%d_%d" % (p, k) for k in range(8)]
            op("S", act(H[:, 5136:5648], H[:, 0:4608].indirect(wu(5)), AF.Copy, got(512)), r=s_ + centre(p) + ["zu"], w=["XZ"])
            op("V", tt(T.CM[:], H[:, 4608:5120], T.B1[:], OP.max, us(512)), r=["Y%d" % p, "B1"], w=["CM"], b=[1])
            op("V", tt(T.CM[:], T.CM[:], T.B2[:], OP.min, us(512)), r=["CM", "B2"], w=["CM"], b=[2])
            op("V", cp(H[:, 0:512], T.CM[:], us(256)), r=["CM"], w=s_[:1])
            op("G", pass_on(H[:, 1040:1552], H[:, 4608:5120], 512), r=["Y%d" % p], w=s_[2:4])
            op("V", tt(T.TM[:], H[:, 5136:5648], T.B1[:], OP.max, us(512)), r=["XZ", "B1"], w=["TMc", "TMd"], b=[1])
            op("V", tt(H[:, 4096:4608], T.TM[:], T.B2[:], OP.min, us(512)), r=["TMc", "B2"], w=centre(p), b=[2])
            for e, (kind, a, z) in zip(CFG["BOTH"][t], cut):
                part, chosen = HW[pn][:, 4096 + a:4096 + z], H[:, 0:4608].indirect(T.WU[:, 64 + a // 16:64 + z // 16])
                op(e, act(part, chosen, AF.Copy, got(z - a)) if e == "S" else cp(part, chosen, got(z - a)), r=dep, w=["C%d%s" % (pn, kind)])
            op("S", act(T.XB[:], H[:, 1040:5648].indirect(wu(2)), AF.Copy, got(512)), r=dep + ["XZ", "zero%d" % p], w=["Xc", "Xd"])
            cut = []
        for kind, a, z in cut:
            name = centre(pn) if len(cut) == 1 else ["C%d%s" % (pn, kind)]
            part = HW[pn][:, 4096 + a:4096 + z]
            chosen = HW[p][:, 0:5120].indirect(T.WU[:, 64 + a // 16:64 + z // 16])
            C = HW[p][:, 4096 + a:4096 + z]
            op("S", act(T.XB[:, a:z], chosen, AF.Copy, got(z - a)), r=dep, w=["Xc", "Xd"] if len(cut) == 1 else ["X" + kind])
            if CFG["PB"]:
                half = us((z - a) // 2)
                op("V", tt(T.CM[:, a:z], T.XB[:, a:z], T.B1[:, a:z], OP.subtract, (half, 5)), r=["X" + kind, "Cp"], w=["CM" + kind], b=[1])
                op("V", ts(T.TM[:, a:z], T.CM[:, a:z], -1.0, 1.0, OP.max, OP.min, c=half), r=["CM" + kind], w=["TM" + kind])
                op("V", tt(part, T.TM[:, a:z], T.B1[:, a:z], OP.add, (half, 5)), r=["TM" + kind, "Cp"], w=name, b=[1])
            elif CFG["MV"][t] == "S":
                bk = 1 + (kind == "d")
                d = T["B%d" % bk][:, a:z]
                op("P", mm([(d, T.NID[:], C), (d, T.ID[:], T.XB[:, a:z])], z - a), r=centre(p) + ["X" + kind, "ID", "NID"], w=["B%d" % bk], b=[bk])
                op("S", act(T.TM[:, a:z], d, AF.Sign, us(z - a)), r=["B%d" % bk], w=["TM" + kind], b=[bk])
                op("V", tt(part, T.TM[:, a:z], C, OP.add, us(z - a)), r=["TM" + kind] + centre(p), w=name)
            else:
                op("V", tt(T.TM[:, a:z], T.XB[:, a:z], T.B1[:, a:z], OP.max, us(z - a)), r=["X" + kind, "B1"], w=["TM" + kind], b=[1])
                op("V", tt(part, T.TM[:, a:z], T.B2[:, a:z], OP.min, us(z - a)), r=["TM" + kind, "B2"], w=name, b=[2])
        for kind, a, z in parts(t + 1) if t < R - 1 else []:
            send(kind, t + 1, centre(pn)[a // 256:(z + 255) // 256], "CA%d%s" % (t + 1, kind), src=HW[pn][:, 4096 + a:4096 + z])
        if t < R - 1:
            own = CA[t + 1][:, 512 * q:512 * q + 512]
            if CFG["CP"] == "G":
                op("G", pass_on(own, new, 512), r=centre(pn) + ["~c", "~d"], w=["CAown"])
            elif CFG["CP"] == "S":
                op("S", act(own, new, AF.Copy, us(512)), r=centre(pn), w=["CAown"])
            else:
                op("V", cp(own, new, us(256)), r=centre(pn), w=["CAown"])

    def exits(t):
        H, p = HW[t % 2], t % 2
        op("G", pass_on(T.SB[:, 512:896], T.SE[:], 384), r=["SE"], w=["SB"])
        op("V", ts(T.OG[:, 0:32], wi_(4), 2055, None, OP.bitwise_and), r=["kz"], w=["og"])
        op("V", ts(T.OG[:, 32:64], T.OG[:, 0:32], -4.0, None, OP.add), r=["og"], w=["og4"])
        op("V", ts(wi_(6), wi_(4), 3, 255, OP.arith_shift_right, OP.bitwise_and), r=["kz"], w=["kc"])
        op("V", ts(wu(1), wi_(6), pf(11), None, OP.add), r=["kc", "PF11"], w=["mu"])
        op("S", act(T.MS[:], T.MT[:, 0:4096].indirect(wu(1)), AF.Copy, got(512)), r=["MT", "mu"], w=["MS"])
        run("V", [ts(T.HIT[:, 64 * o:64 * o + 64], T.OG[:], float(2048 + o), None, OP.is_equal) for o in range(4)], r=["og", "og4"], w=["HIT"])
        hit = ["HIT"]
        op("V", scan(T.INC[:], T.M32[:], T.HIT[:], us(128)), r=["M32"] + hit, w=["INC"])
        op("P", mm([(T.B3[:, 256:512], T.NUP[:], T.HIT[:]), (T.B3[:, 256:512], T.GRP[:], T.INC[:])], 256), r=hit + ["INC", "GRP", "NUP"], w=["pf"], b=[3])
        op("V", ts(T.OB[:, 0:32], T.OG[:, 0:32], 48.0, 512.0 - 48.0 * 2048, OP.mult, OP.add), r=["og"], w=["ob"])
        op("V", tt(T.PRD[:], T.B3[:, 256:512], T.HIT[:], OP.mult, us(256)), r=["pf"] + hit, w=["PRD"], b=[3])
        op("P", mm([(T.B7[:, 128:160], T.ID[:], T.PRD[:, 32 * o:32 * o + 32]) for o in range(8)]), r=["PRD", "ID"], w=["cnt"], b=[7])
        val = T.B4[:, 256:288]
        if CFG["OV"] == "W":
            run("V", [ts(wf(12), T.B7[:, 128:160], 48.0, -2048.0, OP.is_ge, OP.mult), tt(wf(13), T.B7[:, 128:160], T.OB[:, 0:32], OP.add)], r=["cnt", "ob"], w=["ov"], b=[7])
            op("V", tt(wf(14), wf(13), wf(12), OP.add), r=["ov"], w=["val"])
            op("V", tt(wf(15), wf(14), wf(0), OP.max), r=["val", "m"], w=["v3"])
        else:
            op("P", mm([(val, T.ID[:], T.OB[:, 0:32])] + [(val, T.ID[:], T.PRD[:, 32 * o:32 * o + 32]) for o in range(8)], stop=False),
               r=["PRD", "ID", "ob"], w=["val", "mP"], b=[4])
            if CFG["OV"] == "S":
                op("S", act(T.OB[:, 32:64], T.B7[:, 128:160], AF.Relu, bias=-47.0 * 1024, scale=1024.0), r=["cnt"], w=["ov"], b=[7])
            else:
                op("V", ts(T.OB[:, 32:64], T.B7[:, 128:160], 48.0, 2048.0, OP.is_ge, OP.mult), r=["cnt"], w=["ov"], b=[7])
            op("P", mm([(val, T.NID[:], T.OB[:, 32:64])], start=False), r=["ov", "NID"], w=["val", "mP"], b=[4])
            op("V", tt(wf(15), val, wf(0), OP.max), r=["val", "m"], w=["v3"], b=[4])
        op("V", cp(wu(3), wf(15)), r=["v3"], w=["su"])
        n = 512 // CFG["PUT"][0]
        for a in range(0, 512, n):
            op("V", cp(T.SB[:, 0:896].indirect(T.WU[:, 96 + a // 16:96 + (a + n) // 16]), T.MS[:, a:a + n], put(n)), r=["MS", "su"], w=["SB"])
        op("P", mm(sel(T.B4[:, 0:24], WT, lambda r: T.SB[:, 512 + r:896:16])), r=["SB", "WS7"], w=["mP"], b=[4])
        op("P", mm(sel(T.B3[:, 256:280], WY, lambda r: T.SB[:, 512 + r:896:16])), r=["SB", "WS8"], w=["pf"], b=[3])
        op("V", cp(T.META[:, 32 * t:32 * t + 24], T.B4[:, 0:24]), r=["mP"], w=["META%d" % t], b=[4])
        send("m", t, "META%d" % t, "LM%d" % t)
        op("V", cp(T.WU[:, 128:152], T.B3[:, 256:280]), r=["pf"], w=["yu"], b=[3])
        op("S", act(T.YS[:, 384 * t:384 * t + 384], H[:, 4608:5136].indirect(T.WU[:, 128:152]), AF.Copy, got(384)),
           r=["Y%d" % p, "zero%d" % p, "yu"], w=["YS%d" % t])
        send("y", t, "YS%d" % t, "L%d" % t)
        if t < R - 1:
            op("P", mm([(T.B7[:, 224:225], T.ONE[:, 0:128], T.INC[:, 31 + 32 * o:32 + 32 * o]) for o in range(8)]), r=["INC", "ONE"], w=["AP"], b=[7])

    def arrivals(t):
        if t == R - 1:
            op("V", cp(T.EWF[:, 0:4608].indirect(T.LM[:, 32 * t:32 * t + 24]), T.VF[:], put(384)), r=["VT%d" % t, "LM%d" % t], w=["EWF"])
            dma("Y", [(T.ye[:], T.EWF[0:128:16, 0:4096])], "oe", r=["EWF"], lat=2.3)
            rows(T.yn[:], T.EWF[8:128:16, 0:4096], "gn", ["EWF"], ["yn"])
            return
        if t == 0:
            values()
        op("V", cp(T.EW[:, 0:4608].indirect(T.LM[:, 32 * t:32 * t + 24]), T.VT[:, 384 * t:384 * t + 384], put(384)), r=["VT%d" % t, "LM%d" % t], w=["EW"])
        rows(T.yn[:], T.EW[3 + t:128:16, 0:4096], "gn", ["EW"], ["yn"], first=t == 0)
        if t == R - 2:
            rows(T.EWF[0:128:8, 0:4096], T.EW[0:128:8, 0:4096], "gf", ["EW"], ["EWF"], add=False)
            rows(T.EWF[0:128:16, 0:4096], T.EW[1:128:16, 0:4096], "gf", ["EW"], ["EWF"])
        lim = 0.5 - (2048 + 384 * t)
        cuts = CFG["CUTS"]
        for a, z in zip(cuts, cuts[1:]):
            u, us_ = T.B6[:, 64 * a:64 * z], ["U%d" % c for c in range(a, z)]
            op("P", mm(sel(u, WE, lambda r, a=a, z=z: T.EW[:, 1024 * a + r:1024 * z:16]), 64 * (z - a)), r=["EW", "WS6"], w=us_ + ["~U"], b=[6])
            op("V", cp(T.EU[:, 64 * a:64 * z], u, us(64 * (z - a))), r=us_, w=["EU%d" % c for c in range(a, z)], b=[6])
        if CFG["FX"] == "V":
            op("V", ts(T.SG[:, 0:256], T.EU[:], -lim, None, OP.is_ge, c=us(128)), r=["EU%d" % c for c in range(4)] + ["n"], w=["SG%d" % t])
        else:
            op("S", act(T.SG[:, 256 * t:256 * t + 256], T.B6[:, 0:256], AF.Sign, us(256), bias=lim), r=["U%d" % c for c in range(4)], w=["SG%d" % t], b=[6])
        places, landed = T.ZW[:, 384 * t:384 * t + 384], T.ZW[:, 2048 + 384 * t:2048 + 384 * t + 384]
        op(CFG["Z"], {"V": cp(places, landed, us(192)), "G": pass_on(places, landed, 384), "S": act(places, landed, AF.Copy, us(384))}[CFG["Z"]], r=["L%d" % t], w=["Z"])
        if t == R - 2:
            dma("Y", [(T.yz[:, 0:1152], T.ZW[:, 0:1152]), (T.yz[:, 1536:2048], T.ZW[:, 1536:2048])], "oz0", r=["Z"])

    for t in range(R):
        middle = (neighbours, exits, entries, choice, move) if CFG["FOLD"][t] else (entries, neighbours, choice, move, exits)
        for part in (jump, flux) + middle + (arrivals,):
            stage[0] += 1
            part(t)
    dma("Y", [(T.yx[:], T.XB[:])], "ox", r=["Xc", "Xd"])
    dma("Y", [(T.yc[:], T.HW0[:, 4096:4608])], "oc", r=centre(0))
    dma("Y", [(T.yz[:, 1152:1536], T.ZW[:, 3200:3584])], "oz1", r=["L3"])

    if "order" not in ORDER:
        ORDER["order"] = order_calls(calls)
    for i in ORDER["order"]:
        issue(calls[i])
    for sem, val in count.items():
        if known["G"].get(sem, 0) < val:
            g.wait_ge(T.sem[sem], val)
